import numpy as np, ml_dtypes
CORES = [1,5,17,21,33,37,49,53]
N = 8
BF = ml_dtypes.bfloat16
def gentries(a):
    return np.ascontiguousarray(a.reshape(8, 16, -1).transpose(0, 2, 1)).reshape(8, -1)
def gtable(e):
    e = np.asarray(e); return np.ascontiguousarray(e.reshape(8, -1, 16).transpose(0, 2, 1)).reshape(128, -1).astype(np.int32)
W, M, L, D, S = 4096, 4096, 64, 32, 5
K = L * D
def cols(rng, n):
    base = rng.integers(0, 256, (N, 8, 1, n)); amp = rng.integers(0, 129, (N, 8, 1, n))
    return np.clip(np.rint(base + amp * (2.0 * rng.random((N, 8, 16, n)) - 1.0)), 0, 255).astype(np.int64)
def parts(rng):
    X, Z = cols(rng, W), cols(rng, L)
    P = rng.integers(0, W, (N, 8, M)); V = rng.integers(0, W, (N, 8, K)); pool = rng.integers(0, M, (N, 8, 256))
    O = np.where(rng.random((N, 8, K)) < 0.5, rng.integers(0, M, (N, 8, K)), np.take_along_axis(pool, rng.integers(0, 256, (N, 8, K)), 2))
    c = rng.random((N, 8, K)); T = np.where(c < 0.45, rng.integers(0, S + 2, (N, 8, K)), np.where(c < 0.85, 99, rng.integers(0, 99, (N, 8, K))))
    return X, Z, P, O, V, T, rng.integers(200, 3400, (N, 8, S))
def pack(X, Z, P, O, V, T, th):
    return {"x": np.ascontiguousarray(X).reshape(N, 128, W).astype(np.float32).astype(BF), "z": np.ascontiguousarray(Z).reshape(N, 128, L).astype(np.float32).astype(BF), "px": P.astype(np.int32),
            "ol": np.stack([gtable(a) for a in O]), "nl": np.stack([gtable(a) for a in V]), "tl": np.stack([gtable(a) for a in T]), "th": th.astype(np.int32)}
def setup_inputs(rng):
    return pack(*parts(rng))
def setup_inputs_spread(rng):
    X = (np.exp2(8 * rng.random((N, 8, 1, W))) * rng.random((N, 8, 16, W))).astype(np.int64); Z = (np.exp2(8 * rng.random((N, 8, 1, L))) * rng.random((N, 8, 16, L))).astype(np.int64)
    e = rng.integers(1, 5, (3, N, 8, 1))
    P = (W * rng.random((N, 8, M)) ** e[0]).astype(np.int64); O = (M * rng.random((N, 8, K)) ** e[1]).astype(np.int64); V = (W * rng.random((N, 8, K)) ** e[2]).astype(np.int64)
    T = np.where(rng.random((N, 8, K)) < 0.3, 99, (100 * rng.random((N, 8, K)) ** 4).astype(np.int64)); th = (4081 * rng.random((N, 8, S)) ** 2).astype(np.int64)
    return pack(X, Z, P, O, V, T, th)
def setup_inputs_ends(rng):
    def ends(n):
        m = rng.integers(0, 3, (N, 8, 1, n)); return np.where(m == 2, 255 * rng.integers(0, 2, (N, 8, 16, n)), 255 * np.minimum(m, 1)) + np.zeros((N, 8, 16, n), np.int64)
    X, Z = ends(W), ends(L); X[..., 0] = 0; X[..., W - 1] = 255
    P = (W - 1) * rng.integers(0, 2, (N, 8, M)); O = (M - 1) * rng.integers(0, 2, (N, 8, K)); V = (W - 1) * rng.integers(0, 2, (N, 8, K)); T = 99 * rng.integers(0, 2, (N, 8, K))
    th = 4080 * rng.integers(0, 2, (N, 8, S)); th[:, 0, 0] = 0; th[:, 1, 0] = 4080; th[0, 7, 0] = 0; th[N - 1, 7, 0] = 4080
    star = int(np.argmax(((37 * np.arange(M)) & (W - 1)) == W - 1))
    for pair, v, n, o, ks in (((0, L - 1), 0, 0, star, (0, 1, D - 1)), ((1, L - 2), 255, W - 1, star, (0, 1, D - 1)), ((2, L - 3), 0, W - 1, M - 1, (0, 3, D - 1))):
        for l in pair:
            Z[..., l] = v
            for k in ks: V[..., k * L + l] = n; T[..., k * L + l] = 0; O[..., k * L + l] = o
    return pack(X, Z, P, O, V, T, th)
def setup_inputs_corners(rng):
    X, Z, P, O, V, T, th = parts(rng)
    th = np.where(rng.random((N, 8, S)) < 0.5, 4080 * rng.integers(0, 2, (N, 8, S)), th)
    for a in range(N):
        ct, cp, co, cv, cz = [rng.permutation(8) for i in range(5)]
        for g in range(8):
            T[a, g] = rng.choice(np.array(((0,), (99,), (98,), (S,), (S - 1,), (0, 98), (1, 2, 99), (0, 1, 2, S - 1, S, S + 1, 98, 99))[ct[g]]), K)
            if cp[g] < 5: P[a, g] = (np.arange(M) & (W - 1), np.zeros(M, np.int64), np.full(M, W - 1), W - 1 - (np.arange(M) & (W - 1)), rng.choice(np.array([0, W - 1]), M))[cp[g]]
            if co[g] < 4: O[a, g] = (np.zeros(K, np.int64), np.full(K, M - 1), rng.choice(np.array([0, M - 1]), K), np.arange(K))[co[g]]
            if cv[g] < 4: V[a, g] = (np.zeros(K, np.int64), np.full(K, W - 1), rng.choice(np.array([0, W - 1]), K), np.arange(K) & (W - 1))[cv[g]]
            if cz[g] < 2: Z[a, g] = 255 * cz[g]
    e = int(rng.integers(0, 8)); X[:, e] = 255; Z[:, e] = 0; Z[:, e, 0, 1::2] = 1; th[:, e, 0] = 4079
    O[:, e, 1::2] = 32 * (M // 32 - 1 - rng.integers(0, 8, (N, K // 2))) + 17
    return pack(X, Z, P, O, V, T, th)
def setup_inputs_crowd(rng):
    X, Z, P, O, V, T, th = parts(rng); pm = rng.permutation(8)
    for g in range(8):
        c = int(pm[g])
        if c < 2: th[:, g] = 4080; T[:, g] = 99
        if c == 2 or c == 3: th[:, g] = 0
        if c == 4 or c == 5: X[:, g, :, 0] = 0; th[:, g] = rng.integers(100, 1500, (N, S))
        for a in range(N):
            one = int(rng.integers(1, L)); p = int(rng.integers(0, M))
            if c == 1: T[a, g, int(rng.integers(0, K))] = 98
            if 2 <= c < 6: O[a, g] = p
            if c == 4 or c == 5:
                V[a, g] = 0; T[a, g] = 0; v = rng.integers(0, 256, 16); v[0] = 255; v[1] = 0
                Z[a, g] = v[np.argsort(rng.random((16, L)), axis=0)]
            if c == 3 or c == 5: O[a, g, one::L] = (p + 1 + int(rng.integers(0, M - 1))) % M
            if c == 5: Z[a, g, :, one] = rng.integers(0, 256, 16)
            if c == 6:
                l = np.arange(K) % L; w = rng.integers(0, M, L); n = int(rng.integers(0, W)); O[a, g] = w[np.minimum(l, L - 1 - l)]; V[a, g] = n; T[a, g] = 0; X[a, g, :, n] = 0
                Z[a, g, 0] = 255; Z[a, g, 15] = 0; v = Z[a, g][:, np.minimum(np.arange(L), L - 1 - np.arange(L))]
                Z[a, g] = np.where(np.arange(L) < L // 2, v, v[::-1])
            if c == 7: O[a, g] = rng.choice(rng.integers(0, M, 4), K)
    return pack(X, Z, P, O, V, T, th)
def setup_inputs_ties(rng):
    X, Z, P, O, V, T, th = parts(rng)
    pat = 64 * rng.integers(0, 4, (N, 8, 16, 8)); X = np.take_along_axis(pat, rng.integers(0, 8, (N, 8, 1, W)), 3)
    Z = np.where(rng.random((N, 8, 1, L)) < 0.5, np.take_along_axis(np.roll(pat, -1, axis=0), rng.integers(0, 8, (N, 8, 1, L)), 3), 64 * rng.integers(0, 4, (N, 8, 16, L)))
    T = np.where(rng.random((N, 8, K)) < 0.7, rng.integers(0, S + 1, (N, 8, K)), 99); th = 64 * rng.integers(0, 40, (N, 8, S)); th[:, ::3, 1] = 0; th[:, 1::3, 0] = 0
    return pack(X, Z, P, O, V, T, th)
def check_inputs(d):
    bad = []
    for k, lo, hi in (("x", 0, 255), ("z", 0, 255), ("px", 0, W - 1), ("ol", 0, M - 1), ("nl", 0, W - 1), ("tl", 0, 99), ("th", 0, 4080)):
        v = np.asarray(d[k]).astype(np.float64)
        if not (np.min(v) >= lo and np.max(v) <= hi): bad.append("range of " + k)
        elif np.any(v != np.floor(v)): bad.append("whole numbers in " + k)
    return bad
def reference(x, z, px, ol, nl, tl, th):
    X = x.astype(np.float32).astype(np.int64).reshape(N, 8, 16, W); Z = z.astype(np.float32).astype(np.int64).reshape(N, 8, 16, L); P = px.astype(np.int64)
    O, V, T = [np.stack([gentries(a) for a in b]).astype(np.int64) for b in (ol, nl, tl)]
    lower = np.tri(L, L, -1, dtype=bool); lane = np.arange(L); A = np.zeros((N, 8, 1), np.int64)
    for s in range(S):
        R = np.where(T <= s, V, np.take_along_axis(P, O, 2))
        y = np.take_along_axis(X, R[:, :, None, :], 3); u = np.add.reduce(np.abs(y - np.tile(Z, (1, 1, 1, D))), axis=2)
        h = (((u * O) >> 5) + u + 37 * O + A) & (W - 1)
        h, O, V, T, Z = [np.roll(a, 1, axis=0) for a in (h, O, V, T, Z)]
        G = np.take_along_axis(X, h[:, :, None, :], 3); d = np.add.reduce(np.abs(G - np.tile(Z, (1, 1, 1, D))), axis=2)
        lim = th[:, :, s:s + 1].astype(np.int64)
        red = (d <= lim) & ~((T > s) & (T < 99))
        V = np.where(red, h, V); T = np.where(red, s + 2, T); A = np.sum(red.astype(np.int64), axis=2, keepdims=True)
        by = d.reshape(N, 8, D, L); j = np.argmax(by, axis=2) * L + lane; b = np.argmin(by, axis=2) * L + lane
        go = np.take_along_axis(d, j, 2) > lim
        np.put_along_axis(T, j, np.where(go, 99, np.take_along_axis(T, j, 2)), 2)
        oj = np.take_along_axis(O, j, 2); hj = np.take_along_axis(h, j, 2); hb = np.take_along_axis(h, b, 2)
        win = go & ~np.any((oj[..., :, None] == oj[..., None, :]) & lower & go[..., None, :], axis=3)
        q, g, l = np.nonzero(win); P[q, g, oj[q, g, l]] = hj[q, g, l]
        Z = (Z + np.take_along_axis(G, b[:, :, None, :], 3)) >> 1
        win = ~np.any((hb[..., :, None] == hb[..., None, :]) & lower, axis=3)
        q, g, l = np.nonzero(win); X[q, g, :, hb[q, g, l]] = Z[q, g, :, l]
    return {"yx": X.reshape(N, 128, W).astype(np.float32).astype(BF), "yp": P.astype(np.float32), "yz": Z.reshape(N, 128, L).astype(np.float32).astype(BF),
            "yn": np.stack([gtable(a) for a in V]).astype(np.float32), "yt": np.stack([gtable(a) for a in T]).astype(np.float32)}

@@ -1,0 +1,491 @@
+from concourse.mybir import AluOpType as ALU, AxisListType, ActivationFunctionType as ACT
+
+S, PADW, DUMP0, TW = 5, 4176, 4097, 256
+BIG = 1.0e6
+
+
+def _sb(n, dtype="float32", p=128):
+    return ("sbuf", [p, n], dtype)
+
+
+SCRATCH = {
+    "XW": _sb(PADW, "bfloat16"), "PW": _sb(PADW, "bfloat16"), "PF": _sb(PADW),
+    "ztb": ("sbuf", [128, 4, TW], "bfloat16"), "ztc": ("sbuf", [128, 4, TW], "bfloat16"),
+    "DF": _sb(2048, "bfloat16"), "AB": _sb(2048, "bfloat16"), "PG": _sb(2048, "bfloat16"),
+    "W": _sb(2048, "bfloat16"), "WP": _sb(2048, "bfloat16"),
+    "pxi": _sb(256, "int32"), "pxt": _sb(256, "int32"), "LH": _sb(512, "bfloat16"),
+    "oli": _sb(128, "int32"), "nli": _sb(128, "int32"), "tli": _sb(128, "int32"),
+    "thi": _sb(5, "int32", 8), "thf": _sb(5, "float32", 8), "GE1": _sb(128, "float32", 8), "GE": _sb(128, "float32", 8),
+    "ones": _sb(128), "oneb": _sb(128, "bfloat16", 1), "CQ": _sb(128, "bfloat16", 1),
+    "G1": _sb(128), "GM": _sb(128), "ID": _sb(128), "LT": _sb(128), "GA": _sb(8), "GP": _sb(8),
+    "mod16": _sb(128), "colc": _sb(128), "C2": _sb(128), "SEG16": _sb(128), "SEG32": _sb(128), "DM": _sb(128), "ND": _sb(144),
+    "pidx": _sb(1, "int32"), "p16i": _sb(1, "int32"), "p16": _sb(1), "q0": _sb(1), "q1": _sb(1), "wp": _sb(1),
+    "dump0": _sb(8), "dump": _sb(8), "dumpw": _sb(128), "LM": _sb(5),
+    "OW0": _sb(256), "OW1": _sb(256), "OQ0": _sb(128), "OQ1": _sb(128), "HW": _sb(128), "Q32": _sb(128), "A32": _sb(1), "rs": _sb(1),
+    "om": _sb(128), "OM": _sb(128, "uint16"), "NM": _sb(128), "RU": _sb(128, "uint16"),
+    "hm": _sb(128), "hv": _sb(128, "int32"), "hs": _sb(128, "int32"),
+    "e1": _sb(128), "e2": _sb(128), "RT0": _sb(128), "RT": _sb(128), "ST": _sb(128), "hN": _sb(128), "K2": _sb(128), "SM": _sb(256),
+    "KI": _sb(8, "int32"), "CI": _sb(12, "int32"), "nogo": _sb(4, "int32"), "gk": _sb(4), "OFF": _sb(12, "uint16"),
+    "GD": _sb(208), "OWN": _sb(144), "HB": _sb(4, "uint16"), "gz": _sb(64), "zi": _sb(64, "int32"),
+    "E": _sb(128), "F": _sb(128), "f1": _sb(8), "f2": _sb(8), "fu": _sb(16, "uint16"),
+    "hx": _sb(64, "bfloat16"), "ht": _sb(64), "PD": _sb(64, "bfloat16"), "RF": _sb(128),
+    "YN": _sb(128), "YT": _sb(128), "YPg": _sb(256), "LO": _sb(512, "bfloat16"),
+    "ZR": _sb(192 * S, "bfloat16"),
+    "NR": _sb(128 * S),
+    "HS": _sb(128 * S, "uint16"),
+    "HR": _sb(128 * S, "uint16"),
+    "OU": _sb(128 * (S + 1), "uint16"),
+    "ZS": _sb(192 * (S + 1), "bfloat16"),
+    "NS": _sb(128 * (S + 1)),
+}
+for _n in ("pUA", "pUB", "pUC", "pPA", "pPB", "pR", "pM", "pS"):
+    SCRATCH[_n] = ("psum", [128, 512], "float32")
+PIECE = {"%s%d" % (k, s): (k, SCRATCH[k][1][1] // n * s) for k, n in
+         (("ZR", S), ("NR", S), ("HS", S), ("HR", S), ("OU", S + 1), ("ZS", S + 1), ("NS", S + 1)) for s in range(n)}
+RECV = ("rO", "rZ", "rA", "rB", "rC", "rN")
+DMAS = ["d_px", "d_ol", "d_z", "d_tl", "d_nl", "d_th", "d_x", "d_lo", "d_hi",
+        "o_x", "o_lo", "o_hi", "o_pf", "o_p", "o_z", "o_n", "o_t"]
+SEMAPHORES = ["v", "a", "t", "p", "loc"] + ["%s%d" % (k, s) for s in range(S) for k in RECV] + DMAS
+HP = ((0, 64, "pUA", "rA"), (64, 96, "pUB", "rB"), (96, 128, "pUC", "rC"))
+KB = ("pUA", "pUB")
+PB = ("pPA", "pPB")
+A0 = -8388608.0 - 1184.0
+
+
+def rank_program(g, core, T, topo):
+    rank = T.rank_of(core)
+    if rank is None:
+        return
+    nxt = T.cores[(rank + 1) % len(T.cores)]
+    prv = T.cores[(rank - 1) % len(T.cores)]
+    queues = {"v": g.vector, "a": g.scalar, "t": g.tensor, "p": g, "s": g.sync}
+    count = {"v": 0, "a": 0, "t": 0, "p": 0}
+    seen = {q: {} for q in queues}
+    acc = {}
+    psum = set(n for n in SCRATCH if SCRATCH[n][0] == "psum")
+
+    def need(q, regs, write, needs):
+        for (n, lo, hi) in regs:
+            for (qa, sem, val, alo, ahi, aw) in acc.get(n, ()):
+                apart = ahi <= lo or alo >= hi
+                if n in psum and qa != q:
+                    apart = False
+                elif apart or not (aw or write) or (qa == q and write and q == "t"):
+                    continue
+                needs[sem] = max(needs.get(sem, 0), val)
+
+    def note(q, sem, val, regs, write):
+        for (n, lo, hi) in regs:
+            old = acc.get(n, [])
+            if write:
+                old = [a for a in old if not (lo <= a[3] and a[4] <= hi)]
+            acc[n] = old + [(q, sem, val, lo, hi, write)]
+
+    def waits(q, rd, wr):
+        needs = {}
+        need(q, rd, False, needs)
+        need(q, wr, True, needs)
+        for sem in sorted(needs):
+            if seen[q].get(sem, 0) < needs[sem]:
+                queues[q].wait_ge(T.sem[sem], needs[sem])
+                seen[q][sem] = needs[sem]
+
+    def regs(views):
+        return [r for v in views for r in v[1]]
+
+    def op(q, call, rd, wr):
+        rd, wr = regs(rd), regs(wr)
+        waits(q, rd, wr)
+        count[q] += 1
+        call().then_inc(T.sem[q], 1)
+        note(q, q, count[q], rd, False)
+        note(q, q, count[q], wr, True)
+
+    def dma(q, sem, out, in_):
+        waits(q, in_[1], out[1])
+        queues[q].dma_start(out=out[0], in_=in_[0]).then_inc(T.sem[sem], 16)
+        note("d" + sem, sem, 16, in_[1], False)
+        note("d" + sem, sem, 16, out[1], True)
+
+    sent = [0]
+
+    def send(dst_name, src_name, lo, hi, sem):
+        src, dst = V(src_name, lo, hi), V(dst_name, lo, hi)
+        waits("p", src[1], [])
+        rid, pid, _ = topo.addr(nxt)
+        g.remote_dma(out_ap=dst[0], in_ap=src[0], remote_sem=T.sem[sem], local_sem=T.sem["loc"],
+                     pid=pid, routing_id=rid, dma_engine_mask=topo.mask(core, nxt))
+        sent[0] += len(topo.engines(core, nxt))
+        note("r", sem, len(topo.engines(prv, core)), dst[1], True)
+
+    def V(name, lo, hi, st=1):
+        if name in PIECE:
+            name, base = PIECE[name]
+            lo, hi = lo + base, hi + base
+        return (T[name][:, lo:hi] if st == 1 else T[name][:, lo:hi:st], [(name, lo, hi)])
+
+    def ALL(name):
+        return (T[name][:], [(name, 0, SCRATCH[name][1][1] if name in SCRATCH else 1)])
+
+    def IND(win, off):
+        return (win[0].indirect(off[0]), win[1] + off[1])
+
+    def cols(*vs):
+        return [v for v in vs if not isinstance(v, (int, float)) and v is not None]
+
+    def raw(v):
+        return v if isinstance(v, (int, float)) or v is None else v[0]
+
+    def tt(o, a, b, f):
+        op("v", lambda: g.vector.tensor_tensor(out=o[0], in0=a[0], in1=b[0], op=f), [a, b], [o])
+
+    def ts(o, a, s1, f1, s2=None, f2=None):
+        if f2 is None:
+            op("v", lambda: g.vector.tensor_scalar(out=o[0], in0=a[0], scalar1=raw(s1), scalar2=None, op0=f1), [a] + cols(s1), [o])
+        else:
+            op("v", lambda: g.vector.tensor_scalar(out=o[0], in0=a[0], scalar1=raw(s1), scalar2=raw(s2), op0=f1, op1=f2),
+               [a] + cols(s1, s2), [o])
+
+    def cp(o, a):
+        op("v", lambda: g.vector.tensor_copy(out=o[0], in_=a[0]), [a], [o])
+
+    def scan(o, d0, d1, f0, f1):
+        op("v", lambda: g.vector.tensor_tensor_scan(out=o[0], data0=d0[0], data1=d1[0], initial=0.0, op0=f0, op1=f1), [d0, d1], [o])
+
+    def fill(o, c):
+        op("v", lambda: g.vector.memset(o[0], c), [], [o])
+
+    def act(o, a, f=ACT.Copy):
+        op("a", lambda: g.scalar.activation(out=o[0], in_=a[0], func=f), [a], [o])
+
+    def line(o, a, scale, bias):
+        op("a", lambda: g.scalar.activation(out=o[0], in_=a[0], func=ACT.Identity, bias=raw(bias), scale=scale), [a] + cols(bias), [o])
+
+    def mm(o, l, r, start=True, stop=True):
+        op("t", lambda: g.tensor.matmul(out=o[0], lhsT=l[0], rhs=r[0], start=start, stop=stop), [l, r], [o])
+
+    def iota(o, pattern, base, cm):
+        op("p", lambda: g.iota(o[0], pattern, base, cm, allow_small_or_imprecise_dtypes=True), [], [o])
+
+    def select(o, a, pattern, f, base, cm):
+        op("p", lambda: g.affine_select(o[0], a[0], pattern, f, 0.0, base, cm), [a], [o])
+
+    XR, PR = V("XW", 0, 4112), V("PW", 0, 4112)
+    XA, PA = V("XW", 0, PADW), V("PW", 0, PADW)
+
+    def tile(name, src, steps=(0, 16, 32, 64)):
+        t = T[name]
+        for w in steps:
+            if w == 0:
+                act((t[:, :, 0:16], [(name, 0, 16)]), V(src, 0, 64))
+            else:
+                act((t[:, :, w:2 * w], [(name, w, 2 * w)]), (t[:, :, 0:w], [(name, 0, w)]))
+
+    def tile_end(name, copy):
+        t = T[name]
+        copy((t[:, :, 128:256], [(name, 128, 256)]), (t[:, :, 0:128], [(name, 0, 128)]))
+
+    def pgather(a, b):
+        return V("PG", 16 * a, 16 * b), IND(PR, V("OM", a, b))
+
+    def reduce16(src, c0, c1, w, bank, first):
+        out = V(bank, 0, c1 - c0)
+        if first is not None:
+            mm(out, first[0], first[1], True, False)
+        for i in range(16):
+            mm(out, V(w, 128 * i, 128 * i + 128), (T[src][:, 16 * c0 + i:16 * c1:16], [(src, 16 * c0, 16 * c1)]),
+               first is None and i == 0, i == 15)
+
+    def gather_abs(L, j, off, tname):
+        lo = 512 * L + TW * j
+        tt(V("DF", lo, lo + TW), IND(XR, V(off, lo // 16, (lo + TW) // 16)), (T[tname][:, L, 0:TW], [(tname, 0, TW)]), ALU.subtract)
+        act(V("AB", lo, lo + TW), V("DF", lo, lo + TW), ACT.Abs)
+
+    def h_of(piece, s, between=None):
+        a, b, bank, sem = HP[piece]
+        u = V(bank, 0, b - a)
+        tt(V("hm", a, b), u, V("OQ%d" % (s % 2), a, b), ALU.mult)
+        tt(V("pS", 256 + a, 256 + b), u, V("Q32", a, b), ALU.add)
+        if between is not None:
+            between()
+        tt(V("hv", a, b), V("pS", 256 + a, 256 + b), V("hm", a, b), ALU.add)
+        ts(V("hs", a, b), V("hv", a, b), 5, ALU.arith_shift_right, 4095, ALU.bitwise_and)
+        ts(V("HS%d" % s, a, b), V("hs", a, b), 1.0, ALU.add)
+        send("HR%d" % s, "HS%d" % s, a, b, "%s%d" % (sem, s))
+
+    dma("s", "d_px", V("pxi", 0, 256), ALL("px"))
+    dma("a", "d_ol", V("oli", 0, 128), ALL("ol"))
+    dma("s", "d_z", V("ZS0", 0, 64), ALL("z"))
+    dma("a", "d_tl", V("tli", 0, 128), ALL("tl"))
+    fill(V("ones", 0, 128), 1.0)
+    fill(V("XW", 0, 16), 0.0)
+    fill(V("XW", 4096, PADW), 0.0)
+    dma("s", "d_x", V("XW", 1, 4097), ALL("x"))
+    dma("a", "d_nl", V("nli", 0, 128), ALL("nl"))
+    dma("a", "d_th", ALL("thi"), ALL("th"))
+    iota(V("pidx", 0, 1), [[0, 1]], 0, 1)
+    select(V("G1", 0, 128), V("ones", 0, 128), [[-16, 8], [0, 16]], ALU.is_ge, 0, 1)
+    select(V("GM", 0, 128), V("G1", 0, 128), [[16, 8], [0, 16]], ALU.is_ge, 15, -1)
+    select(V("ID", 0, 128), V("ones", 0, 128), [[1, 128]], ALU.is_equal, 0, -1)
+    iota(V("W", 0, 2048), [[0, 2048]], 0, 0)
+    fill(V("PW", 0, PADW), 0.0)
+    ts(V("LH", 256, 512), V("pxi", 0, 256), 1, ALU.add)
+    waits("a", [("LH", 256, 512), ("PW", 0, PADW)], [])
+    g.scalar.dma_start(out=T["PW"][1:128:16, 1:4097], in_=T["LH"][:, 256:512]).then_inc(T.sem["d_hi"], 16)
+    ts(V("pxt", 0, 256), V("pxi", 0, 256), 1, ALU.add)
+    ts(V("p16i", 0, 1), V("pidx", 0, 1), 15, ALU.bitwise_and)
+    tt(V("LH", 0, 256), V("pxt", 0, 256), V("LH", 256, 512), ALU.subtract)
+    dma("s", "d_lo", (T["PW"][0:128:16, 1:4097], [("PW", 1, 4097)]), V("LH", 0, 256))
+    note("dd_hi", "d_hi", 16, [("LH", 256, 512)], False)
+    acc["PW"] = acc["PW"] + [("dd_hi", "d_hi", 16, 1, 4097, True)]
+    cp(V("p16", 0, 1), V("p16i", 0, 1))
+    for L in range(4):
+        cp(V("ZS0", 64 + 32 * L, 96 + 32 * L), V("tli", L, 128, 4))
+    ts(V("q0", 0, 1), V("p16", 0, 1), 0.0, ALU.is_equal)
+    ts(V("q1", 0, 1), V("p16", 0, 1), 1.0, ALU.is_equal)
+    for L in range(4):
+        ts(V("OW0", 32 * L, 32 * L + 32), V("oli", L, 128, 4), 1, ALU.add)
+    ts(V("pS", 384, 512), V("ZS0", 64, 192), 0.0, ALU.is_gt)
+    tt(V("wp", 0, 1), V("q1", 0, 1), V("q0", 0, 1), ALU.add)
+    ts(V("GA", 0, 8), V("GM", 0, 128, 16), 32.0, ALU.mult)
+    tt(V("om", 0, 128), V("pS", 384, 512), V("OW0", 0, 128), ALU.mult)
+    ts(V("GP", 0, 8), V("GM", 0, 128, 16), V("wp", 0, 1), ALU.mult)
+    fill(V("WP", 0, 2048), 0.0)
+    cp(V("OM", 0, 128), V("om", 0, 128))
+    ts(V("pS", 256, 384), V("ZS0", 64, 192), 0.0, ALU.is_le)
+    for i in range(16):
+        cp(V("WP", 128 * i + i, 128 * i + 128, 16), V("GP", 0, 8))
+    for L in range(4):
+        ts(V("NS0", 32 * L, 32 * L + 32), V("nli", L, 128, 4), 1, ALU.add)
+    cp(V("OU0", 0, 128), V("OW0", 0, 128))
+    tt(V("NM", 0, 128), V("pS", 256, 384), V("NS0", 0, 128), ALU.mult)
+    tile("ztb", "ZS0")
+    tile_end("ztb", act)
+    act(*pgather(0, 64))
+    cp(*pgather(64, 128))
+    for i in range(16):
+        act(V("W", 128 * i + i, 128 * i + 128, 16), V("GA", 0, 8))
+    select(V("LT", 0, 128), V("GM", 0, 128), [[1, 128]], ALU.is_gt, 0, -1)
+    iota(V("mod16", 0, 128), [[0, 8], [1, 16]], 0, 0)
+    iota(V("colc", 0, 128), [[1, 128]], 0, 0)
+    iota(V("dump0", 0, 8), [[0, 2], [16, 4]], DUMP0, 0)
+    iota(V("dumpw", 0, 128), [[16, 4], [0, 32]], DUMP0, 0)
+    select(V("SEG16", 0, 128), V("ones", 0, 128), [[0, 8], [1, 16]], ALU.is_gt, 0, 0)
+    select(V("SEG32", 0, 128), V("ones", 0, 128), [[0, 4], [1, 32]], ALU.is_gt, 0, 0)
+    select(ALL("GE1"), (T["ones"][0:8, 0:128], [("ones", 0, 128)]), [[1, 128]], ALU.is_ge, 0, -16)
+    select(ALL("GE"), ALL("GE1"), [[-1, 128]], ALU.is_ge, 15, 16)
+
+    def late_constants():
+        cp(ALL("thf"), ALL("thi"))
+        fill(ALL("oneb"), 1.0)
+        mm(V("pM", 128, 133), ALL("GE"), ALL("thf"))
+        line(ALL("CQ"), (T["colc"][0:1, 0:128], [("colc", 0, 128)]), -0.25, 31.75)
+        line(V("C2", 0, 128), V("colc", 0, 128), -0.5, 130560.0 + 63.5)
+        ts(V("DM", 0, 128), V("mod16", 0, 128), V("p16", 0, 1), ALU.is_equal)
+        ts(V("ND", 0, 128), V("mod16", 0, 128), V("p16", 0, 1), ALU.not_equal)
+        fill(V("ND", 128, 144), 1.0)
+        ts(V("dump", 0, 8), V("dump0", 0, 8), V("p16", 0, 1), ALU.add)
+        ts(V("OW1", 128, 256), V("dumpw", 0, 128), V("p16", 0, 1), ALU.add)
+        ts(V("OW0", 128, 256), V("dumpw", 0, 128), V("p16", 0, 1), ALU.add)
+        fill(V("GD", 192, 208), 0.0)
+        ts(V("LM", 0, 5), V("pM", 128, 133), 32.0, ALU.mult, 31.75, ALU.add)
+
+    for s in range(S):
+        par, nxp = s % 2, (s + 1) % 2
+        last = s == S - 1
+        zr, nr, hr, zs1 = "ZR%d" % s, "NR%d" % s, "HR%d" % s, "ZS%d" % (s + 1)
+        send("OU%d" % (s + 1), "OU%d" % s, 0, 128, "rO%d" % s)
+        send(zr, "ZS%d" % s, 0, 192, "rZ%d" % s)
+        for half in (0, 1):
+            a, b = 64 * half, 64 * half + 64
+            reduce16("PG", a, b, "WP", PB[half], (V("ID", 0, 128), V("NM", a, b)))
+            if half == 0 and s > 0:
+                mm(V("pM", 136, 137), V("GM", 0, 128), V("rs", 0, 1))
+        cp(V("RU", 0, 64), V(PB[0], 0, 64))
+        for L in (0, 1):
+            for j in (0, 1):
+                gather_abs(L, j, "RU", "ztb")
+        reduce16("AB", 0, 64, "W", "pUA", None)
+        if s > 0:
+            line(V("A32", 0, 1), V("pM", 136, 137), 32.0, A0)
+            line(V("Q32", 0, 128), V("OW%d" % par, 0, 128), 1184.0, V("A32", 0, 1))
+            tt(V("pS", 128, 256), V("pS", 0, 128), V("hN", 0, 128), ALU.mult)
+            cp(V("RU", 64, 128), V(PB[1], 0, 64))
+            tt(V("NS%d" % s, 0, 128), V("pS", 128, 256), V("NR%d" % (s - 1), 0, 128), ALU.add)
+        else:
+            line(V("OQ0", 0, 128), V("OW0", 0, 128), 1.0 / 32, -1.0 / 32)
+            line(V("Q32", 0, 128), V("OW0", 0, 128), 1184.0, A0)
+            cp(V("RU", 64, 128), V(PB[1], 0, 64))
+        for j in (0, 1):
+            gather_abs(2, j, "RU", "ztb")
+            if s > 0:
+                tile("ztc", zr, ((0,), (16,))[j])
+        reduce16("AB", 64, 96, "W", "pUB", None)
+        gather_abs(3, 0, "RU", "ztb")
+        if s > 0:
+            tile("ztc", zr, (32,))
+        h_of(0, s, lambda: gather_abs(3, 1, "RU", "ztb"))
+        reduce16("AB", 96, 128, "W", "pUC", None)
+        tile("ztc", zr, (64,) if s > 0 else (0, 16, 32, 64))
+        tile_end("ztc", act)
+        h_of(1, s)
+        date = V(zr, 64, 192)
+        if s == 0:
+            late_constants()
+
+        def known():
+            cp(V("OW%d" % nxp, 0, 128), V("OU%d" % (s + 1), 0, 128))
+            ts(V("e1", 0, 128), date, float(s), ALU.is_gt, -BIG, ALU.mult)
+            ts(V("e2", 0, 128), date, 99.0, ALU.is_lt)
+
+        if s > 0:
+            known()
+        h_of(2, s)
+        send(nr, "NS%d" % s, 0, 128, "rN%d" % s)
+        if s == 0:
+            known()
+        if last:
+            dma("s", "o_lo", V("LO", 0, 256), (T["PW"][0:128:16, 1:4097], [("PW", 1, 4097)]))
+            dma("s", "o_hi", V("LO", 256, 512), (T["PW"][1:128:16, 1:4097], [("PW", 1, 4097)]))
+        line(V("OQ%d" % nxp, 0, 128), V("OW%d" % nxp, 0, 128), 1.0 / 32, -1.0 / 32)
+        line(V("ST", 0, 128), date, -1.0, float(s + 2))
+        for half in (0, 1):
+            a, b = 64 * half, 64 * half + 64
+            for L in (2 * half, 2 * half + 1):
+                for j in (0, 1):
+                    gather_abs(L, j, hr, "ztc")
+            if last and half == 0:
+                line(V("pR", 256, 512), V("LO", 256, 512), 1.0, -1.0)
+            reduce16("AB", a, b, "W", KB[half], (ALL("oneb"), (T["CQ"][:, a:b], [("CQ", a, b)])))
+        cp(V("HW", 0, 128), V(hr, 0, 128))
+
+        def keys(half, between=None):
+            a, b = 64 * half, 64 * half + 64
+            kd = V(KB[half], 0, 64)
+            tt(V("K2", a, b), V("C2", a, b), kd, ALU.subtract)
+            scan(V("SM", a, b), V("SEG32", a, b), kd, ALU.mult, ALU.max)
+            if between is not None:
+                between()
+            scan(V("SM", 128 + a, 128 + b), V("SEG32", a, b), V("K2", a, b), ALU.mult, ALU.max)
+
+        def redeem(half, n):
+            a, b = 64 * half, 64 * half + 64
+            if n == 0:
+                tt(V("pS", a, b), V(KB[half], 0, 64), V("RT", a, b), ALU.is_le)
+            elif n == 1:
+                tt(V("pS", 128 + a, 128 + b), V("pS", a, b), V("ST", a, b), ALU.mult)
+            else:
+                tt(V("pS", 256 + a, 256 + b), V("pS", 128 + a, 128 + b), V(zr, 64 + a, 64 + b), ALU.add)
+
+        def refuse(L):
+            ts(V("RF", 32 * L, 32 * L + 32), V(KB[L // 2], 32 * (L % 2), 32 * (L % 2) + 32), V("gk", L, L + 1),
+               ALU.is_equal, 99.0, ALU.mult)
+
+        def newdate(half):
+            a, b = 64 * half, 64 * half + 64
+            tt(V(zs1, 64 + a, 64 + b), V("pS", 256 + a, 256 + b), V("RF", a, b), ALU.max)
+
+        def onward(n):
+            if last:
+                return
+            if n == 0:
+                ts(V("pS", 384, 512), V(zs1, 64, 192), float(s + 1), ALU.is_gt)
+            elif n == 1:
+                ts(V("pS", 256, 384), V(zs1, 64, 192), float(s + 1), ALU.is_le)
+            elif n == 2:
+                tt(V("om", 0, 128), V("pS", 384, 512), V("OW%d" % nxp, 0, 128), ALU.mult)
+            elif n == 3:
+                cp(V("OM", 0, 128), V("om", 0, 128))
+            else:
+                tt(V("NM", 0, 128), V("pS", 256, 384), V(nr, 0, 128), ALU.mult)
+
+        def write(L, win, fu, data):
+            cp(IND(win, V("fu", fu + 2 * L, fu + 2 * L + 1)), V(data, 16 * L, 16 * L + 16))
+
+        if last:
+            tt(V("YPg", 0, 256), V("pR", 256, 512), V("LO", 0, 256), ALU.add)
+            dma("s", "o_pf", (T["PF"][0:128:16, 1:4097], [("PF", 1, 4097)]), V("YPg", 0, 256))
+        tt(V("RT0", 0, 128), V("e1", 0, 128), V("e2", 0, 128), ALU.mult)
+        keys(0)
+        ts(V("RT", 0, 128), V("RT0", 0, 128), V("LM", s, s + 1), ALU.add)
+        tt(V("hN", 0, 128), V("HW", 0, 128), V(nr, 0, 128), ALU.subtract)
+        for n in (0, 1, 2):
+            redeem(0, n)
+        keys(1, lambda: redeem(1, 0))
+        lastk = V("SM", 31, 128, 32)
+        ts(V("nogo", 0, 4), lastk, V("LM", s, s + 1), ALU.is_le, 128.0, ALU.mult)
+        redeem(1, 1)
+        ts(V("KI", 0, 8), V("SM", 31, 256, 32), 4.0, ALU.mult)
+        ts(V("CI", 0, 8), V("KI", 0, 8), 127, ALU.bitwise_and)
+        tt(V("gk", 0, 4), lastk, V("nogo", 0, 4), ALU.subtract)
+        ts(V("OFF", 0, 8), V("CI", 0, 8), -1.0, ALU.mult, 127.0, ALU.add)
+        tt(V("CI", 8, 12), V("CI", 0, 4), V("nogo", 0, 4), ALU.subtract)
+        redeem(1, 2)
+        tt(V("GD", 0, 128), IND(V("HW", 0, 128), V("OFF", 0, 8)), V("DM", 0, 128), ALU.mult)
+        ts(V("OFF", 8, 12), V("CI", 8, 12), -1.0, ALU.mult, 127.0, ALU.add)
+        refuse(0)
+        tt(V("GD", 128, 192), IND(V("OW%d" % nxp, 0, 256), V("OFF", 8, 12)), V("DM", 0, 64), ALU.mult)
+        mm(V("pM", 0, 128), V("LT", 0, 128), V("GD", 64, 192))
+        mm(V("pR", 64, 128), V("GM", 0, 128), V("GD", 0, 64))
+        scan(V("OWN", 0, 144), V("ND", 0, 144), V("GD", 64, 208), ALU.mult, ALU.add)
+        refuse(1)
+        cp(V("HB", 0, 4), V("OWN", 15, 64, 16))
+        refuse(2)
+        refuse(3)
+        tt(V("gz", 0, 64), IND(XR, V("HB", 0, 4)), V(zr, 0, 64), ALU.add)
+        tt(V("E", 0, 128), V("OWN", 16, 144), V("pM", 0, 128), ALU.is_equal)
+        ts(V("zi", 0, 64), V("gz", 0, 64), 0.5, ALU.mult, -0.25, ALU.add)
+        if not last:
+            ts(V("hx", 0, 64), V("pR", 64, 128), V("q1", 0, 1), ALU.mult)
+        scan(V("F", 0, 128), V("SEG16", 0, 128), V("E", 0, 128), ALU.mult, ALU.max)
+        cp(V(zs1, 0, 64), V("zi", 0, 64))
+        if not last:
+            tile("ztb", zs1)
+            tt(V("PD", 0, 64), V("pR", 64, 128), V("hx", 0, 64), ALU.subtract)
+        else:
+            dma("a", "o_z", ALL("yz"), V(zs1, 0, 64))
+            ts(V("ht", 0, 64), V("pR", 64, 128), -1.0, ALU.add)
+        tt(V("f1", 0, 8), V("F", 15, 128, 16), V("dump", 0, 8), ALU.mult)
+        newdate(0)
+        newdate(1)
+        tt(V("f2", 0, 8), V("f1", 0, 8), V("OWN", 15, 128, 16), ALU.max)
+        onward(0)
+        cp(V("fu", 0, 16, 2), V("f2", 0, 8))
+        onward(1)
+        if not last:
+            for L in (3, 2, 1, 0):
+                write(L, PA, 8, "PD")
+                if L:
+                    onward(5 - L)
+            act(*pgather(0, 32))
+            cp(*pgather(32, 64))
+            act(*pgather(64, 112))
+            write(3, XA, 0, "zi")
+            tile_end("ztb", cp)
+            write(2, XA, 0, "zi")
+            op("v", lambda: g.vector.tensor_reduce(out=T["rs"][:, 0:1], in_=T["pS"][:, 0:128], axis=AxisListType.X, op=ALU.add),
+               [V("pS", 0, 128)], [V("rs", 0, 1)])
+            write(1, XA, 0, "zi")
+            cp(*pgather(112, 128))
+            write(0, XA, 0, "zi")
+        else:
+            tt(V("pS", 128, 256), V("pS", 0, 128), V("hN", 0, 128), ALU.mult)
+            for L in (3, 2, 1, 0):
+                write(L, XA, 0, "zi")
+                cp(V("YT", L, 128, 4), V(zs1, 64 + 32 * L, 96 + 32 * L))
+            dma("s", "o_x", ALL("yx"), V("XW", 1, 4097))
+            dma("a", "o_t", ALL("yt"), V("YT", 0, 128))
+            tt(V("NS%d" % (s + 1), 0, 128), V("pS", 128, 256), V(nr, 0, 128), ALU.add)
+            for L in (3, 2, 1, 0):
+                write(L, V("PF", 0, PADW), 8, "ht")
+                ts(V("YN", L, 128, 4), V("NS%d" % (s + 1), 32 * L, 32 * L + 32), -1.0, ALU.add)
+            dma("a", "o_p", ALL("yp"), (T["PF"][0:128:16, 1:4097], [("PF", 1, 4097)]))
+            dma("s", "o_n", ALL("yn"), V("YN", 0, 128))
+    for q in ("v", "a", "t", "p"):
+        g.wait_ge(T.sem[q], count[q])
+    g.wait_ge(T.sem["loc"], sent[0])
+    for n in DMAS:
+        g.wait_ge(T.sem[n], 16)
+    for s in range(S):
+        for k in RECV:
+            g.wait_ge(T.sem["%s%d" % (k, s)], len(topo.engines(prv, core)))

@@ -1,7 +1,7 @@
-from concourse.mybir import AluOpType as ALU, AxisListType, ActivationFunctionType as ACT
+from concourse.mybir import AluOpType as ALU, ActivationFunctionType as ACT
 
-S, PADW, DUMP0, TW = 5, 4176, 4097, 256
-BIG = 1.0e6
+S, B0, WW, TW = 5, 32, 4128, 512
+BIG, CUT, EVEN = 2097152.0, 8192.0, 25165824.0
 
 
 def _sb(n, dtype="float32", p=128):
@@ -9,47 +9,56 @@ def _sb(n, dtype="float32", p=128):
 
 
 SCRATCH = {
-    "XW": _sb(PADW, "bfloat16"), "PW": _sb(PADW, "bfloat16"), "PF": _sb(PADW),
-    "ztb": ("sbuf", [128, 4, TW], "bfloat16"), "ztc": ("sbuf", [128, 4, TW], "bfloat16"),
+    "XW": _sb(WW, "bfloat16"), "PW": _sb(WW, "bfloat16"), "PF": _sb(WW),
     "DF": _sb(2048, "bfloat16"), "AB": _sb(2048, "bfloat16"), "PG": _sb(2048, "bfloat16"),
-    "W": _sb(2048, "bfloat16"), "WP": _sb(2048, "bfloat16"),
+    "DG": _sb(2048, "bfloat16"), "AC": _sb(2048, "bfloat16"),
+    "Z1": _sb(144, "bfloat16"), "ZK": _sb(144, "bfloat16"),
     "pxi": _sb(256, "int32"), "pxt": _sb(256, "int32"), "LH": _sb(512, "bfloat16"),
     "oli": _sb(128, "int32"), "nli": _sb(128, "int32"), "tli": _sb(128, "int32"),
     "thi": _sb(5, "int32", 8), "thf": _sb(5, "float32", 8), "GE1": _sb(128, "float32", 8), "GE": _sb(128, "float32", 8),
-    "ones": _sb(128), "oneb": _sb(128, "bfloat16", 1), "CQ": _sb(128, "bfloat16", 1),
-    "G1": _sb(128), "GM": _sb(128), "ID": _sb(128), "LT": _sb(128), "GA": _sb(8), "GP": _sb(8),
-    "mod16": _sb(128), "colc": _sb(128), "C2": _sb(128), "SEG16": _sb(128), "SEG32": _sb(128), "DM": _sb(128), "ND": _sb(144),
-    "pidx": _sb(1, "int32"), "p16i": _sb(1, "int32"), "p16": _sb(1), "q0": _sb(1), "q1": _sb(1), "wp": _sb(1),
-    "dump0": _sb(8), "dump": _sb(8), "dumpw": _sb(128), "LM": _sb(5),
-    "OW0": _sb(256), "OW1": _sb(256), "OQ0": _sb(128), "OQ1": _sb(128), "HW": _sb(128), "Q32": _sb(128), "A32": _sb(1), "rs": _sb(1),
-    "om": _sb(128), "OM": _sb(128, "uint16"), "NM": _sb(128), "RU": _sb(128, "uint16"),
+    "ones": _sb(128), "oneb": _sb(128, "bfloat16", 1), "mid": _sb(128, "bfloat16", 1),
+    "G1": _sb(128), "GM": _sb(128), "GMb": _sb(128, "bfloat16"), "G01": _sb(128), "ID": _sb(128), "NID": _sb(128), "NIb": _sb(128, "bfloat16"),
+    "mod16": _sb(128), "colc": _sb(128), "DM": _sb(128), "ND": _sb(128), "UP": _sb(32), "DN": _sb(32), "L8": _sb(8),
+    "pidx": _sb(1, "int32"), "p16i": _sb(1, "int32"), "p16": _sb(1), "q1": _sb(1), "dump": _sb(1), "LM": _sb(5),
+    "HW": _sb(136), "Q": _sb(128), "A32": _sb(1), "junk": _sb(128),
+    "OM": _sb(128, "uint16"), "NM": _sb(128), "RU": _sb(128, "uint16"), "r12": _sb(256, "bfloat16"),
     "hm": _sb(128), "hv": _sb(128, "int32"), "hs": _sb(128, "int32"),
-    "e1": _sb(128), "e2": _sb(128), "RT0": _sb(128), "RT": _sb(128), "ST": _sb(128), "hN": _sb(128), "K2": _sb(128), "SM": _sb(256),
-    "KI": _sb(8, "int32"), "CI": _sb(12, "int32"), "nogo": _sb(4, "int32"), "gk": _sb(4), "OFF": _sb(12, "uint16"),
-    "GD": _sb(208), "OWN": _sb(144), "HB": _sb(4, "uint16"), "gz": _sb(64), "zi": _sb(64, "int32"),
-    "E": _sb(128), "F": _sb(128), "f1": _sb(8), "f2": _sb(8), "fu": _sb(16, "uint16"),
-    "hx": _sb(64, "bfloat16"), "ht": _sb(64), "PD": _sb(64, "bfloat16"), "RF": _sb(128),
+    "e1": _sb(128), "e2": _sb(128), "RT": _sb(128), "red": _sb(128, "bfloat16"), "SM": _sb(256), "zh": _sb(64),
+    "KI": _sb(8, "int32"), "CI": _sb(8, "int32"), "NC": _sb(4), "OFF": _sb(8, "uint16"),
+    "GD": _sb(192), "OWN": _sb(128), "NE": _sb(128), "FS": _sb(128), "fu": _sb(16, "uint16"),
+    "HB": _sb(4, "uint16"), "gz": _sb(64), "ev": _sb(64),
+    "hx": _sb(64, "bfloat16"), "ht": _sb(64), "PD": _sb(64, "bfloat16"), "rf": _sb(128), "RF": _sb(128),
     "YN": _sb(128), "YT": _sb(128), "YPg": _sb(256), "LO": _sb(512, "bfloat16"),
-    "ZR": _sb(192 * S, "bfloat16"),
+    "ZC": _sb((128 + TW) * S, "bfloat16"),
     "NR": _sb(128 * S),
     "HS": _sb(128 * S, "uint16"),
     "HR": _sb(128 * S, "uint16"),
-    "OU": _sb(128 * (S + 1), "uint16"),
-    "ZS": _sb(192 * (S + 1), "bfloat16"),
+    "OW": _sb(136 * (S + 1)),
+    "ZT": _sb((128 + TW) * (S + 1), "bfloat16"),
     "NS": _sb(128 * (S + 1)),
 }
-for _n in ("pUA", "pUB", "pUC", "pPA", "pPB", "pR", "pM", "pS"):
+for _n in ("pU0", "pU1", "pU2", "pP0", "pP1", "pR", "pM", "pS"):
     SCRATCH[_n] = ("psum", [128, 512], "float32")
 PIECE = {"%s%d" % (k, s): (k, SCRATCH[k][1][1] // n * s) for k, n in
-         (("ZR", S), ("NR", S), ("HS", S), ("HR", S), ("OU", S + 1), ("ZS", S + 1), ("NS", S + 1)) for s in range(n)}
-RECV = ("rO", "rZ", "rA", "rB", "rC", "rN")
-DMAS = ["d_px", "d_ol", "d_z", "d_tl", "d_nl", "d_th", "d_x", "d_lo", "d_hi",
+         (("ZC", S), ("NR", S), ("HS", S), ("HR", S), ("OW", S + 1), ("ZT", S + 1), ("NS", S + 1)) for s in range(n)}
+PGATHER = (("a", 0, 16), ("v", 16, 32), ("a", 32, 64), ("a", 64, 96), ("a", 96, 128))
+ROADS = ((0, 32), (32, 64), (64, 96), (96, 128))
+UGATHER = ((0, 32), (32, 64), (64, 80), (80, 96), (96, 112), (112, 128))
+HPIECES = ((0, 32), (32, 64), (64, 96), (96, 128))
+DGATHER = ((0, 32), (32, 64), (64, 96), (96, 112), (112, 128))
+DSUMS = ((0, 64), (64, 128))
+TILEB, TILEC, ROUNDS = "aav", "ppp", 2
+RECV = ("rO", "rZ", "rN") + tuple("rH%d_" % i for i in range(len(HPIECES)))
+DMAS = ["d_px", "d_ol", "d_z", "d_tl", "d_nl", "d_th", "d_x", "d_x2", "d_lo", "d_hi",
         "o_x", "o_lo", "o_hi", "o_pf", "o_p", "o_z", "o_n", "o_t"]
 SEMAPHORES = ["v", "a", "t", "p", "loc"] + ["%s%d" % (k, s) for s in range(S) for k in RECV] + DMAS
-HP = ((0, 64, "pUA", "rA"), (64, 96, "pUB", "rB"), (96, 128, "pUC", "rC"))
-KB = ("pUA", "pUB")
-PB = ("pPA", "pPB")
-A0 = -8388608.0 - 1184.0
+UB = ("pU0", "pU1", "pU2", "pU0")
+PB = ("pP0", "pP1", "pP0", "pP1")
+KD = "pU1"
+A0 = 65536.0 - 8388608.0 - 3232.0 * B0
+INORDER = True
+CALL, GATHER, SCATTER, PE, WAKE, LOAD, HOP = 60, 1.56, 3.8, 0.55, 150, 1900, 1900
+PLAN = {}
 
 
 def rank_program(g, core, T, topo):
@@ -59,76 +68,140 @@ def rank_program(g, core, T, topo):
     nxt = T.cores[(rank + 1) % len(T.cores)]
     prv = T.cores[(rank - 1) % len(T.cores)]
     queues = {"v": g.vector, "a": g.scalar, "t": g.tensor, "p": g, "s": g.sync}
-    count = {"v": 0, "a": 0, "t": 0, "p": 0}
-    seen = {q: {} for q in queues}
-    acc = {}
     psum = set(n for n in SCRATCH if SCRATCH[n][0] == "psum")
+    nodes, acc = [], {}
 
-    def need(q, regs, write, needs):
-        for (n, lo, hi) in regs:
-            for (qa, sem, val, alo, ahi, aw) in acc.get(n, ()):
-                apart = ahi <= lo or alo >= hi
-                if n in psum and qa != q:
-                    apart = False
-                elif apart or not (aw or write) or (qa == q and write and q == "t"):
-                    continue
-                needs[sem] = max(needs.get(sem, 0), val)
+    def node(q, calls, rd, wr, busy, lag=0.0, signal=None, beside=None):
+        me, before = len(nodes), {}
+        for views, write in ((rd, False), (wr, True)):
+            for (n, lo, hi) in [r for v in views for r in v[1]]:
+                for (k, alo, ahi, aw) in acc.get(n, ()):
+                    same = nodes[k]["q"] == q and nodes[k]["signal"] is None and signal is None
+                    if k == beside or (not (n in psum and (not same or q == "t")) and (ahi <= lo or alo >= hi or not (aw or write))):
+                        continue
+                    before[k] = before.get(k, False) or not (same and write and (q == "t" or n[:4] == "turn" or (INORDER and not aw)))
+        nodes.append({"q": q, "calls": calls, "before": before, "busy": busy, "lag": lag, "signal": signal})
+        for views, write in ((rd, False), (wr, True)):
+            for (n, lo, hi) in [r for v in views for r in v[1]]:
+                old = acc.get(n, [])
+                if write and n not in psum and beside is None:
+                    old = [a for a in old if not (lo <= a[1] and a[2] <= hi)]
+                acc[n] = old + [(me, lo, hi, write)]
+        return me
 
-    def note(q, sem, val, regs, write):
-        for (n, lo, hi) in regs:
-            old = acc.get(n, [])
-            if write:
-                old = [a for a in old if not (lo <= a[3] and a[4] <= hi)]
-            acc[n] = old + [(q, sem, val, lo, hi, write)]
+    def width(name):
+        return 2 if SCRATCH[name][2] in ("bfloat16", "uint16") else 4
 
-    def waits(q, rd, wr):
-        needs = {}
-        need(q, rd, False, needs)
-        need(q, wr, True, needs)
-        for sem in sorted(needs):
-            if seen[q].get(sem, 0) < needs[sem]:
-                queues[q].wait_ge(T.sem[sem], needs[sem])
-                seen[q][sem] = needs[sem]
+    def cycles(o, ins, both):
+        if len(ins[0]) > 3:
+            return CALL + GATHER * ins[0][2]
+        if len(o) > 3:
+            return CALL + SCATTER * o[2]
+        if both:
+            return max(64, ins[0][2] * (1 if any(v[1][0][0] in psum for v in ins) else 2))
+        return max(64, ins[0][2] * (0.5 if all(width(v[1][0][0]) == 2 for v in [o] + ins) else 1))
 
-    def regs(views):
-        return [r for v in views for r in v[1]]
-
-    def op(q, call, rd, wr):
-        rd, wr = regs(rd), regs(wr)
-        waits(q, rd, wr)
-        count[q] += 1
-        call().then_inc(T.sem[q], 1)
-        note(q, q, count[q], rd, False)
-        note(q, q, count[q], wr, True)
-
-    def dma(q, sem, out, in_):
-        waits(q, in_[1], out[1])
-        queues[q].dma_start(out=out[0], in_=in_[0]).then_inc(T.sem[sem], 16)
-        note("d" + sem, sem, 16, in_[1], False)
-        note("d" + sem, sem, 16, out[1], True)
-
-    sent = [0]
+    def dma(q, sem, out, in_, size, beside=None, behind=()):
+        return node(q, [lambda: queues[q].dma_start(out=out[0], in_=in_[0])], [in_] + list(behind), [out], 60, LOAD + size / 300.0,
+                    (sem, 16), beside)
 
     def send(dst_name, src_name, lo, hi, sem):
         src, dst = V(src_name, lo, hi), V(dst_name, lo, hi)
-        waits("p", src[1], [])
         rid, pid, _ = topo.addr(nxt)
-        g.remote_dma(out_ap=dst[0], in_ap=src[0], remote_sem=T.sem[sem], local_sem=T.sem["loc"],
-                     pid=pid, routing_id=rid, dma_engine_mask=topo.mask(core, nxt))
-        sent[0] += len(topo.engines(core, nxt))
-        note("r", sem, len(topo.engines(prv, core)), dst[1], True)
+        node("p", [lambda: g.remote_dma(out_ap=dst[0], in_ap=src[0], remote_sem=T.sem[sem], local_sem=T.sem["loc"],
+                                        pid=pid, routing_id=rid, dma_engine_mask=topo.mask(core, nxt))],
+             [src], [dst], 180 + 128 * src[2] * width(src[1][0][0]) / 55.0, HOP, (sem, len(topo.engines(prv, core))))
+
+    def issue():
+        n = len(nodes)
+        before = [{j: nodes[j]["lag"] + WAKE if hard else 0.0 for j, hard in nd["before"].items()} for nd in nodes]
+        after = [{} for _ in nodes]
+        for k in range(n):
+            for j, gap in before[k].items():
+                after[j][k] = gap
+
+        def place(pre, post, head, urgency):
+            missing = [len(p) for p in pre]
+            ready = {k: head[k] for k in range(n) if not missing[k]}
+            order, end = {q: [] for q in queues}, [0.0] * n
+            while ready:
+                k = max(ready, key=lambda j: (urgency[j], -j))
+                at, busy, taken = ready.pop(k), nodes[k]["busy"], order[nodes[k]["q"]]
+                i = len(taken)
+                while i and end[taken[i - 1]] > at:
+                    i -= 1
+                while i < len(taken) and end[taken[i]] - nodes[taken[i]]["busy"] < at + busy:
+                    at = max(at, end[taken[i]])
+                    i += 1
+                taken.insert(i, k)
+                end[k] = at + busy
+                for j in post[k]:
+                    missing[j] -= 1
+                    if not missing[j]:
+                        ready[j] = max([head[j]] + [end[i] + gap for i, gap in pre[j].items()])
+            return max(end[k] + nodes[k]["lag"] for k in range(n)), order, end
+
+        if "order" not in PLAN:
+            back, best = [0.0] * n, None
+            for k in range(n - 1, -1, -1):
+                back[k] = nodes[k]["busy"] + max([nodes[k]["lag"]] + [back[j] + gap for j, gap in after[k].items()])
+            for _ in range(ROUNDS):
+                span, order, end = place(before, after, [0.0] * n, back)
+                if best is None or span < best:
+                    best, PLAN["order"] = span, order
+                PLAN.setdefault("spans", []).append(span)
+                back = place(after, before, [nd["lag"] for nd in nodes], end)[2]
+        order = PLAN["order"]
+        count = {}
+        for q in queues:
+            for k in order[q]:
+                if nodes[k]["signal"] is None:
+                    count[q] = count.get(q, 0) + 1
+                    nodes[k]["done"] = (q, count[q])
+                else:
+                    nodes[k]["done"] = nodes[k]["signal"]
+        for q in queues:
+            seen = {}
+            for k in order[q]:
+                needs = {}
+                for j, hard in nodes[k]["before"].items():
+                    if hard:
+                        sem, val = nodes[j]["done"]
+                        needs[sem] = max(needs.get(sem, 0), val)
+                for sem in sorted(needs):
+                    if seen.get(sem, 0) < needs[sem]:
+                        queues[q].wait_ge(T.sem[sem], needs[sem])
+                        seen[sem] = needs[sem]
+                made = [call() for call in nodes[k]["calls"]]
+                if nodes[k]["signal"] is None:
+                    made[-1].then_inc(T.sem[q], 1)
+                elif q != "p":
+                    made[-1].then_inc(T.sem[nodes[k]["signal"][0]], 16)
+        for q in count:
+            g.wait_ge(T.sem[q], count[q])
+        g.wait_ge(T.sem["loc"], len(topo.engines(core, nxt)) * len([nd for nd in nodes if nd["q"] == "p" and nd["signal"]]))
+        for nd in nodes:
+            if nd["signal"]:
+                g.wait_ge(T.sem[nd["signal"][0]], nd["signal"][1])
 
     def V(name, lo, hi, st=1):
         if name in PIECE:
             name, base = PIECE[name]
             lo, hi = lo + base, hi + base
-        return (T[name][:, lo:hi] if st == 1 else T[name][:, lo:hi:st], [(name, lo, hi)])
+        return (T[name][:, lo:hi] if st == 1 else T[name][:, lo:hi:st], [(name, lo, hi)], len(range(lo, hi, st)))
+
+    def BACK(name, lo, hi):
+        return (T[name][:, hi - 1::-1] if lo == 0 else T[name][:, hi - 1:lo - 1:-1], [(name, lo, hi)], hi - lo)
 
     def ALL(name):
-        return (T[name][:], [(name, 0, SCRATCH[name][1][1] if name in SCRATCH else 1)])
+        n = SCRATCH[name][1][1] if name in SCRATCH else 1
+        return (T[name][:], [(name, 0, n)], n)
+
+    def ROW(name, first):
+        return (T[name][first:128:16, B0:WW], [(name, B0, WW)], WW - B0)
 
     def IND(win, off):
-        return (win[0].indirect(off[0]), win[1] + off[1])
+        return (win[0].indirect(off[0]), win[1] + off[1], 16 * off[2], off)
 
     def cols(*vs):
         return [v for v in vs if not isinstance(v, (int, float)) and v is not None]
@@ -136,356 +209,238 @@ def rank_program(g, core, T, topo):
     def raw(v):
         return v if isinstance(v, (int, float)) or v is None else v[0]
 
+    def op(q, call, rd, wr, busy):
+        turn = [(None, [("turn" + q, 0, 1)])] if rd and len(rd[0]) > 3 and rd[0][2] >= 256 else []
+        node(q, [call], rd + [o[3] for o in wr if len(o) > 3], [(o[0], o[1][:1]) for o in wr] + turn, busy)
+
     def tt(o, a, b, f):
-        op("v", lambda: g.vector.tensor_tensor(out=o[0], in0=a[0], in1=b[0], op=f), [a, b], [o])
+        op("v", lambda: g.vector.tensor_tensor(out=o[0], in0=a[0], in1=b[0], op=f), [a, b], [o], cycles(o, [a, b], True))
 
     def ts(o, a, s1, f1, s2=None, f2=None):
         if f2 is None:
-            op("v", lambda: g.vector.tensor_scalar(out=o[0], in0=a[0], scalar1=raw(s1), scalar2=None, op0=f1), [a] + cols(s1), [o])
+            op("v", lambda: g.vector.tensor_scalar(out=o[0], in0=a[0], scalar1=raw(s1), scalar2=None, op0=f1), [a] + cols(s1), [o],
+               cycles(o, [a], False))
         else:
             op("v", lambda: g.vector.tensor_scalar(out=o[0], in0=a[0], scalar1=raw(s1), scalar2=raw(s2), op0=f1, op1=f2),
-               [a] + cols(s1, s2), [o])
+               [a] + cols(s1, s2), [o], cycles(o, [a], False))
 
     def cp(o, a):
-        op("v", lambda: g.vector.tensor_copy(out=o[0], in_=a[0]), [a], [o])
+        op("v", lambda: g.vector.tensor_copy(out=o[0], in_=a[0]), [a], [o], cycles(o, [a], False))
 
-    def scan(o, d0, d1, f0, f1):
-        op("v", lambda: g.vector.tensor_tensor_scan(out=o[0], data0=d0[0], data1=d1[0], initial=0.0, op0=f0, op1=f1), [d0, d1], [o])
+    def scan(o, d0, d1, first, f0, f1):
+        op("v", lambda: g.vector.tensor_tensor_scan(out=o[0], data0=d0[0], data1=d1[0], initial=raw(first), op0=f0, op1=f1),
+           [d0, d1] + cols(first), [o], cycles(o, [d0, d1], False))
 
     def fill(o, c):
-        op("v", lambda: g.vector.memset(o[0], c), [], [o])
+        op("v", lambda: g.vector.memset(o[0], c), [], [o], cycles(o, [o], False))
 
     def act(o, a, f=ACT.Copy):
-        op("a", lambda: g.scalar.activation(out=o[0], in_=a[0], func=f), [a], [o])
+        op("a", lambda: g.scalar.activation(out=o[0], in_=a[0], func=f), [a], [o], CALL + GATHER * a[2] if len(a) > 3 else max(64, a[2]))
 
-    def line(o, a, scale, bias):
-        op("a", lambda: g.scalar.activation(out=o[0], in_=a[0], func=ACT.Identity, bias=raw(bias), scale=scale), [a] + cols(bias), [o])
+    def line(o, a, scale, bias, f=ACT.Identity, total=None):
+        op("a", lambda: g.scalar.activation(out=o[0], in_=a[0], func=f, bias=raw(bias), scale=raw(scale), accum_out=raw(total)),
+           [a] + cols(bias, scale), [o] + cols(total), max(64, a[2]))
+
+    def mms(o, pairs, start=True, stop=True):
+        node("t", [lambda l=l, r=r, i=i: g.tensor.matmul(out=o[0], lhsT=l[0], rhs=r[0], start=start and i == 0,
+                                                         stop=stop and i == len(pairs) - 1) for i, (l, r) in enumerate(pairs)],
+             [v for p in pairs for v in p], [o], sum(PE * max(64, r[2]) * width(r[1][0][0]) ** 2 / 4 for l, r in pairs))
 
     def mm(o, l, r, start=True, stop=True):
-        op("t", lambda: g.tensor.matmul(out=o[0], lhsT=l[0], rhs=r[0], start=start, stop=stop), [l, r], [o])
+        mms(o, [(l, r)], start, stop)
 
     def iota(o, pattern, base, cm):
-        op("p", lambda: g.iota(o[0], pattern, base, cm, allow_small_or_imprecise_dtypes=True), [], [o])
+        op("p", lambda: g.iota(o[0], pattern, base, cm, allow_small_or_imprecise_dtypes=True), [], [o], 150 + 2 * o[2])
 
     def select(o, a, pattern, f, base, cm):
-        op("p", lambda: g.affine_select(o[0], a[0], pattern, f, 0.0, base, cm), [a], [o])
+        op("p", lambda: g.affine_select(o[0], a[0], pattern, f, 0.0, base, cm), [a], [o], 200 + 2 * o[2])
 
-    XR, PR = V("XW", 0, 4112), V("PW", 0, 4112)
-    XA, PA = V("XW", 0, PADW), V("PW", 0, PADW)
+    def pool_copy(o, a):
+        select(o, a, [[0, o[2]]], ALU.is_ge, 0, 0)
 
-    def tile(name, src, steps=(0, 16, 32, 64)):
-        t = T[name]
-        for w in steps:
-            if w == 0:
-                act((t[:, :, 0:16], [(name, 0, 16)]), V(src, 0, 64))
-            else:
-                act((t[:, :, w:2 * w], [(name, w, 2 * w)]), (t[:, :, 0:w], [(name, 0, w)]))
+    XA, PA = V("XW", 0, WW), V("PW", 0, WW)
+    copy = {"v": cp, "a": act, "p": pool_copy}
 
-    def tile_end(name, copy):
-        t = T[name]
-        copy((t[:, :, 128:256], [(name, 128, 256)]), (t[:, :, 0:128], [(name, 0, 128)]))
+    def tile(name, engines):
+        for w, e in zip((64, 128, 256), engines):
+            copy[e](V(name, 128 + w, 128 + 2 * w), V(name, 128, 128 + w))
 
-    def pgather(a, b):
-        return V("PG", 16 * a, 16 * b), IND(PR, V("OM", a, b))
-
-    def reduce16(src, c0, c1, w, bank, first):
-        out = V(bank, 0, c1 - c0)
+    def reduce16(src, c0, c1, w, out, first):
         if first is not None:
             mm(out, first[0], first[1], True, False)
-        for i in range(16):
-            mm(out, V(w, 128 * i, 128 * i + 128), (T[src][:, 16 * c0 + i:16 * c1:16], [(src, 16 * c0, 16 * c1)]),
-               first is None and i == 0, i == 15)
+        mms(out, [(V(w, 15 - i, 143 - i), V(src, 16 * c0 + i, 16 * c1, 16)) for i in range(16)], first is None, True)
 
-    def gather_abs(L, j, off, tname):
-        lo = 512 * L + TW * j
-        tt(V("DF", lo, lo + TW), IND(XR, V(off, lo // 16, (lo + TW) // 16)), (T[tname][:, L, 0:TW], [(tname, 0, TW)]), ALU.subtract)
-        act(V("AB", lo, lo + TW), V("DF", lo, lo + TW), ACT.Abs)
+    def distance(df, ab, a, b, off, tname):
+        tt(V(df, 16 * a, 16 * b), IND(XA, V(off, a, b)), V(tname, 128, 128 + 16 * (b - a)), ALU.subtract)
+        act(V(ab, 16 * a, 16 * b), V(df, 16 * a, 16 * b), ACT.Abs)
 
-    def h_of(piece, s, between=None):
-        a, b, bank, sem = HP[piece]
-        u = V(bank, 0, b - a)
-        tt(V("hm", a, b), u, V("OQ%d" % (s % 2), a, b), ALU.mult)
-        tt(V("pS", 256 + a, 256 + b), u, V("Q32", a, b), ALU.add)
-        if between is not None:
-            between()
-        tt(V("hv", a, b), V("pS", 256 + a, 256 + b), V("hm", a, b), ALU.add)
+    def h_of(q, s):
+        a, b = HPIECES[q]
+        reduce16("AB", a, b, "Z1", V(UB[q], 0, b - a), (ALL("oneb"), V("mid", 0, b - a)))
+        tt(V("hm", a, b), V(UB[q], 0, b - a), V("OW%d" % s, 8 + a, 8 + b), ALU.mult)
+        tt(V("hv", a, b), V("hm", a, b), V("Q", a, b), ALU.add)
         ts(V("hs", a, b), V("hv", a, b), 5, ALU.arith_shift_right, 4095, ALU.bitwise_and)
-        ts(V("HS%d" % s, a, b), V("hs", a, b), 1.0, ALU.add)
-        send("HR%d" % s, "HS%d" % s, a, b, "%s%d" % (sem, s))
+        ts(V("HS%d" % s, a, b), V("hs", a, b), float(B0), ALU.add)
+        send("HR%d" % s, "HS%d" % s, a, b, "rH%d_%d" % (q, s))
 
-    dma("s", "d_px", V("pxi", 0, 256), ALL("px"))
-    dma("a", "d_ol", V("oli", 0, 128), ALL("ol"))
-    dma("s", "d_z", V("ZS0", 0, 64), ALL("z"))
-    dma("a", "d_tl", V("tli", 0, 128), ALL("tl"))
+    def ways_open(s, names):
+        mm(V("pP1", 0, 128), V("ID", 0, 128), V("OW%d" % s, 8, 136), True, False)
+        mm(V("pU2", 0, 128), V("ID", 0, 128), names, True, False)
+
+    def ways(s):
+        date = V("ZT%d" % s, 0, 128)
+        line(V("r12", 0, 128), date, -CUT, CUT * (s + 1), ACT.Relu)
+        mm(V("pP1", 0, 128), V("NIb", 0, 128), V("r12", 0, 128), False, True)
+        cp(V("OM", 0, 128), V("pP1", 0, 128))
+        line(V("r12", 128, 256), date, CUT, -CUT * s, ACT.Relu)
+        mm(V("pU2", 0, 128), V("NIb", 0, 128), V("r12", 128, 256), False, True)
+        act(V("NM", 0, 128), V("pU2", 0, 128), ACT.Relu)
+
+    def write(win, fu, data, base=0):
+        for L in (3, 2, 1, 0):
+            cp(IND(win, V("fu", fu + 2 * L, fu + 2 * L + 1)), V(data, base + 16 * L, base + 16 * L + 16))
+
+    dma("s", "d_px", V("pxi", 0, 256), ALL("px"), 131072)
+    dma("a", "d_ol", V("oli", 0, 128), ALL("ol"), 65536)
+    dma("s", "d_tl", V("tli", 0, 128), ALL("tl"), 65536)
+    dma("a", "d_nl", V("nli", 0, 128), ALL("nl"), 65536)
+    dma("s", "d_z", V("ZT0", 128, 192), ALL("z"), 16384)
+    dma("a", "d_th", ALL("thi"), ALL("th"), 160)
+    dma("s", "d_x", V("XW", B0, B0 + 2048), (T["x"][:, 0:2048], []), 0)
     fill(V("ones", 0, 128), 1.0)
-    fill(V("XW", 0, 16), 0.0)
-    fill(V("XW", 4096, PADW), 0.0)
-    dma("s", "d_x", V("XW", 1, 4097), ALL("x"))
-    dma("a", "d_nl", V("nli", 0, 128), ALL("nl"))
-    dma("a", "d_th", ALL("thi"), ALL("th"))
-    iota(V("pidx", 0, 1), [[0, 1]], 0, 1)
+    fill(V("PW", 0, WW), 0.0)
+    select(V("ID", 0, 128), V("ones", 0, 128), [[1, 128]], ALU.is_equal, 0, -1)
     select(V("G1", 0, 128), V("ones", 0, 128), [[-16, 8], [0, 16]], ALU.is_ge, 0, 1)
     select(V("GM", 0, 128), V("G1", 0, 128), [[16, 8], [0, 16]], ALU.is_ge, 15, -1)
-    select(V("ID", 0, 128), V("ones", 0, 128), [[1, 128]], ALU.is_equal, 0, -1)
-    iota(V("W", 0, 2048), [[0, 2048]], 0, 0)
-    fill(V("PW", 0, PADW), 0.0)
-    ts(V("LH", 256, 512), V("pxi", 0, 256), 1, ALU.add)
-    waits("a", [("LH", 256, 512), ("PW", 0, PADW)], [])
-    g.scalar.dma_start(out=T["PW"][1:128:16, 1:4097], in_=T["LH"][:, 256:512]).then_inc(T.sem["d_hi"], 16)
-    ts(V("pxt", 0, 256), V("pxi", 0, 256), 1, ALU.add)
-    ts(V("p16i", 0, 1), V("pidx", 0, 1), 15, ALU.bitwise_and)
+    fill(V("XW", 0, B0), 0.0)
+    fill(V("Z1", 0, 144), 0.0)
+    fill(V("OW0", 0, 8), 0.0)
+    ts(V("LH", 256, 512), V("pxi", 0, 256), B0, ALU.add)
+    high = dma("a", "d_hi", ROW("PW", 1), V("LH", 256, 512), 65536)
+    ts(V("pxt", 0, 256), V("pxi", 0, 256), B0, ALU.add)
     tt(V("LH", 0, 256), V("pxt", 0, 256), V("LH", 256, 512), ALU.subtract)
-    dma("s", "d_lo", (T["PW"][0:128:16, 1:4097], [("PW", 1, 4097)]), V("LH", 0, 256))
-    note("dd_hi", "d_hi", 16, [("LH", 256, 512)], False)
-    acc["PW"] = acc["PW"] + [("dd_hi", "d_hi", 16, 1, 4097, True)]
-    cp(V("p16", 0, 1), V("p16i", 0, 1))
-    for L in range(4):
-        cp(V("ZS0", 64 + 32 * L, 96 + 32 * L), V("tli", L, 128, 4))
-    ts(V("q0", 0, 1), V("p16", 0, 1), 0.0, ALU.is_equal)
-    ts(V("q1", 0, 1), V("p16", 0, 1), 1.0, ALU.is_equal)
-    for L in range(4):
-        ts(V("OW0", 32 * L, 32 * L + 32), V("oli", L, 128, 4), 1, ALU.add)
-    ts(V("pS", 384, 512), V("ZS0", 64, 192), 0.0, ALU.is_gt)
-    tt(V("wp", 0, 1), V("q1", 0, 1), V("q0", 0, 1), ALU.add)
-    ts(V("GA", 0, 8), V("GM", 0, 128, 16), 32.0, ALU.mult)
-    tt(V("om", 0, 128), V("pS", 384, 512), V("OW0", 0, 128), ALU.mult)
-    ts(V("GP", 0, 8), V("GM", 0, 128, 16), V("wp", 0, 1), ALU.mult)
-    fill(V("WP", 0, 2048), 0.0)
-    cp(V("OM", 0, 128), V("om", 0, 128))
-    ts(V("pS", 256, 384), V("ZS0", 64, 192), 0.0, ALU.is_le)
-    for i in range(16):
-        cp(V("WP", 128 * i + i, 128 * i + 128, 16), V("GP", 0, 8))
-    for L in range(4):
-        ts(V("NS0", 32 * L, 32 * L + 32), V("nli", L, 128, 4), 1, ALU.add)
-    cp(V("OU0", 0, 128), V("OW0", 0, 128))
-    tt(V("NM", 0, 128), V("pS", 256, 384), V("NS0", 0, 128), ALU.mult)
-    tile("ztb", "ZS0")
-    tile_end("ztb", act)
-    act(*pgather(0, 64))
-    cp(*pgather(64, 128))
-    for i in range(16):
-        act(V("W", 128 * i + i, 128 * i + 128, 16), V("GA", 0, 8))
-    select(V("LT", 0, 128), V("GM", 0, 128), [[1, 128]], ALU.is_gt, 0, -1)
+    dma("s", "d_lo", ROW("PW", 0), V("LH", 0, 256), 65536, high)
+    dma("s", "d_x2", V("XW", B0 + 2048, WW), (T["x"][:, 2048:4096], []), 0, None, [V("LH", 0, 256)])
+    ts(V("OW0", 8, 136), V("oli", 0, 128), B0, ALU.add)
+    cp(V("ZT0", 0, 128), V("tli", 0, 128))
+    ts(V("NS0", 0, 128), V("nli", 0, 128), B0, ALU.add)
+    line(V("NIb", 0, 128), V("ID", 0, 128), -1.0, 0.0)
+    ways_open(0, V("NS0", 0, 128))
+    ways(0)
+    cp(V("Z1", 15, 143, 16), V("GM", 0, 128, 16))
+    tile("ZT0", "vvv")
+    line(V("Q", 0, 128), V("OW0", 8, 136), 3232.0, A0)
+    fill(ALL("oneb"), 1.0)
+    fill(ALL("mid"), -2048.0)
+    iota(V("pidx", 0, 1), [[0, 1]], 0, 1)
     iota(V("mod16", 0, 128), [[0, 8], [1, 16]], 0, 0)
     iota(V("colc", 0, 128), [[1, 128]], 0, 0)
-    iota(V("dump0", 0, 8), [[0, 2], [16, 4]], DUMP0, 0)
-    iota(V("dumpw", 0, 128), [[16, 4], [0, 32]], DUMP0, 0)
-    select(V("SEG16", 0, 128), V("ones", 0, 128), [[0, 8], [1, 16]], ALU.is_gt, 0, 0)
-    select(V("SEG32", 0, 128), V("ones", 0, 128), [[0, 4], [1, 32]], ALU.is_gt, 0, 0)
-    select(ALL("GE1"), (T["ones"][0:8, 0:128], [("ones", 0, 128)]), [[1, 128]], ALU.is_ge, 0, -16)
+    iota(V("L8", 0, 4), [[-1, 4]], 3, 0)
+    iota(V("L8", 4, 8), [[1, 4]], 124, 0)
+    select(V("G01", 0, 128), V("GM", 0, 128), [[0, 8], [-1, 16]], ALU.is_ge, 1, 0)
+    select(ALL("GE1"), (T["ones"][0:8, 0:128], [("ones", 0, 128)], 128), [[1, 128]], ALU.is_ge, 0, -16)
     select(ALL("GE"), ALL("GE1"), [[-1, 128]], ALU.is_ge, 15, 16)
-
-    def late_constants():
-        cp(ALL("thf"), ALL("thi"))
-        fill(ALL("oneb"), 1.0)
-        mm(V("pM", 128, 133), ALL("GE"), ALL("thf"))
-        line(ALL("CQ"), (T["colc"][0:1, 0:128], [("colc", 0, 128)]), -0.25, 31.75)
-        line(V("C2", 0, 128), V("colc", 0, 128), -0.5, 130560.0 + 63.5)
-        ts(V("DM", 0, 128), V("mod16", 0, 128), V("p16", 0, 1), ALU.is_equal)
-        ts(V("ND", 0, 128), V("mod16", 0, 128), V("p16", 0, 1), ALU.not_equal)
-        fill(V("ND", 128, 144), 1.0)
-        ts(V("dump", 0, 8), V("dump0", 0, 8), V("p16", 0, 1), ALU.add)
-        ts(V("OW1", 128, 256), V("dumpw", 0, 128), V("p16", 0, 1), ALU.add)
-        ts(V("OW0", 128, 256), V("dumpw", 0, 128), V("p16", 0, 1), ALU.add)
-        fill(V("GD", 192, 208), 0.0)
-        ts(V("LM", 0, 5), V("pM", 128, 133), 32.0, ALU.mult, 31.75, ALU.add)
+    ts(V("p16i", 0, 1), V("pidx", 0, 1), 15, ALU.bitwise_and)
+    cp(ALL("thf"), ALL("thi"))
+    cp(V("p16", 0, 1), V("p16i", 0, 1))
+    fill(V("UP", 0, 32), 4.0)
+    fill(V("DN", 0, 32), -4.0)
+    fill(V("HW", 0, 8), 0.0)
+    ts(V("ZK", 0, 144), V("Z1", 0, 144), 256.0, ALU.mult)
+    ts(V("DM", 0, 128), V("mod16", 0, 128), V("p16", 0, 1), ALU.is_equal)
+    ts(V("ND", 0, 128), V("mod16", 0, 128), V("p16", 0, 1), ALU.not_equal)
+    ts(V("q1", 0, 1), V("p16", 0, 1), 1.0, ALU.is_equal)
+    ts(V("dump", 0, 1), V("p16", 0, 1), 16.0, ALU.add)
+    line(V("NID", 0, 128), V("ID", 0, 128), -1.0, 0.0)
+    act(V("GMb", 0, 128), V("GM", 0, 128))
+    mm(V("pM", 128, 133), ALL("GE"), ALL("thf"))
+    line(V("LM", 0, 5), V("pM", 128, 133), 256.0, 0.0)
 
     for s in range(S):
-        par, nxp = s % 2, (s + 1) % 2
         last = s == S - 1
-        zr, nr, hr, zs1 = "ZR%d" % s, "NR%d" % s, "HR%d" % s, "ZS%d" % (s + 1)
-        send("OU%d" % (s + 1), "OU%d" % s, 0, 128, "rO%d" % s)
-        send(zr, "ZS%d" % s, 0, 192, "rZ%d" % s)
-        for half in (0, 1):
-            a, b = 64 * half, 64 * half + 64
-            reduce16("PG", a, b, "WP", PB[half], (V("ID", 0, 128), V("NM", a, b)))
-            if half == 0 and s > 0:
-                mm(V("pM", 136, 137), V("GM", 0, 128), V("rs", 0, 1))
-        cp(V("RU", 0, 64), V(PB[0], 0, 64))
-        for L in (0, 1):
-            for j in (0, 1):
-                gather_abs(L, j, "RU", "ztb")
-        reduce16("AB", 0, 64, "W", "pUA", None)
-        if s > 0:
-            line(V("A32", 0, 1), V("pM", 136, 137), 32.0, A0)
-            line(V("Q32", 0, 128), V("OW%d" % par, 0, 128), 1184.0, V("A32", 0, 1))
-            tt(V("pS", 128, 256), V("pS", 0, 128), V("hN", 0, 128), ALU.mult)
-            cp(V("RU", 64, 128), V(PB[1], 0, 64))
-            tt(V("NS%d" % s, 0, 128), V("pS", 128, 256), V("NR%d" % (s - 1), 0, 128), ALU.add)
-        else:
-            line(V("OQ0", 0, 128), V("OW0", 0, 128), 1.0 / 32, -1.0 / 32)
-            line(V("Q32", 0, 128), V("OW0", 0, 128), 1184.0, A0)
-            cp(V("RU", 64, 128), V(PB[1], 0, 64))
-        for j in (0, 1):
-            gather_abs(2, j, "RU", "ztb")
-            if s > 0:
-                tile("ztc", zr, ((0,), (16,))[j])
-        reduce16("AB", 64, 96, "W", "pUB", None)
-        gather_abs(3, 0, "RU", "ztb")
-        if s > 0:
-            tile("ztc", zr, (32,))
-        h_of(0, s, lambda: gather_abs(3, 1, "RU", "ztb"))
-        reduce16("AB", 96, 128, "W", "pUC", None)
-        tile("ztc", zr, (64,) if s > 0 else (0, 16, 32, 64))
-        tile_end("ztc", act)
-        h_of(1, s)
-        date = V(zr, 64, 192)
-        if s == 0:
-            late_constants()
-
-        def known():
-            cp(V("OW%d" % nxp, 0, 128), V("OU%d" % (s + 1), 0, 128))
-            ts(V("e1", 0, 128), date, float(s), ALU.is_gt, -BIG, ALU.mult)
-            ts(V("e2", 0, 128), date, 99.0, ALU.is_lt)
-
-        if s > 0:
-            known()
-        h_of(2, s)
+        zt, zc, nr, hr, zt1, ow1 = "ZT%d" % s, "ZC%d" % s, "NR%d" % s, "HR%d" % s, "ZT%d" % (s + 1), "OW%d" % (s + 1)
+        date, lim = V(zc, 0, 128), V("LM", s, s + 1)
+        send(zc, zt, 0, 192, "rZ%d" % s)
+        send(ow1, "OW%d" % s, 0, 136, "rO%d" % s)
         send(nr, "NS%d" % s, 0, 128, "rN%d" % s)
-        if s == 0:
-            known()
+        tile(zc, TILEC)
+        for (e, a, b) in PGATHER:
+            copy[e](V("PG", 16 * a, 16 * b), IND(PA, V("OM", a, b)))
+        for q, (a, b) in enumerate(ROADS):
+            reduce16("PG", a, b, "Z1", V(PB[q], 0, b - a), (V("ID", 0, 128), V("NM", a, b)))
+            cp(V("RU", a, b), V(PB[q], 0, b - a))
+        for (a, b) in UGATHER:
+            distance("DF", "AB", a, b, "RU", zt)
+        for q in range(len(HPIECES)):
+            h_of(q, s)
         if last:
-            dma("s", "o_lo", V("LO", 0, 256), (T["PW"][0:128:16, 1:4097], [("PW", 1, 4097)]))
-            dma("s", "o_hi", V("LO", 256, 512), (T["PW"][1:128:16, 1:4097], [("PW", 1, 4097)]))
-        line(V("OQ%d" % nxp, 0, 128), V("OW%d" % nxp, 0, 128), 1.0 / 32, -1.0 / 32)
-        line(V("ST", 0, 128), date, -1.0, float(s + 2))
-        for half in (0, 1):
-            a, b = 64 * half, 64 * half + 64
-            for L in (2 * half, 2 * half + 1):
-                for j in (0, 1):
-                    gather_abs(L, j, hr, "ztc")
-            if last and half == 0:
-                line(V("pR", 256, 512), V("LO", 256, 512), 1.0, -1.0)
-            reduce16("AB", a, b, "W", KB[half], (ALL("oneb"), (T["CQ"][:, a:b], [("CQ", a, b)])))
-        cp(V("HW", 0, 128), V(hr, 0, 128))
-
-        def keys(half, between=None):
-            a, b = 64 * half, 64 * half + 64
-            kd = V(KB[half], 0, 64)
-            tt(V("K2", a, b), V("C2", a, b), kd, ALU.subtract)
-            scan(V("SM", a, b), V("SEG32", a, b), kd, ALU.mult, ALU.max)
-            if between is not None:
-                between()
-            scan(V("SM", 128 + a, 128 + b), V("SEG32", a, b), V("K2", a, b), ALU.mult, ALU.max)
-
-        def redeem(half, n):
-            a, b = 64 * half, 64 * half + 64
-            if n == 0:
-                tt(V("pS", a, b), V(KB[half], 0, 64), V("RT", a, b), ALU.is_le)
-            elif n == 1:
-                tt(V("pS", 128 + a, 128 + b), V("pS", a, b), V("ST", a, b), ALU.mult)
-            else:
-                tt(V("pS", 256 + a, 256 + b), V("pS", 128 + a, 128 + b), V(zr, 64 + a, 64 + b), ALU.add)
-
-        def refuse(L):
-            ts(V("RF", 32 * L, 32 * L + 32), V(KB[L // 2], 32 * (L % 2), 32 * (L % 2) + 32), V("gk", L, L + 1),
-               ALU.is_equal, 99.0, ALU.mult)
-
-        def newdate(half):
-            a, b = 64 * half, 64 * half + 64
-            tt(V(zs1, 64 + a, 64 + b), V("pS", 256 + a, 256 + b), V("RF", a, b), ALU.max)
-
-        def onward(n):
-            if last:
-                return
-            if n == 0:
-                ts(V("pS", 384, 512), V(zs1, 64, 192), float(s + 1), ALU.is_gt)
-            elif n == 1:
-                ts(V("pS", 256, 384), V(zs1, 64, 192), float(s + 1), ALU.is_le)
-            elif n == 2:
-                tt(V("om", 0, 128), V("pS", 384, 512), V("OW%d" % nxp, 0, 128), ALU.mult)
-            elif n == 3:
-                cp(V("OM", 0, 128), V("om", 0, 128))
-            else:
-                tt(V("NM", 0, 128), V("pS", 256, 384), V(nr, 0, 128), ALU.mult)
-
-        def write(L, win, fu, data):
-            cp(IND(win, V("fu", fu + 2 * L, fu + 2 * L + 1)), V(data, 16 * L, 16 * L + 16))
-
-        if last:
+            dma("s", "o_lo", V("LO", 0, 256), ROW("PW", 0), 65536)
+            dma("s", "o_hi", V("LO", 256, 512), ROW("PW", 1), 65536)
+            line(V("pR", 256, 512), V("LO", 256, 512), 1.0, -float(B0))
             tt(V("YPg", 0, 256), V("pR", 256, 512), V("LO", 0, 256), ALU.add)
-            dma("s", "o_pf", (T["PF"][0:128:16, 1:4097], [("PF", 1, 4097)]), V("YPg", 0, 256))
-        tt(V("RT0", 0, 128), V("e1", 0, 128), V("e2", 0, 128), ALU.mult)
-        keys(0)
-        ts(V("RT", 0, 128), V("RT0", 0, 128), V("LM", s, s + 1), ALU.add)
-        tt(V("hN", 0, 128), V("HW", 0, 128), V(nr, 0, 128), ALU.subtract)
-        for n in (0, 1, 2):
-            redeem(0, n)
-        keys(1, lambda: redeem(1, 0))
-        lastk = V("SM", 31, 128, 32)
-        ts(V("nogo", 0, 4), lastk, V("LM", s, s + 1), ALU.is_le, 128.0, ALU.mult)
-        redeem(1, 1)
-        ts(V("KI", 0, 8), V("SM", 31, 256, 32), 4.0, ALU.mult)
-        ts(V("CI", 0, 8), V("KI", 0, 8), 127, ALU.bitwise_and)
-        tt(V("gk", 0, 4), lastk, V("nogo", 0, 4), ALU.subtract)
-        ts(V("OFF", 0, 8), V("CI", 0, 8), -1.0, ALU.mult, 127.0, ALU.add)
-        tt(V("CI", 8, 12), V("CI", 0, 4), V("nogo", 0, 4), ALU.subtract)
-        redeem(1, 2)
-        tt(V("GD", 0, 128), IND(V("HW", 0, 128), V("OFF", 0, 8)), V("DM", 0, 128), ALU.mult)
-        ts(V("OFF", 8, 12), V("CI", 8, 12), -1.0, ALU.mult, 127.0, ALU.add)
-        refuse(0)
-        tt(V("GD", 128, 192), IND(V("OW%d" % nxp, 0, 256), V("OFF", 8, 12)), V("DM", 0, 64), ALU.mult)
-        mm(V("pM", 0, 128), V("LT", 0, 128), V("GD", 64, 192))
-        mm(V("pR", 64, 128), V("GM", 0, 128), V("GD", 0, 64))
-        scan(V("OWN", 0, 144), V("ND", 0, 144), V("GD", 64, 208), ALU.mult, ALU.add)
-        refuse(1)
-        cp(V("HB", 0, 4), V("OWN", 15, 64, 16))
-        refuse(2)
-        refuse(3)
-        tt(V("gz", 0, 64), IND(XR, V("HB", 0, 4)), V(zr, 0, 64), ALU.add)
-        tt(V("E", 0, 128), V("OWN", 16, 144), V("pM", 0, 128), ALU.is_equal)
-        ts(V("zi", 0, 64), V("gz", 0, 64), 0.5, ALU.mult, -0.25, ALU.add)
+            dma("s", "o_pf", ROW("PF", 0), V("YPg", 0, 256), 131072)
+        line(V("e1", 0, 128), date, 1.0, -(s + 99) / 2.0, ACT.Abs)
+        line(V("e2", 0, 128), V("e1", 0, 128), -BIG, BIG * (99 - s) / 2.0, ACT.Relu)
+        line(V("RT", 0, 128), V("e2", 0, 128), -1.0, lim)
+        line(V("pP0", 0, 128), date, -1.0, float(s + 2))
+        line(V("zh", 0, 64), V(zc, 128, 192), 1.0, -0.5)
+        for (a, b) in DGATHER:
+            distance("DG", "AC", a, b, hr, zc)
+        for (a, b) in DSUMS:
+            reduce16("AC", a, b, "ZK", V(KD, a, b), None)
         if not last:
-            ts(V("hx", 0, 64), V("pR", 64, 128), V("q1", 0, 1), ALU.mult)
-        scan(V("F", 0, 128), V("SEG16", 0, 128), V("E", 0, 128), ALU.mult, ALU.max)
-        cp(V(zs1, 0, 64), V("zi", 0, 64))
+            ways_open(s + 1, V(nr, 0, 128))
+        cp(V("HW", 8, 136), V(hr, 0, 128))
+        mms(V("pU0", 0, 128), [(V("ID", 0, 128), V("HW", 8, 136)), (V("NID", 0, 128), V(nr, 0, 128))])
+        for L in range(4):
+            scan(V("SM", 32 * L, 32 * L + 32), V("UP", 0, 32), V(KD, L, 128, 4), lim, ALU.add, ALU.max)
+        for L in range(4):
+            scan(V("SM", 128 + 32 * L, 160 + 32 * L), V("DN", 0, 32), V(KD, L, 128, 4), BIG, ALU.add, ALU.min)
+        tt(V("red", 0, 128), V(KD, 0, 128), V("RT", 0, 128), ALU.is_le)
+        tt(V("KI", 0, 8), V("SM", 31, 256, 32), V("L8", 0, 8), ALU.add)
+        ts(V("CI", 0, 8), V("KI", 0, 8), 255, ALU.bitwise_and)
+        ts(V("OFF", 4, 8), V("CI", 0, 4), -1.0, ALU.mult, 135.0, ALU.add)
+        ts(V("NC", 0, 4), V("CI", 0, 4), -127.0, ALU.add)
+        ts(V("OFF", 0, 4), V("CI", 4, 8), 8.0, ALU.add)
+        tt(V("pS", 0, 128), V("pP0", 0, 128), V("red", 0, 128), ALU.mult)
+        tt(V("pS", 256, 384), V("pS", 0, 128), date, ALU.add)
+        for L in range(4):
+            line(V("rf", L, 128, 4), V("colc", L, 128, 4), 1.0, V("NC", L, L + 1), ACT.Abs)
+        line(V("RF", 0, 128), V("rf", 0, 128), -99.0, 99.0, ACT.Relu)
+        tt(V("YT", 0, 128) if last else V(zt1, 0, 128), V("pS", 256, 384), V("RF", 0, 128), ALU.max)
         if not last:
-            tile("ztb", zs1)
-            tt(V("PD", 0, 64), V("pR", 64, 128), V("hx", 0, 64), ALU.subtract)
-        else:
-            dma("a", "o_z", ALL("yz"), V(zs1, 0, 64))
-            ts(V("ht", 0, 64), V("pR", 64, 128), -1.0, ALU.add)
-        tt(V("f1", 0, 8), V("F", 15, 128, 16), V("dump", 0, 8), ALU.mult)
-        newdate(0)
-        newdate(1)
-        tt(V("f2", 0, 8), V("f1", 0, 8), V("OWN", 15, 128, 16), ALU.max)
-        onward(0)
-        cp(V("fu", 0, 16, 2), V("f2", 0, 8))
-        onward(1)
+            ways(s + 1)
+        tt(V("GD", 0, 64), IND(V(ow1, 0, 136), V("OFF", 4, 8)), V("DM", 0, 64), ALU.mult)
+        tt(V("GD", 64, 192), IND(V("HW", 0, 136), V("OFF", 0, 8)), V("DM", 0, 128), ALU.mult)
+        mm(V("pM", 0, 64), V("GM", 0, 128), V("GD", 0, 64))
+        mm(V("pM", 64, 128), V("GM", 0, 128), V("GD", 64, 128))
+        mm(V("pR", 0, 64), V("G01", 0, 128), V("GD", 128, 192))
+        scan(BACK("OWN", 0, 128), BACK("ND", 0, 128), BACK("GD", 0, 128), 0.0, ALU.mult, ALU.add)
+        tt(V("NE", 0, 128), V("OWN", 0, 128), V("pM", 0, 128), ALU.not_equal)
+        scan(BACK("FS", 0, 128), BACK("NE", 0, 128), BACK("GD", 0, 128), 0.0, ALU.mult, ALU.add)
+        ts(V("fu", 0, 16, 2), V("FS", 0, 128, 16), V("dump", 0, 1), ALU.max)
+        cp(V("HB", 0, 4), V("OWN", 64, 128, 16))
+        tt(V("gz", 0, 64), IND(XA, V("HB", 0, 4)), V("zh", 0, 64), ALU.add)
+        ts(V("ev", 0, 64), V("gz", 0, 64), EVEN, ALU.add, -EVEN, ALU.add)
+        line(V(zt1, 128, 192), V("ev", 0, 64), 0.5, 0.0)
         if not last:
-            for L in (3, 2, 1, 0):
-                write(L, PA, 8, "PD")
-                if L:
-                    onward(5 - L)
-            act(*pgather(0, 32))
-            cp(*pgather(32, 64))
-            act(*pgather(64, 112))
-            write(3, XA, 0, "zi")
-            tile_end("ztb", cp)
-            write(2, XA, 0, "zi")
-            op("v", lambda: g.vector.tensor_reduce(out=T["rs"][:, 0:1], in_=T["pS"][:, 0:128], axis=AxisListType.X, op=ALU.add),
-               [V("pS", 0, 128)], [V("rs", 0, 1)])
-            write(1, XA, 0, "zi")
-            cp(*pgather(112, 128))
-            write(0, XA, 0, "zi")
-        else:
-            tt(V("pS", 128, 256), V("pS", 0, 128), V("hN", 0, 128), ALU.mult)
-            for L in (3, 2, 1, 0):
-                write(L, XA, 0, "zi")
-                cp(V("YT", L, 128, 4), V(zs1, 64 + 32 * L, 96 + 32 * L))
-            dma("s", "o_x", ALL("yx"), V("XW", 1, 4097))
-            dma("a", "o_t", ALL("yt"), V("YT", 0, 128))
-            tt(V("NS%d" % (s + 1), 0, 128), V("pS", 128, 256), V(nr, 0, 128), ALU.add)
-            for L in (3, 2, 1, 0):
-                write(L, V("PF", 0, PADW), 8, "ht")
-                ts(V("YN", L, 128, 4), V("NS%d" % (s + 1), 32 * L, 32 * L + 32), -1.0, ALU.add)
-            dma("a", "o_p", ALL("yp"), (T["PF"][0:128:16, 1:4097], [("PF", 1, 4097)]))
-            dma("s", "o_n", ALL("yn"), V("YN", 0, 128))
-    for q in ("v", "a", "t", "p"):
-        g.wait_ge(T.sem[q], count[q])
-    g.wait_ge(T.sem["loc"], sent[0])
-    for n in DMAS:
-        g.wait_ge(T.sem[n], 16)
-    for s in range(S):
-        for k in RECV:
-            g.wait_ge(T.sem["%s%d" % (k, s)], len(topo.engines(prv, core)))
+            line(V("hx", 0, 64), V("pR", 0, 64), V("q1", 0, 1), 0.0)
+            tt(V("PD", 0, 64), V("pR", 0, 64), V("hx", 0, 64), ALU.subtract)
+            write(PA, 0, "PD")
+            tile(zt1, TILEB)
+            mm(V("pU0", 128, 256), V("GMb", 0, 128), V("red", 0, 128))
+            line(V("junk", 0, 128), V("pU0", 128, 256), 32.0, A0 / 128, ACT.Identity, V("A32", 0, 1))
+            line(V("Q", 0, 128), V(ow1, 8, 136), 3232.0, V("A32", 0, 1))
+        write(XA, 8, zt1, 128)
+        tt(V("pS", 128, 256), V("pU0", 0, 128), V("red", 0, 128), ALU.mult)
+        tt(V("NS%d" % (s + 1), 0, 128), V("pS", 128, 256), V(nr, 0, 128), ALU.add)
+        if last:
+            dma("s", "o_x", ALL("yx"), V("XW", B0, WW), 1048576)
+            line(V("ht", 0, 64), V("pR", 0, 64), 1.0, -float(B0))
+            write(V("PF", 0, WW), 0, "ht")
+            ts(V("YN", 0, 128), V("NS%d" % (s + 1), 0, 128), -float(B0), ALU.add)
+            dma("s", "o_t", ALL("yt"), V("YT", 0, 128), 65536)
+            dma("a", "o_z", ALL("yz"), V(zt1, 128, 192), 16384)
+            dma("a", "o_p", ALL("yp"), ROW("PF", 0), 131072)
+            dma("s", "o_n", ALL("yn"), V("YN", 0, 128), 65536)
+    issue()

@@ -1,7 +1,9 @@
+import math
 from concourse.mybir import AluOpType as ALU, ActivationFunctionType as ACT
 
 S, B0, WW, TW = 5, 32, 4128, 512
 BIG, CUT, EVEN = 2097152.0, 8192.0, 25165824.0
+PAIRED = True
 
 
 def _sb(n, dtype="float32", p=128):
@@ -22,11 +24,12 @@ SCRATCH = {
     "pidx": _sb(1, "int32"), "p16i": _sb(1, "int32"), "p16": _sb(1), "q1": _sb(1), "dump": _sb(1), "LM": _sb(5),
     "HW": _sb(136), "Q": _sb(128), "A32": _sb(1), "junk": _sb(128),
     "OM": _sb(128, "uint16"), "NM": _sb(128), "RU": _sb(128, "uint16"), "r12": _sb(256, "bfloat16"),
-    "hm": _sb(128), "hv": _sb(128, "int32"), "hs": _sb(128, "int32"),
-    "e1": _sb(128), "e2": _sb(128), "RT": _sb(128), "red": _sb(128, "bfloat16"), "SM": _sb(256), "zh": _sb(64),
+    "hm": _sb(128), "hv": _sb(256, "int32"), "hs": _sb(128, "int32"), "OQ": _sb(256), "beta": _sb(128, "bfloat16", 1),
+    "e1": _sb(128), "e2": _sb(128), "RT": _sb(128), "red": _sb(128, "bfloat16"), "SM": _sb(256, "int32" if PAIRED else "float32"),
+    "zh": _sb(64),
     "KI": _sb(8, "int32"), "CI": _sb(8, "int32"), "NC": _sb(4), "OFF": _sb(8, "uint16"),
     "GD": _sb(192), "OWN": _sb(128), "NE": _sb(128), "FS": _sb(128), "fu": _sb(16, "uint16"),
-    "HB": _sb(4, "uint16"), "gz": _sb(64), "ev": _sb(64),
+    "HB": _sb(4, "uint16"), "gz": _sb(64), "zi": _sb(64, "int32"),
     "hx": _sb(64, "bfloat16"), "ht": _sb(64), "PD": _sb(64, "bfloat16"), "rf": _sb(128), "RF": _sb(128),
     "YN": _sb(128), "YT": _sb(128), "YPg": _sb(256), "LO": _sb(512, "bfloat16"),
     "ZC": _sb((128 + TW) * S, "bfloat16"),
@@ -41,13 +44,15 @@ for _n in ("pU0", "pU1", "pU2", "pP0", "pP1", "pR", "pM", "pS"):
     SCRATCH[_n] = ("psum", [128, 512], "float32")
 PIECE = {"%s%d" % (k, s): (k, SCRATCH[k][1][1] // n * s) for k, n in
          (("ZC", S), ("NR", S), ("HS", S), ("HR", S), ("OW", S + 1), ("ZT", S + 1), ("NS", S + 1)) for s in range(n)}
-PGATHER = (("a", 0, 16), ("v", 16, 32), ("a", 32, 64), ("a", 64, 96), ("a", 96, 128))
+PGATHER = (("a", 0, 16), ("v", 16, 32), ("a", 32, 48), ("v", 48, 64), ("a", 64, 96), ("a", 96, 128))
 ROADS = ((0, 32), (32, 64), (64, 96), (96, 128))
-UGATHER = ((0, 32), (32, 64), (64, 80), (80, 96), (96, 112), (112, 128))
+UGATHER = ((0, 16), (16, 32), (32, 48), (48, 64), (64, 80), (80, 96), (96, 112), (112, 128))
 HPIECES = ((0, 32), (32, 64), (64, 96), (96, 128))
-DGATHER = ((0, 32), (32, 64), (64, 96), (96, 112), (112, 128))
+DGATHER = ((0, 32), (32, 64), (64, 96), (96, 120), (120, 128))
 DSUMS = ((0, 64), (64, 128))
-TILEB, TILEC, ROUNDS = "aav", "ppp", 2
+TURNS = ()
+TILEB = "aav"
+TILEC = "ppp"
 RECV = ("rO", "rZ", "rN") + tuple("rH%d_" % i for i in range(len(HPIECES)))
 DMAS = ["d_px", "d_ol", "d_z", "d_tl", "d_nl", "d_th", "d_x", "d_x2", "d_lo", "d_hi",
         "o_x", "o_lo", "o_hi", "o_pf", "o_p", "o_z", "o_n", "o_t"]
@@ -57,8 +62,85 @@ PB = ("pP0", "pP1", "pP0", "pP1")
 KD = "pU1"
 A0 = 65536.0 - 8388608.0 - 3232.0 * B0
 INORDER = True
-CALL, GATHER, SCATTER, PE, WAKE, LOAD, HOP = 60, 1.56, 3.8, 0.55, 150, 1900, 1900
+CALL, GATHER, SCATTER, PE, WAKE, LOAD, HOP = 60, 1.56, 3.8, 0.55, 210, 1900, 1750
+AHEAD = 200
+LATE = 2.0
+TRIES = 16000
 PLAN = {}
+
+
+def tighten(nodes, before, order, marks):
+    n, last, seed = len(nodes), len(marks) - 1, [12345]
+    busy, on = [nd["busy"] for nd in nodes], [nd["q"] for nd in nodes]
+    step = [max(i for i in range(last + 1) if marks[i] <= k) for k in range(n)]
+    pre, post = [list(b.items()) for b in before], [[] for _ in nodes]
+    for k in range(n):
+        for j in before[k]:
+            post[j].append(k)
+
+    def draw(m):
+        seed[0] = (seed[0] * 1103515245 + 12345) % 2147483648
+        return (seed[0] >> 8) % m
+
+    def path(order):
+        prev, nxt, miss = [-1] * n, [-1] * n, [len(p) for p in pre]
+        for q in order.values():
+            for a, b in zip(q, q[1:]):
+                prev[b], nxt[a] = a, b
+                miss[b] += 1
+        end, why, todo, done = [0.0] * n, [-1] * n, [k for k in range(n) if not miss[k]], 0
+        while todo:
+            k = todo.pop()
+            done += 1
+            t, w = (end[prev[k]], prev[k]) if prev[k] >= 0 else (0.0, -1)
+            for j, gap in pre[k]:
+                if end[j] + gap >= t:
+                    t, w = end[j] + gap, j
+            end[k], why[k] = t + busy[k], w
+            for j in post[k] + ([nxt[k]] if nxt[k] >= 0 else []):
+                miss[j] -= 1
+                if not miss[j]:
+                    todo.append(j)
+        if done < n:
+            return None
+        k = max(range(n), key=lambda j: end[j] + nodes[j]["lag"])
+        span, arcs = end[k] + nodes[k]["lag"], []
+        while why[k] >= 0:
+            if why[k] not in before[k]:
+                arcs.append((why[k], k))
+            k = why[k]
+        return span + 0.02 * sum(end) / n, arcs
+
+    now = path(order)
+    best = (now[0], order)
+    for it in range(TRIES):
+        forward = draw(2)
+        if draw(4) and now[1]:
+            a, b = now[1][draw(len(now[1]))]
+            q = order[on[a]]
+            i = q.index(a)
+            a, b = (q[max(0, i - (0, 0, 1, 2, 3)[draw(5)])], b) if forward else (a, q[min(len(q) - 1, i + 1 + draw(4))])
+        else:
+            q = order["vvvaatp"[draw(7)]]
+            i = draw(len(q) - 1)
+            a, b = q[i], q[min(len(q) - 1, i + (1, 1, 2, 3)[draw(4)])]
+        q = list(q)
+        for d in range(-last, last + 1):
+            if d == 0 or all(0 < s < last for s in (step[a], step[b], step[a] + d, step[b] + d)):
+                i, j = q.index(a + marks[step[a] + d] - marks[step[a]]), q.index(b + marks[step[b] + d] - marks[step[b]])
+                if i < j and forward:
+                    q.insert(i, q.pop(j))
+                elif i < j:
+                    q.insert(j, q.pop(i))
+        other = dict(order)
+        other[on[a]] = q
+        new = path(other)
+        if new is not None and new[0] - now[0] <= -math.log((draw(4096) + 1) / 4097.0) * 150.0 * (1.0 - it / TRIES) ** 2:
+            order, now = other, new
+            if now[0] < best[0]:
+                best = (now[0], order)
+    PLAN["spans"] = [best[0]]
+    return best[1]
 
 
 def rank_program(g, core, T, topo):
@@ -67,26 +149,27 @@ def rank_program(g, core, T, topo):
         return
     nxt = T.cores[(rank + 1) % len(T.cores)]
     prv = T.cores[(rank - 1) % len(T.cores)]
-    queues = {"v": g.vector, "a": g.scalar, "t": g.tensor, "p": g, "s": g.sync}
+    queues = {"v": g.vector, "a": g.scalar, "t": g.tensor, "p": g, "s": g.sync, "l": None}
     psum = set(n for n in SCRATCH if SCRATCH[n][0] == "psum")
-    nodes, acc = [], {}
+    nodes, acc, marks = [], {}, [0]
 
     def node(q, calls, rd, wr, busy, lag=0.0, signal=None, beside=None):
         me, before = len(nodes), {}
         for views, write in ((rd, False), (wr, True)):
-            for (n, lo, hi) in [r for v in views for r in v[1]]:
-                for (k, alo, ahi, aw) in acc.get(n, ()):
+            for (n, lo, hi, st) in [r for v in views for r in v[1]]:
+                for (k, alo, ahi, ast, aw) in acc.get(n, ()):
                     same = nodes[k]["q"] == q and nodes[k]["signal"] is None and signal is None
-                    if k == beside or (not (n in psum and (not same or q == "t")) and (ahi <= lo or alo >= hi or not (aw or write))):
+                    apart = ahi <= lo or alo >= hi or (st == ast and (lo - alo) % st)
+                    if k == beside or (not (n in psum and (not same or q == "t")) and (apart or not (aw or write))):
                         continue
                     before[k] = before.get(k, False) or not (same and write and (q == "t" or n[:4] == "turn" or (INORDER and not aw)))
         nodes.append({"q": q, "calls": calls, "before": before, "busy": busy, "lag": lag, "signal": signal})
         for views, write in ((rd, False), (wr, True)):
-            for (n, lo, hi) in [r for v in views for r in v[1]]:
+            for (n, lo, hi, st) in [r for v in views for r in v[1]]:
                 old = acc.get(n, [])
-                if write and n not in psum and beside is None:
+                if write and st == 1 and n not in psum and beside is None:
                     old = [a for a in old if not (lo <= a[1] and a[2] <= hi)]
-                acc[n] = old + [(me, lo, hi, write)]
+                acc[n] = old + [(me, lo, hi, st, write)]
         return me
 
     def width(name):
@@ -108,12 +191,14 @@ def rank_program(g, core, T, topo):
     def send(dst_name, src_name, lo, hi, sem):
         src, dst = V(src_name, lo, hi), V(dst_name, lo, hi)
         rid, pid, _ = topo.addr(nxt)
-        node("p", [lambda: g.remote_dma(out_ap=dst[0], in_ap=src[0], remote_sem=T.sem[sem], local_sem=T.sem["loc"],
-                                        pid=pid, routing_id=rid, dma_engine_mask=topo.mask(core, nxt))],
-             [src], [dst], 180 + 128 * src[2] * width(src[1][0][0]) / 55.0, HOP, (sem, len(topo.engines(prv, core))))
+        call = node("p", [lambda: g.remote_dma(out_ap=dst[0], in_ap=src[0], remote_sem=T.sem[sem], local_sem=T.sem["loc"],
+                                               pid=pid, routing_id=rid, dma_engine_mask=topo.mask(core, nxt))],
+                    [src], [], 180, 0.0, ("loc", 0))
+        landing = node("l", [], [], [dst], 128 * src[2] * width(src[1][0][0]) / 55.0 + 150, HOP, (sem, len(topo.engines(prv, core))))
+        nodes[landing]["before"][call] = False
 
     def issue():
-        n = len(nodes)
+        n, on = len(nodes), [nd["q"] for nd in nodes]
         before = [{j: nodes[j]["lag"] + WAKE if hard else 0.0 for j, hard in nd["before"].items()} for nd in nodes]
         after = [{} for _ in nodes]
         for k in range(n):
@@ -123,34 +208,26 @@ def rank_program(g, core, T, topo):
         def place(pre, post, head, urgency):
             missing = [len(p) for p in pre]
             ready = {k: head[k] for k in range(n) if not missing[k]}
-            order, end = {q: [] for q in queues}, [0.0] * n
+            free, order, end = {q: 0.0 for q in queues}, {q: [] for q in queues}, [0.0] * n
             while ready:
-                k = max(ready, key=lambda j: (urgency[j], -j))
-                at, busy, taken = ready.pop(k), nodes[k]["busy"], order[nodes[k]["q"]]
-                i = len(taken)
-                while i and end[taken[i - 1]] > at:
-                    i -= 1
-                while i < len(taken) and end[taken[i]] - nodes[taken[i]]["busy"] < at + busy:
-                    at = max(at, end[taken[i]])
-                    i += 1
-                taken.insert(i, k)
-                end[k] = at + busy
+                first = min(ready, key=lambda j: (max(ready[j], free[on[j]]), j))
+                q = on[first]
+                now = max(ready[first], free[q])
+                k = max((j for j in ready if on[j] == q and ready[j] <= now + AHEAD),
+                        key=lambda j: (urgency[j] - LATE * max(0.0, ready[j] - now), -j))
+                free[q] = end[k] = max(ready.pop(k), free[q]) + nodes[k]["busy"]
+                order[q].append(k)
                 for j in post[k]:
                     missing[j] -= 1
                     if not missing[j]:
                         ready[j] = max([head[j]] + [end[i] + gap for i, gap in pre[j].items()])
             return max(end[k] + nodes[k]["lag"] for k in range(n)), order, end
 
+        back, end = [0.0] * n, place(before, after, [0.0] * n, [0.0] * n)[2]
+        for k in sorted(range(n), key=lambda j: -end[j]):
+            back[k] = nodes[k]["busy"] + max([nodes[k]["lag"]] + [back[j] + gap for j, gap in after[k].items()])
         if "order" not in PLAN:
-            back, best = [0.0] * n, None
-            for k in range(n - 1, -1, -1):
-                back[k] = nodes[k]["busy"] + max([nodes[k]["lag"]] + [back[j] + gap for j, gap in after[k].items()])
-            for _ in range(ROUNDS):
-                span, order, end = place(before, after, [0.0] * n, back)
-                if best is None or span < best:
-                    best, PLAN["order"] = span, order
-                PLAN.setdefault("spans", []).append(span)
-                back = place(after, before, [nd["lag"] for nd in nodes], end)[2]
+            PLAN["order"] = tighten(nodes, before, place(before, after, [0.0] * n, back)[1], marks)
         order = PLAN["order"]
         count = {}
         for q in queues:
@@ -173,6 +250,8 @@ def rank_program(g, core, T, topo):
                         queues[q].wait_ge(T.sem[sem], needs[sem])
                         seen[sem] = needs[sem]
                 made = [call() for call in nodes[k]["calls"]]
+                if q == "l":
+                    continue
                 if nodes[k]["signal"] is None:
                     made[-1].then_inc(T.sem[q], 1)
                 elif q != "p":
@@ -181,24 +260,24 @@ def rank_program(g, core, T, topo):
             g.wait_ge(T.sem[q], count[q])
         g.wait_ge(T.sem["loc"], len(topo.engines(core, nxt)) * len([nd for nd in nodes if nd["q"] == "p" and nd["signal"]]))
         for nd in nodes:
-            if nd["signal"]:
+            if nd["signal"] and nd["q"] != "p":
                 g.wait_ge(T.sem[nd["signal"][0]], nd["signal"][1])
 
     def V(name, lo, hi, st=1):
         if name in PIECE:
             name, base = PIECE[name]
             lo, hi = lo + base, hi + base
-        return (T[name][:, lo:hi] if st == 1 else T[name][:, lo:hi:st], [(name, lo, hi)], len(range(lo, hi, st)))
+        return (T[name][:, lo:hi] if st == 1 else T[name][:, lo:hi:st], [(name, lo, hi, st)], len(range(lo, hi, st)))
 
     def BACK(name, lo, hi):
-        return (T[name][:, hi - 1::-1] if lo == 0 else T[name][:, hi - 1:lo - 1:-1], [(name, lo, hi)], hi - lo)
+        return (T[name][:, hi - 1::-1] if lo == 0 else T[name][:, hi - 1:lo - 1:-1], [(name, lo, hi, 1)], hi - lo)
 
     def ALL(name):
         n = SCRATCH[name][1][1] if name in SCRATCH else 1
-        return (T[name][:], [(name, 0, n)], n)
+        return (T[name][:], [(name, 0, n, 1)], n)
 
     def ROW(name, first):
-        return (T[name][first:128:16, B0:WW], [(name, B0, WW)], WW - B0)
+        return (T[name][first:128:16, B0:WW], [(name, B0, WW, 1)], WW - B0)
 
     def IND(win, off):
         return (win[0].indirect(off[0]), win[1] + off[1], 16 * off[2], off)
@@ -210,7 +289,7 @@ def rank_program(g, core, T, topo):
         return v if isinstance(v, (int, float)) or v is None else v[0]
 
     def op(q, call, rd, wr, busy):
-        turn = [(None, [("turn" + q, 0, 1)])] if rd and len(rd[0]) > 3 and rd[0][2] >= 256 else []
+        turn = [(None, [("turn" + q, 0, 1, 1)])] if rd and len(rd[0]) > 3 and rd[0][2] >= 256 else []
         node(q, [call], rd + [o[3] for o in wr if len(o) > 3], [(o[0], o[1][:1]) for o in wr] + turn, busy)
 
     def tt(o, a, b, f):
@@ -270,17 +349,49 @@ def rank_program(g, core, T, topo):
             mm(out, first[0], first[1], True, False)
         mms(out, [(V(w, 15 - i, 143 - i), V(src, 16 * c0 + i, 16 * c1, 16)) for i in range(16)], first is None, True)
 
-    def distance(df, ab, a, b, off, tname):
+    named = {}
+
+    def name(word):
+        named[word] = len(nodes) - 1
+
+    def in_turn(words):
+        turn = [named[w] for w in words.split() if w in named]
+        for a, b in zip(turn, turn[1:]):
+            nodes[b]["before"].setdefault(a, False)
+
+    def distance(df, ab, a, b, off, tname, words):
         tt(V(df, 16 * a, 16 * b), IND(XA, V(off, a, b)), V(tname, 128, 128 + 16 * (b - a)), ALU.subtract)
+        name(words[0])
         act(V(ab, 16 * a, 16 * b), V(df, 16 * a, 16 * b), ACT.Abs)
+        name(words[1])
+
+    def h_terms(s, bias):
+        if not PAIRED:
+            line(V("Q", 0, 128), V("OW%d" % s, 8, 136), 3232.0, bias)
+            return
+        act(V("OQ", 1, 256, 2), V("OW%d" % s, 8, 136))
+        for q, (a, b) in enumerate(HPIECES):
+            line(V(UB[q], 2 * a + 1, 2 * b, 2), V("OW%d" % s, 8 + a, 8 + b), 3232.0, bias)
 
     def h_of(q, s):
         a, b = HPIECES[q]
-        reduce16("AB", a, b, "Z1", V(UB[q], 0, b - a), (ALL("oneb"), V("mid", 0, b - a)))
-        tt(V("hm", a, b), V(UB[q], 0, b - a), V("OW%d" % s, 8 + a, 8 + b), ALU.mult)
-        tt(V("hv", a, b), V("hm", a, b), V("Q", a, b), ALU.add)
-        ts(V("hs", a, b), V("hv", a, b), 5, ALU.arith_shift_right, 4095, ALU.bitwise_and)
+        u = V(UB[q], 2 * a, 2 * b, 2) if PAIRED else V(UB[q], 0, b - a)
+        reduce16("AB", a, b, "Z1", u, (ALL("oneb"), V("mid", 0, b - a)))
+        name("u%d" % q)
+        if PAIRED:
+            scan(V("hv", 2 * a, 2 * b), V("OQ", 2 * a, 2 * b), V(UB[q], 2 * a, 2 * b), 0.0, ALU.mult, ALU.add)
+            name("m%d" % q)
+            whole = V("hv", 2 * a + 1, 2 * b, 2)
+        else:
+            tt(V("hm", a, b), u, V("OW%d" % s, 8 + a, 8 + b), ALU.mult)
+            name("m%d" % q)
+            tt(V("hv", a, b), V("hm", a, b), V("Q", a, b), ALU.add)
+            name("v%d" % q)
+            whole = V("hv", a, b)
+        ts(V("hs", a, b), whole, 5, ALU.arith_shift_right, 4095, ALU.bitwise_and)
+        name("s%d" % q)
         ts(V("HS%d" % s, a, b), V("hs", a, b), float(B0), ALU.add)
+        name("H%d" % q)
         send("HR%d" % s, "HS%d" % s, a, b, "rH%d_%d" % (q, s))
 
     def ways_open(s, names):
@@ -299,6 +410,7 @@ def rank_program(g, core, T, topo):
     def write(win, fu, data, base=0):
         for L in (3, 2, 1, 0):
             cp(IND(win, V("fu", fu + 2 * L, fu + 2 * L + 1)), V(data, base + 16 * L, base + 16 * L + 16))
+            name("%s%d" % (win[1][0][0][0].lower(), L))
 
     dma("s", "d_px", V("pxi", 0, 256), ALL("px"), 131072)
     dma("a", "d_ol", V("oli", 0, 128), ALL("ol"), 65536)
@@ -329,16 +441,17 @@ def rank_program(g, core, T, topo):
     ways(0)
     cp(V("Z1", 15, 143, 16), V("GM", 0, 128, 16))
     tile("ZT0", "vvv")
-    line(V("Q", 0, 128), V("OW0", 8, 136), 3232.0, A0)
+    fill(V("OQ", 0, 256, 2), 0.0)
+    h_terms(0, A0)
+    iota(ALL("beta"), [[0, 32], [-1, 4]], 3, 0)
     fill(ALL("oneb"), 1.0)
     fill(ALL("mid"), -2048.0)
     iota(V("pidx", 0, 1), [[0, 1]], 0, 1)
     iota(V("mod16", 0, 128), [[0, 8], [1, 16]], 0, 0)
     iota(V("colc", 0, 128), [[1, 128]], 0, 0)
-    iota(V("L8", 0, 4), [[-1, 4]], 3, 0)
-    iota(V("L8", 4, 8), [[1, 4]], 124, 0)
+    iota(V("L8", 0, 4), [[2, 4]], 121, 0)
     select(V("G01", 0, 128), V("GM", 0, 128), [[0, 8], [-1, 16]], ALU.is_ge, 1, 0)
-    select(ALL("GE1"), (T["ones"][0:8, 0:128], [("ones", 0, 128)], 128), [[1, 128]], ALU.is_ge, 0, -16)
+    select(ALL("GE1"), (T["ones"][0:8, 0:128], [("ones", 0, 128, 1)], 128), [[1, 128]], ALU.is_ge, 0, -16)
     select(ALL("GE"), ALL("GE1"), [[-1, 128]], ALU.is_ge, 15, 16)
     ts(V("p16i", 0, 1), V("pidx", 0, 1), 15, ALU.bitwise_and)
     cp(ALL("thf"), ALL("thi"))
@@ -354,23 +467,27 @@ def rank_program(g, core, T, topo):
     line(V("NID", 0, 128), V("ID", 0, 128), -1.0, 0.0)
     act(V("GMb", 0, 128), V("GM", 0, 128))
     mm(V("pM", 128, 133), ALL("GE"), ALL("thf"))
-    line(V("LM", 0, 5), V("pM", 128, 133), 256.0, 0.0)
+    line(V("LM", 0, 5), V("pM", 128, 133), 256.0, 3.0)
 
     for s in range(S):
         last = s == S - 1
+        marks.append(len(nodes))
         zt, zc, nr, hr, zt1, ow1 = "ZT%d" % s, "ZC%d" % s, "NR%d" % s, "HR%d" % s, "ZT%d" % (s + 1), "OW%d" % (s + 1)
         date, lim = V(zc, 0, 128), V("LM", s, s + 1)
         send(zc, zt, 0, 192, "rZ%d" % s)
         send(ow1, "OW%d" % s, 0, 136, "rO%d" % s)
         send(nr, "NS%d" % s, 0, 128, "rN%d" % s)
         tile(zc, TILEC)
-        for (e, a, b) in PGATHER:
+        for i, (e, a, b) in enumerate(PGATHER):
             copy[e](V("PG", 16 * a, 16 * b), IND(PA, V("OM", a, b)))
+            name("P%d" % i)
         for q, (a, b) in enumerate(ROADS):
             reduce16("PG", a, b, "Z1", V(PB[q], 0, b - a), (V("ID", 0, 128), V("NM", a, b)))
+            name("r%d" % q)
             cp(V("RU", a, b), V(PB[q], 0, b - a))
-        for (a, b) in UGATHER:
-            distance("DF", "AB", a, b, "RU", zt)
+            name("R%d" % q)
+        for i, (a, b) in enumerate(UGATHER):
+            distance("DF", "AB", a, b, "RU", zt, ("U%d" % i, "A%d" % i))
         for q in range(len(HPIECES)):
             h_of(q, s)
         if last:
@@ -383,11 +500,12 @@ def rank_program(g, core, T, topo):
         line(V("e2", 0, 128), V("e1", 0, 128), -BIG, BIG * (99 - s) / 2.0, ACT.Relu)
         line(V("RT", 0, 128), V("e2", 0, 128), -1.0, lim)
         line(V("pP0", 0, 128), date, -1.0, float(s + 2))
-        line(V("zh", 0, 64), V(zc, 128, 192), 1.0, -0.5)
-        for (a, b) in DGATHER:
-            distance("DG", "AC", a, b, hr, zc)
+        for i, (a, b) in enumerate(DGATHER):
+            distance("DG", "AC", a, b, hr, zc, ("D%d" % i, "B%d" % i))
         for (a, b) in DSUMS:
-            reduce16("AC", a, b, "ZK", V(KD, a, b), None)
+            reduce16("AC", a, b, "ZK", V(KD, a, b), (ALL("oneb"), V("beta", a, b)))
+        for words in TURNS:
+            in_turn(words)
         if not last:
             ways_open(s + 1, V(nr, 0, 128))
         cp(V("HW", 8, 136), V(hr, 0, 128))
@@ -397,11 +515,16 @@ def rank_program(g, core, T, topo):
         for L in range(4):
             scan(V("SM", 128 + 32 * L, 160 + 32 * L), V("DN", 0, 32), V(KD, L, 128, 4), BIG, ALU.add, ALU.min)
         tt(V("red", 0, 128), V(KD, 0, 128), V("RT", 0, 128), ALU.is_le)
-        tt(V("KI", 0, 8), V("SM", 31, 256, 32), V("L8", 0, 8), ALU.add)
-        ts(V("CI", 0, 8), V("KI", 0, 8), 255, ALU.bitwise_and)
-        ts(V("OFF", 4, 8), V("CI", 0, 4), -1.0, ALU.mult, 135.0, ALU.add)
+        if PAIRED:
+            ts(V("CI", 0, 4), V("SM", 31, 128, 32), 255, ALU.bitwise_and)
+        else:
+            cp(V("KI", 0, 4), V("SM", 31, 128, 32))
+            ts(V("CI", 0, 4), V("KI", 0, 4), 255, ALU.bitwise_and)
+        ts(V("OFF", 0, 4), V("CI", 0, 4), -1.0, ALU.mult, 135.0, ALU.add)
         ts(V("NC", 0, 4), V("CI", 0, 4), -127.0, ALU.add)
-        ts(V("OFF", 0, 4), V("CI", 4, 8), 8.0, ALU.add)
+        tt(V("KI", 4, 8), V("SM", 159, 256, 32), V("L8", 0, 4), ALU.add)
+        ts(V("CI", 4, 8), V("KI", 4, 8), 255, ALU.bitwise_and)
+        ts(V("OFF", 4, 8), V("CI", 4, 8), 8.0, ALU.add)
         tt(V("pS", 0, 128), V("pP0", 0, 128), V("red", 0, 128), ALU.mult)
         tt(V("pS", 256, 384), V("pS", 0, 128), date, ALU.add)
         for L in range(4):
@@ -410,19 +533,20 @@ def rank_program(g, core, T, topo):
         tt(V("YT", 0, 128) if last else V(zt1, 0, 128), V("pS", 256, 384), V("RF", 0, 128), ALU.max)
         if not last:
             ways(s + 1)
-        tt(V("GD", 0, 64), IND(V(ow1, 0, 136), V("OFF", 4, 8)), V("DM", 0, 64), ALU.mult)
-        tt(V("GD", 64, 192), IND(V("HW", 0, 136), V("OFF", 0, 8)), V("DM", 0, 128), ALU.mult)
-        mm(V("pM", 0, 64), V("GM", 0, 128), V("GD", 0, 64))
-        mm(V("pM", 64, 128), V("GM", 0, 128), V("GD", 64, 128))
+        for t, (window, bank) in enumerate(((ow1, "pM"), ("HW", "pP0"))):
+            a, b = 64 * t, 64 * t + 64
+            tt(V("GD", a, b), IND(V(window, 0, 136), V("OFF", 4 * t, 4 * t + 4)), V("DM", 0, 64), ALU.mult)
+            mm(V(bank, 128, 192), V("GM", 0, 128), V("GD", a, b))
+            scan(BACK("OWN", a, b), BACK("ND", 0, 64), BACK("GD", a, b), 0.0, ALU.mult, ALU.add)
+            tt(V("NE", a, b), V(bank, 128, 192), V("OWN", a, b), ALU.not_equal)
+            scan(BACK("FS", a, b), BACK("NE", a, b), BACK("GD", a, b), 0.0, ALU.mult, ALU.add)
+            ts(V("fu", 8 * t, 8 * t + 8, 2), V("FS", a, b, 16), V("dump", 0, 1), ALU.max)
+        tt(V("GD", 128, 192), IND(V("HW", 0, 136), V("OFF", 0, 4)), V("DM", 0, 64), ALU.mult)
         mm(V("pR", 0, 64), V("G01", 0, 128), V("GD", 128, 192))
-        scan(BACK("OWN", 0, 128), BACK("ND", 0, 128), BACK("GD", 0, 128), 0.0, ALU.mult, ALU.add)
-        tt(V("NE", 0, 128), V("OWN", 0, 128), V("pM", 0, 128), ALU.not_equal)
-        scan(BACK("FS", 0, 128), BACK("NE", 0, 128), BACK("GD", 0, 128), 0.0, ALU.mult, ALU.add)
-        ts(V("fu", 0, 16, 2), V("FS", 0, 128, 16), V("dump", 0, 1), ALU.max)
         cp(V("HB", 0, 4), V("OWN", 64, 128, 16))
-        tt(V("gz", 0, 64), IND(XA, V("HB", 0, 4)), V("zh", 0, 64), ALU.add)
-        ts(V("ev", 0, 64), V("gz", 0, 64), EVEN, ALU.add, -EVEN, ALU.add)
-        line(V(zt1, 128, 192), V("ev", 0, 64), 0.5, 0.0)
+        tt(V("gz", 0, 64), IND(XA, V("HB", 0, 4)), V(zc, 128, 192), ALU.add)
+        ts(V("zi", 0, 64), V("gz", 0, 64), 0.5, ALU.mult, -0.25, ALU.add)
+        cp(V(zt1, 128, 192), V("zi", 0, 64))
         if not last:
             line(V("hx", 0, 64), V("pR", 0, 64), V("q1", 0, 1), 0.0)
             tt(V("PD", 0, 64), V("pR", 0, 64), V("hx", 0, 64), ALU.subtract)
@@ -430,10 +554,11 @@ def rank_program(g, core, T, topo):
             tile(zt1, TILEB)
             mm(V("pU0", 128, 256), V("GMb", 0, 128), V("red", 0, 128))
             line(V("junk", 0, 128), V("pU0", 128, 256), 32.0, A0 / 128, ACT.Identity, V("A32", 0, 1))
-            line(V("Q", 0, 128), V(ow1, 8, 136), 3232.0, V("A32", 0, 1))
-        write(XA, 8, zt1, 128)
+        write(XA, 8, "zi")
         tt(V("pS", 128, 256), V("pU0", 0, 128), V("red", 0, 128), ALU.mult)
         tt(V("NS%d" % (s + 1), 0, 128), V("pS", 128, 256), V(nr, 0, 128), ALU.add)
+        if not last:
+            h_terms(s + 1, V("A32", 0, 1))
         if last:
             dma("s", "o_x", ALL("yx"), V("XW", B0, WW), 1048576)
             line(V("ht", 0, 64), V("pR", 0, 64), 1.0, -float(B0))

@@ -1,9 +1,13 @@
 import math
+import numpy as np
 from concourse.mybir import AluOpType as ALU, ActivationFunctionType as ACT
 
-S, B0, WW, TW = 5, 32, 4128, 512
-BIG, CUT, EVEN = 2097152.0, 8192.0, 25165824.0
-PAIRED = True
+S, B0, WW, TW = 5, 96, 4192, 512
+DIRECT = True
+SPREAD = "aa"
+BIG, CUT = 2097152.0, 8192.0
+DATES = "t"
+NAMES = "t"
 
 
 def _sb(n, dtype="float32", p=128):
@@ -14,23 +18,25 @@ SCRATCH = {
     "XW": _sb(WW, "bfloat16"), "PW": _sb(WW, "bfloat16"), "PF": _sb(WW),
     "DF": _sb(2048, "bfloat16"), "AB": _sb(2048, "bfloat16"), "PG": _sb(2048, "bfloat16"),
     "DG": _sb(2048, "bfloat16"), "AC": _sb(2048, "bfloat16"),
-    "Z1": _sb(144, "bfloat16"), "ZK": _sb(144, "bfloat16"),
     "pxi": _sb(256, "int32"), "pxt": _sb(256, "int32"), "LH": _sb(512, "bfloat16"),
     "oli": _sb(128, "int32"), "nli": _sb(128, "int32"), "tli": _sb(128, "int32"),
     "thi": _sb(5, "int32", 8), "thf": _sb(5, "float32", 8), "GE1": _sb(128, "float32", 8), "GE": _sb(128, "float32", 8),
-    "ones": _sb(128), "oneb": _sb(128, "bfloat16", 1), "mid": _sb(128, "bfloat16", 1),
-    "G1": _sb(128), "GM": _sb(128), "GMb": _sb(128, "bfloat16"), "G01": _sb(128), "ID": _sb(128), "NID": _sb(128), "NIb": _sb(128, "bfloat16"),
-    "mod16": _sb(128), "colc": _sb(128), "DM": _sb(128), "ND": _sb(128), "UP": _sb(32), "DN": _sb(32), "L8": _sb(8),
-    "pidx": _sb(1, "int32"), "p16i": _sb(1, "int32"), "p16": _sb(1), "q1": _sb(1), "dump": _sb(1), "LM": _sb(5),
-    "HW": _sb(136), "Q": _sb(128), "A32": _sb(1), "junk": _sb(128),
+    "Z1": _sb(144, "bfloat16"), "ZK": _sb(144, "bfloat16"), "ones": _sb(128),
+    "oneb": _sb(128, "bfloat16", 1), "mid": _sb(128, "bfloat16", 1), "beta": _sb(128, "bfloat16", 1),
+    "G1": _sb(128), "GM": _sb(128), "GMb": _sb(128, "bfloat16"), "G01": _sb(128), "ID": _sb(128), "NID": _sb(128),
+    "NIb": _sb(128, "bfloat16"), "IDb": _sb(128, "bfloat16"), "N200": _sb(128, "bfloat16"), "N2": _sb(128, "bfloat16"),
+    "I8k": _sb(128, "bfloat16"), "N4k": _sb(128, "bfloat16"),
+    "mod16": _sb(64), "colc": _sb(128), "DM": _sb(64), "ND": _sb(64), "UP": _sb(32), "DN": _sb(32), "L8": _sb(4),
+    "pidx": _sb(1, "int32"), "p16i": _sb(1, "int32"), "p16": _sb(1), "p16m": _sb(1), "q1": _sb(1), "dump": _sb(8), "LM": _sb(5),
+    "HW": _sb(136), "A32": _sb(1), "junk": _sb(128), "OQ": _sb(256), "hv": _sb(256, "int32"), "hs": _sb(128, "int32"),
     "OM": _sb(128, "uint16"), "NM": _sb(128), "RU": _sb(128, "uint16"), "r12": _sb(256, "bfloat16"),
-    "hm": _sb(128), "hv": _sb(256, "int32"), "hs": _sb(128, "int32"), "OQ": _sb(256), "beta": _sb(128, "bfloat16", 1),
-    "e1": _sb(128), "e2": _sb(128), "RT": _sb(128), "red": _sb(128, "bfloat16"), "SM": _sb(256, "int32" if PAIRED else "float32"),
-    "zh": _sb(64),
-    "KI": _sb(8, "int32"), "CI": _sb(8, "int32"), "NC": _sb(4), "OFF": _sb(8, "uint16"),
-    "GD": _sb(192), "OWN": _sb(128), "NE": _sb(128), "FS": _sb(128), "fu": _sb(16, "uint16"),
-    "HB": _sb(4, "uint16"), "gz": _sb(64), "zi": _sb(64, "int32"),
-    "hx": _sb(64, "bfloat16"), "ht": _sb(64), "PD": _sb(64, "bfloat16"), "rf": _sb(128), "RF": _sb(128),
+    "e1": _sb(128), "e2": _sb(128), "RT": _sb(128), "red": _sb(128, "bfloat16"), "SM": _sb(256, "int32"),
+    "nmx": _sb(128, "bfloat16"), "Tz": _sb(128, "bfloat16"), "Tq": _sb(128, "bfloat16"), "Nw": _sb(128),
+    "KI": _sb(4, "int32"), "CI": _sb(8, "int32"), "NC": _sb(4), "OFF": _sb(8, "uint16"),
+    "GD": _sb(192), "OWN": _sb(128), "GX": _sb(528), "NE": _sb(528), "FS": _sb(528, "uint16" if DIRECT else "float32"),
+    "fu": _sb(8, "uint16"),
+    "HB": _sb(4, "uint16"), "zi": _sb(64, "int32"),
+    "hx": _sb(64, "bfloat16"), "ht": _sb(64), "PD": _sb(64, "bfloat16"), "rf": _sb(128), "RF": _sb(128, "bfloat16"),
     "YN": _sb(128), "YT": _sb(128), "YPg": _sb(256), "LO": _sb(512, "bfloat16"),
     "ZC": _sb((128 + TW) * S, "bfloat16"),
     "NR": _sb(128 * S),
@@ -44,82 +50,128 @@ for _n in ("pU0", "pU1", "pU2", "pP0", "pP1", "pR", "pM", "pS"):
     SCRATCH[_n] = ("psum", [128, 512], "float32")
 PIECE = {"%s%d" % (k, s): (k, SCRATCH[k][1][1] // n * s) for k, n in
          (("ZC", S), ("NR", S), ("HS", S), ("HR", S), ("OW", S + 1), ("ZT", S + 1), ("NS", S + 1)) for s in range(n)}
-PGATHER = (("a", 0, 16), ("v", 16, 32), ("a", 32, 48), ("v", 48, 64), ("a", 64, 96), ("a", 96, 128))
-ROADS = ((0, 32), (32, 64), (64, 96), (96, 128))
+PGATHER = (("a", 0, 16), ("a", 16, 40), ("v", 40, 64), ("a", 64, 96), ("a", 96, 128))
+ROADS = ((0, 16), (16, 64), (64, 96), (96, 128))
 UGATHER = ((0, 16), (16, 32), (32, 48), (48, 64), (64, 80), (80, 96), (96, 112), (112, 128))
 HPIECES = ((0, 32), (32, 64), (64, 96), (96, 128))
-DGATHER = ((0, 32), (32, 64), (64, 96), (96, 120), (120, 128))
+DGATHER = ((0, 32), (32, 48), (48, 64), (64, 96), (96, 112), (112, 128))
+DSHARE = (48, 96)
 DSUMS = ((0, 64), (64, 128))
-TURNS = ()
-TILEB = "aav"
+TILEB = "aa"
 TILEC = "ppp"
 RECV = ("rO", "rZ", "rN") + tuple("rH%d_" % i for i in range(len(HPIECES)))
 DMAS = ["d_px", "d_ol", "d_z", "d_tl", "d_nl", "d_th", "d_x", "d_x2", "d_lo", "d_hi",
         "o_x", "o_lo", "o_hi", "o_pf", "o_p", "o_z", "o_n", "o_t"]
 SEMAPHORES = ["v", "a", "t", "p", "loc"] + ["%s%d" % (k, s) for s in range(S) for k in RECV] + DMAS
-UB = ("pU0", "pU1", "pU2", "pU0")
+UB = ("pU0", "pU1", "pU2", "pU0", "pU1", "pU2")
 PB = ("pP0", "pP1", "pP0", "pP1")
 KD = "pU1"
 A0 = 65536.0 - 8388608.0 - 3232.0 * B0
-INORDER = True
-CALL, GATHER, SCATTER, PE, WAKE, LOAD, HOP = 60, 1.56, 3.8, 0.55, 210, 1900, 1750
-AHEAD = 200
-LATE = 2.0
-TRIES = 16000
+CYCLE, PE, GATHER, SCATTER, WAKE, LOAD, HOP, FIRST, LOCAL, LINK = [np.array(c) for c in (
+    (0.83, 1.16), (0.45, 0.63), (1.56, 1.9), (3.8, 5.0), (180.0, 200.0), (1600.0, 2000.0), (1600.0, 2200.0), (1500.0, 2000.0),
+    (300.0, 200.0), (60.0, 45.0))]
+WEIGHT = (1.0, 0.73)
+TRIES = 30000
 PLAN = {}
 
 
-def tighten(nodes, before, order, marks):
+def arrange(nodes, marks):
     n, last, seed = len(nodes), len(marks) - 1, [12345]
-    busy, on = [nd["busy"] for nd in nodes], [nd["q"] for nd in nodes]
+    on, busy0, busy1 = [nd["q"] for nd in nodes], [float(nd["busy"][0]) for nd in nodes], [float(nd["busy"][1]) for nd in nodes]
     step = [max(i for i in range(last + 1) if marks[i] <= k) for k in range(n)]
-    pre, post = [list(b.items()) for b in before], [[] for _ in nodes]
-    for k in range(n):
-        for j in before[k]:
+    pre, post, later, older = [], [[] for _ in nodes], [[] for _ in nodes], []
+    for k, nd in enumerate(nodes):
+        gaps = {j: (nd["gap"] if on[k] in "ld" else WAKE) if hard else WAKE * 0 for j, hard in nd["before"].items()}
+        pre.append([(j, float(gap[0]), float(gap[1])) for j, gap in gaps.items()
+                    if not any(older[m] >> j & 1 and other[0] >= gap[0] for m, other in gaps.items())])
+        older.append(0)
+        for j, gap, _ in pre[k]:
+            older[k] |= older[j] | 1 << j
             post[j].append(k)
+            later[j].append((k, gap, 0.0))
 
     def draw(m):
         seed[0] = (seed[0] * 1103515245 + 12345) % 2147483648
         return (seed[0] >> 8) % m
 
+    def landings(order):
+        order["l"] = [k + 1 for k in order["p"] if nodes[k]["signal"]]
+        order["d"] = [k for k in range(n) if on[k] == "d"]
+        return order
+
     def path(order):
-        prev, nxt, miss = [-1] * n, [-1] * n, [len(p) for p in pre]
+        prev, nxt, miss = [n] * n, [-1] * n, [len(p) for p in pre]
         for q in order.values():
             for a, b in zip(q, q[1:]):
                 prev[b], nxt[a] = a, b
                 miss[b] += 1
-        end, why, todo, done = [0.0] * n, [-1] * n, [k for k in range(n) if not miss[k]], 0
+        end0, end1, why0, why1 = [0.0] * (n + 1), [0.0] * (n + 1), [n] * n, [n] * n
+        todo, done = [k for k in range(n) if not miss[k]], 0
         while todo:
             k = todo.pop()
             done += 1
-            t, w = (end[prev[k]], prev[k]) if prev[k] >= 0 else (0.0, -1)
-            for j, gap in pre[k]:
-                if end[j] + gap >= t:
-                    t, w = end[j] + gap, j
-            end[k], why[k] = t + busy[k], w
-            for j in post[k] + ([nxt[k]] if nxt[k] >= 0 else []):
+            w0 = w1 = prev[k]
+            t0, t1 = end0[w0], end1[w1]
+            for j, gap0, gap1 in pre[k]:
+                if end0[j] + gap0 >= t0:
+                    t0, w0 = end0[j] + gap0, j
+                if end1[j] + gap1 >= t1:
+                    t1, w1 = end1[j] + gap1, j
+            end0[k], end1[k], why0[k], why1[k] = t0 + busy0[k], t1 + busy1[k], w0, w1
+            for j in post[k]:
+                miss[j] -= 1
+                if not miss[j]:
+                    todo.append(j)
+            j = nxt[k]
+            if j >= 0:
                 miss[j] -= 1
                 if not miss[j]:
                     todo.append(j)
         if done < n:
             return None
-        k = max(range(n), key=lambda j: end[j] + nodes[j]["lag"])
-        span, arcs = end[k] + nodes[k]["lag"], []
-        while why[k] >= 0:
-            if why[k] not in before[k]:
-                arcs.append((why[k], k))
-            k = why[k]
-        return span + 0.02 * sum(end) / n, arcs
+        arcs = []
+        for end, why in ((end0, why0), (end1, why1)):
+            k = end.index(max(end))
+            while why[k] < n:
+                if why[k] == prev[k] and why[k] not in nodes[k]["before"] and on[k] != "d":
+                    arcs.append((why[k], k))
+                k = why[k]
+        return sum(w * (max(end) + 0.05 * sum(end) / n) for w, end in zip(WEIGHT, (end0, end1))) / 2, arcs, end0, (max(end0), max(end1))
 
+    def pack(links, urgency):
+        order, end = {q: [] for q in "vatpsld"}, [0.0] * n
+        for k in sorted(range(n), key=lambda j: -urgency[j]):
+            at, taken = max([0.0] + [end[j] + gap for j, gap, _ in links[k]]), order[on[k]]
+            i = len(taken)
+            while i and end[taken[i - 1]] > at:
+                i -= 1
+            while i < len(taken) and end[taken[i]] - busy0[taken[i]] < at + busy0[k]:
+                at = max(at, end[taken[i]])
+                i += 1
+            taken.insert(i, k)
+            end[k] = at + busy0[k]
+        return landings(order), end
+
+    ahead = [0.0] * n
+    for k in range(n - 1, -1, -1):
+        ahead[k] = busy0[k] + max([0.0] + [ahead[j] + gap for j, gap, _ in later[k]])
+    order = pack(pre, ahead)[0]
     now = path(order)
-    best = (now[0], order)
+    best = (now[0], order, now[3])
     for it in range(TRIES):
+        if it % 500 == 0:
+            for urgency in ([busy0[k] - now[2][k] for k in range(n)], pack(later, now[2])[1]):
+                other = pack(pre, urgency)[0]
+                new = path(other)
+                if new is not None and new[0] < now[0]:
+                    order, now = other, new
         forward = draw(2)
         if draw(4) and now[1]:
             a, b = now[1][draw(len(now[1]))]
+            a, b = (a - 1, b - 1) if on[a] == "l" else (a, b)
             q = order[on[a]]
             i = q.index(a)
-            a, b = (q[max(0, i - (0, 0, 1, 2, 3)[draw(5)])], b) if forward else (a, q[min(len(q) - 1, i + 1 + draw(4))])
+            a, b = (q[max(0, i - (0, 0, 1, 2, 3)[draw(5)])], b) if forward else (a, q[min(len(q) - 1, q.index(b) + draw(4))])
         else:
             q = order["vvvaatp"[draw(7)]]
             i = draw(len(q) - 1)
@@ -134,12 +186,12 @@ def tighten(nodes, before, order, marks):
                     q.insert(j, q.pop(i))
         other = dict(order)
         other[on[a]] = q
-        new = path(other)
-        if new is not None and new[0] - now[0] <= -math.log((draw(4096) + 1) / 4097.0) * 150.0 * (1.0 - it / TRIES) ** 2:
+        new = path(landings(other))
+        if new is not None and new[0] - now[0] <= -math.log((draw(4096) + 1) / 4097.0) * 35.0 * (1.0 - it / TRIES) ** 2:
             order, now = other, new
             if now[0] < best[0]:
-                best = (now[0], order)
-    PLAN["spans"] = [best[0]]
+                best = (now[0], order, now[3])
+    PLAN["spans"] = best[2]
     return best[1]
 
 
@@ -149,94 +201,71 @@ def rank_program(g, core, T, topo):
         return
     nxt = T.cores[(rank + 1) % len(T.cores)]
     prv = T.cores[(rank - 1) % len(T.cores)]
-    queues = {"v": g.vector, "a": g.scalar, "t": g.tensor, "p": g, "s": g.sync, "l": None}
+    queues = {"v": g.vector, "a": g.scalar, "t": g.tensor, "p": g, "s": g.sync}
     psum = set(n for n in SCRATCH if SCRATCH[n][0] == "psum")
-    nodes, acc, marks = [], {}, [0]
+    nodes, acc, marks, sends = [], {}, [0], []
 
-    def node(q, calls, rd, wr, busy, lag=0.0, signal=None, beside=None):
-        me, before = len(nodes), {}
+    def node(q, calls, rd, wr, busy, signal=None, beside=None, landing=None):
+        before = {}
         for views, write in ((rd, False), (wr, True)):
             for (n, lo, hi, st) in [r for v in views for r in v[1]]:
                 for (k, alo, ahi, ast, aw) in acc.get(n, ()):
-                    same = nodes[k]["q"] == q and nodes[k]["signal"] is None and signal is None
+                    same = nodes[k]["q"] == q and (signal is None or n[:4] == "turn")
                     apart = ahi <= lo or alo >= hi or (st == ast and (lo - alo) % st)
                     if k == beside or (not (n in psum and (not same or q == "t")) and (apart or not (aw or write))):
                         continue
-                    before[k] = before.get(k, False) or not (same and write and (q == "t" or n[:4] == "turn" or (INORDER and not aw)))
-        nodes.append({"q": q, "calls": calls, "before": before, "busy": busy, "lag": lag, "signal": signal})
+                    before[k] = before.get(k, False) or not (same and write and (q == "t" or n[:4] == "turn" or not aw))
+        nodes.append({"q": q, "calls": calls, "before": before, "busy": busy + 0 * WAKE, "signal": signal})
+        first = len(nodes) - 1
+        if landing is not None:
+            nodes.append({"q": landing[0], "calls": [], "before": {first: True}, "gap": landing[1], "busy": landing[2], "signal": signal})
+        me = len(nodes) - 1
         for views, write in ((rd, False), (wr, True)):
             for (n, lo, hi, st) in [r for v in views for r in v[1]]:
                 old = acc.get(n, [])
                 if write and st == 1 and n not in psum and beside is None:
                     old = [a for a in old if not (lo <= a[1] and a[2] <= hi)]
-                acc[n] = old + [(me, lo, hi, st, write)]
+                acc[n] = old + [(first if n[:4] == "turn" else me, lo, hi, st, write)]
         return me
+
+    def turn(word):
+        return (None, [("turn" + word, 0, 1, 1)])
 
     def width(name):
         return 2 if SCRATCH[name][2] in ("bfloat16", "uint16") else 4
 
-    def cycles(o, ins, both):
+    def cost(o, ins, both=False):
         if len(ins[0]) > 3:
-            return CALL + GATHER * ins[0][2]
+            return 50 + GATHER * CYCLE * ins[0][2]
         if len(o) > 3:
-            return CALL + SCATTER * o[2]
+            return 50 + SCATTER * CYCLE * o[2]
         if both:
-            return max(64, ins[0][2] * (1 if any(v[1][0][0] in psum for v in ins) else 2))
-        return max(64, ins[0][2] * (0.5 if all(width(v[1][0][0]) == 2 for v in [o] + ins) else 1))
+            return CYCLE * max(64, ins[0][2] * (1 if any(v[1][0][0] in psum for v in ins) else 2))
+        return CYCLE * max(64, ins[0][2] * (0.5 if all(width(v[1][0][0]) == 2 for v in [o] + ins) else 1))
 
     def dma(q, sem, out, in_, size, beside=None, behind=()):
-        return node(q, [lambda: queues[q].dma_start(out=out[0], in_=in_[0])], [in_] + list(behind), [out], 60, LOAD + size / 300.0,
-                    (sem, 16), beside)
+        return node(q, [lambda: queues[q].dma_start(out=out[0], in_=in_[0])], [in_] + list(behind), [out, turn("d" + q)], 50,
+                    (sem, 16), beside, ("d", LOAD, size / LOCAL + 80))
 
     def send(dst_name, src_name, lo, hi, sem):
         src, dst = V(src_name, lo, hi), V(dst_name, lo, hi)
         rid, pid, _ = topo.addr(nxt)
-        call = node("p", [lambda: g.remote_dma(out_ap=dst[0], in_ap=src[0], remote_sem=T.sem[sem], local_sem=T.sem["loc"],
-                                               pid=pid, routing_id=rid, dma_engine_mask=topo.mask(core, nxt))],
-                    [src], [], 180, 0.0, ("loc", 0))
-        landing = node("l", [], [], [dst], 128 * src[2] * width(src[1][0][0]) / 55.0 + 150, HOP, (sem, len(topo.engines(prv, core))))
-        nodes[landing]["before"][call] = False
+        node("p", [lambda: g.remote_dma(out_ap=dst[0], in_ap=src[0], remote_sem=T.sem[sem], local_sem=T.sem["loc"],
+                                        pid=pid, routing_id=rid, dma_engine_mask=topo.mask(core, nxt))],
+             [src], [dst, turn("send")], 150 + (0 if sends else FIRST),
+             (sem, len(topo.engines(prv, core))), None, ("l", HOP - 150, 128 * src[2] * width(src[1][0][0]) / LINK + 160))
+        sends.append(sem)
 
     def issue():
-        n, on = len(nodes), [nd["q"] for nd in nodes]
-        before = [{j: nodes[j]["lag"] + WAKE if hard else 0.0 for j, hard in nd["before"].items()} for nd in nodes]
-        after = [{} for _ in nodes]
-        for k in range(n):
-            for j, gap in before[k].items():
-                after[j][k] = gap
-
-        def place(pre, post, head, urgency):
-            missing = [len(p) for p in pre]
-            ready = {k: head[k] for k in range(n) if not missing[k]}
-            free, order, end = {q: 0.0 for q in queues}, {q: [] for q in queues}, [0.0] * n
-            while ready:
-                first = min(ready, key=lambda j: (max(ready[j], free[on[j]]), j))
-                q = on[first]
-                now = max(ready[first], free[q])
-                k = max((j for j in ready if on[j] == q and ready[j] <= now + AHEAD),
-                        key=lambda j: (urgency[j] - LATE * max(0.0, ready[j] - now), -j))
-                free[q] = end[k] = max(ready.pop(k), free[q]) + nodes[k]["busy"]
-                order[q].append(k)
-                for j in post[k]:
-                    missing[j] -= 1
-                    if not missing[j]:
-                        ready[j] = max([head[j]] + [end[i] + gap for i, gap in pre[j].items()])
-            return max(end[k] + nodes[k]["lag"] for k in range(n)), order, end
-
-        back, end = [0.0] * n, place(before, after, [0.0] * n, [0.0] * n)[2]
-        for k in sorted(range(n), key=lambda j: -end[j]):
-            back[k] = nodes[k]["busy"] + max([nodes[k]["lag"]] + [back[j] + gap for j, gap in after[k].items()])
         if "order" not in PLAN:
-            PLAN["order"] = tighten(nodes, before, place(before, after, [0.0] * n, back)[1], marks)
+            PLAN["order"] = arrange(nodes, marks)
         order = PLAN["order"]
         count = {}
-        for q in queues:
+        for q in order:
             for k in order[q]:
                 if nodes[k]["signal"] is None:
                     count[q] = count.get(q, 0) + 1
-                    nodes[k]["done"] = (q, count[q])
-                else:
-                    nodes[k]["done"] = nodes[k]["signal"]
+                nodes[k]["done"] = nodes[k]["signal"] or (q, count[q])
         for q in queues:
             seen = {}
             for k in order[q]:
@@ -250,18 +279,15 @@ def rank_program(g, core, T, topo):
                         queues[q].wait_ge(T.sem[sem], needs[sem])
                         seen[sem] = needs[sem]
                 made = [call() for call in nodes[k]["calls"]]
-                if q == "l":
-                    continue
                 if nodes[k]["signal"] is None:
                     made[-1].then_inc(T.sem[q], 1)
                 elif q != "p":
                     made[-1].then_inc(T.sem[nodes[k]["signal"][0]], 16)
         for q in count:
             g.wait_ge(T.sem[q], count[q])
-        g.wait_ge(T.sem["loc"], len(topo.engines(core, nxt)) * len([nd for nd in nodes if nd["q"] == "p" and nd["signal"]]))
-        for nd in nodes:
-            if nd["signal"] and nd["q"] != "p":
-                g.wait_ge(T.sem[nd["signal"][0]], nd["signal"][1])
+        g.wait_ge(T.sem["loc"], len(topo.engines(core, nxt)) * len(sends))
+        for k in order["l"] + order["d"]:
+            g.wait_ge(T.sem[nodes[k]["signal"][0]], nodes[k]["signal"][1])
 
     def V(name, lo, hi, st=1):
         if name in PIECE:
@@ -269,8 +295,8 @@ def rank_program(g, core, T, topo):
             lo, hi = lo + base, hi + base
         return (T[name][:, lo:hi] if st == 1 else T[name][:, lo:hi:st], [(name, lo, hi, st)], len(range(lo, hi, st)))
 
-    def BACK(name, lo, hi):
-        return (T[name][:, hi - 1::-1] if lo == 0 else T[name][:, hi - 1:lo - 1:-1], [(name, lo, hi, 1)], hi - lo)
+    def BACK(name, lo, hi, st=1):
+        return (T[name][:, hi - st::-st] if lo < st else T[name][:, hi - st:lo - 1:-st], [(name, lo, hi, st)], (hi - lo) // st)
 
     def ALL(name):
         n = SCRATCH[name][1][1] if name in SCRATCH else 1
@@ -289,36 +315,36 @@ def rank_program(g, core, T, topo):
         return v if isinstance(v, (int, float)) or v is None else v[0]
 
     def op(q, call, rd, wr, busy):
-        turn = [(None, [("turn" + q, 0, 1, 1)])] if rd and len(rd[0]) > 3 and rd[0][2] >= 256 else []
-        node(q, [call], rd + [o[3] for o in wr if len(o) > 3], [(o[0], o[1][:1]) for o in wr] + turn, busy)
+        long = [turn(q)] if rd and len(rd[0]) > 3 and rd[0][2] >= 128 else []
+        node(q, [call], rd + [o[3] for o in wr if len(o) > 3], [(o[0], o[1][:1]) for o in wr] + long, busy)
 
     def tt(o, a, b, f):
-        op("v", lambda: g.vector.tensor_tensor(out=o[0], in0=a[0], in1=b[0], op=f), [a, b], [o], cycles(o, [a, b], True))
+        op("v", lambda: g.vector.tensor_tensor(out=o[0], in0=a[0], in1=b[0], op=f), [a, b], [o], cost(o, [a, b], True))
 
     def ts(o, a, s1, f1, s2=None, f2=None):
         if f2 is None:
             op("v", lambda: g.vector.tensor_scalar(out=o[0], in0=a[0], scalar1=raw(s1), scalar2=None, op0=f1), [a] + cols(s1), [o],
-               cycles(o, [a], False))
+               cost(o, [a]))
         else:
             op("v", lambda: g.vector.tensor_scalar(out=o[0], in0=a[0], scalar1=raw(s1), scalar2=raw(s2), op0=f1, op1=f2),
-               [a] + cols(s1, s2), [o], cycles(o, [a], False))
+               [a] + cols(s1, s2), [o], cost(o, [a]))
 
     def cp(o, a):
-        op("v", lambda: g.vector.tensor_copy(out=o[0], in_=a[0]), [a], [o], cycles(o, [a], False))
+        op("v", lambda: g.vector.tensor_copy(out=o[0], in_=a[0]), [a], [o], cost(o, [a]))
 
     def scan(o, d0, d1, first, f0, f1):
         op("v", lambda: g.vector.tensor_tensor_scan(out=o[0], data0=d0[0], data1=d1[0], initial=raw(first), op0=f0, op1=f1),
-           [d0, d1] + cols(first), [o], cycles(o, [d0, d1], False))
+           [d0, d1] + cols(first), [o], cost(o, [d0, d1]))
 
     def fill(o, c):
-        op("v", lambda: g.vector.memset(o[0], c), [], [o], cycles(o, [o], False))
+        op("v", lambda: g.vector.memset(o[0], c), [], [o], cost(o, [o]))
 
     def act(o, a, f=ACT.Copy):
-        op("a", lambda: g.scalar.activation(out=o[0], in_=a[0], func=f), [a], [o], CALL + GATHER * a[2] if len(a) > 3 else max(64, a[2]))
+        op("a", lambda: g.scalar.activation(out=o[0], in_=a[0], func=f), [a], [o], 15 + cost(o, [a]) if len(a) > 3 else CYCLE * max(64, a[2]))
 
     def line(o, a, scale, bias, f=ACT.Identity, total=None):
         op("a", lambda: g.scalar.activation(out=o[0], in_=a[0], func=f, bias=raw(bias), scale=raw(scale), accum_out=raw(total)),
-           [a] + cols(bias, scale), [o] + cols(total), max(64, a[2]))
+           [a] + cols(bias, scale), [o] + cols(total), CYCLE * max(64, a[2]))
 
     def mms(o, pairs, start=True, stop=True):
         node("t", [lambda l=l, r=r, i=i: g.tensor.matmul(out=o[0], lhsT=l[0], rhs=r[0], start=start and i == 0,
@@ -329,10 +355,10 @@ def rank_program(g, core, T, topo):
         mms(o, [(l, r)], start, stop)
 
     def iota(o, pattern, base, cm):
-        op("p", lambda: g.iota(o[0], pattern, base, cm, allow_small_or_imprecise_dtypes=True), [], [o], 150 + 2 * o[2])
+        op("p", lambda: g.iota(o[0], pattern, base, cm, allow_small_or_imprecise_dtypes=True), [], [o], 130 + 2 * CYCLE * o[2])
 
     def select(o, a, pattern, f, base, cm):
-        op("p", lambda: g.affine_select(o[0], a[0], pattern, f, 0.0, base, cm), [a], [o], 200 + 2 * o[2])
+        op("p", lambda: g.affine_select(o[0], a[0], pattern, f, 0.0, base, cm), [a], [o], 170 + 2 * CYCLE * o[2])
 
     def pool_copy(o, a):
         select(o, a, [[0, o[2]]], ALU.is_ge, 0, 0)
@@ -345,72 +371,40 @@ def rank_program(g, core, T, topo):
             copy[e](V(name, 128 + w, 128 + 2 * w), V(name, 128, 128 + w))
 
     def reduce16(src, c0, c1, w, out, first):
-        if first is not None:
-            mm(out, first[0], first[1], True, False)
-        mms(out, [(V(w, 15 - i, 143 - i), V(src, 16 * c0 + i, 16 * c1, 16)) for i in range(16)], first is None, True)
+        mm(out, first[0], first[1], True, False)
+        mms(out, [(V(w, 15 - i, 143 - i), V(src, 16 * c0 + i, 16 * c1, 16)) for i in range(16)], False, True)
 
-    named = {}
-
-    def name(word):
-        named[word] = len(nodes) - 1
-
-    def in_turn(words):
-        turn = [named[w] for w in words.split() if w in named]
-        for a, b in zip(turn, turn[1:]):
-            nodes[b]["before"].setdefault(a, False)
-
-    def distance(df, ab, a, b, off, tname, words):
+    def distance(df, ab, a, b, off, tname):
         tt(V(df, 16 * a, 16 * b), IND(XA, V(off, a, b)), V(tname, 128, 128 + 16 * (b - a)), ALU.subtract)
-        name(words[0])
         act(V(ab, 16 * a, 16 * b), V(df, 16 * a, 16 * b), ACT.Abs)
-        name(words[1])
 
     def h_terms(s, bias):
-        if not PAIRED:
-            line(V("Q", 0, 128), V("OW%d" % s, 8, 136), 3232.0, bias)
-            return
-        act(V("OQ", 1, 256, 2), V("OW%d" % s, 8, 136))
+        line(V("OQ", 1, 256, 2), V("OW%d" % s, 8, 136), 1.0, 32.0 - B0)
         for q, (a, b) in enumerate(HPIECES):
             line(V(UB[q], 2 * a + 1, 2 * b, 2), V("OW%d" % s, 8 + a, 8 + b), 3232.0, bias)
 
     def h_of(q, s):
         a, b = HPIECES[q]
-        u = V(UB[q], 2 * a, 2 * b, 2) if PAIRED else V(UB[q], 0, b - a)
-        reduce16("AB", a, b, "Z1", u, (ALL("oneb"), V("mid", 0, b - a)))
-        name("u%d" % q)
-        if PAIRED:
-            scan(V("hv", 2 * a, 2 * b), V("OQ", 2 * a, 2 * b), V(UB[q], 2 * a, 2 * b), 0.0, ALU.mult, ALU.add)
-            name("m%d" % q)
-            whole = V("hv", 2 * a + 1, 2 * b, 2)
-        else:
-            tt(V("hm", a, b), u, V("OW%d" % s, 8 + a, 8 + b), ALU.mult)
-            name("m%d" % q)
-            tt(V("hv", a, b), V("hm", a, b), V("Q", a, b), ALU.add)
-            name("v%d" % q)
-            whole = V("hv", a, b)
-        ts(V("hs", a, b), whole, 5, ALU.arith_shift_right, 4095, ALU.bitwise_and)
-        name("s%d" % q)
+        reduce16("AB", a, b, "Z1", V(UB[q], 2 * a, 2 * b, 2), (ALL("oneb"), V("mid", 0, b - a)))
+        scan(V("hv", 2 * a, 2 * b), V("OQ", 2 * a, 2 * b), V(UB[q], 2 * a, 2 * b), 0.0, ALU.mult, ALU.add)
+        ts(V("hs", a, b), V("hv", 2 * a + 1, 2 * b, 2), 5, ALU.arith_shift_right, 4095, ALU.bitwise_and)
         ts(V("HS%d" % s, a, b), V("hs", a, b), float(B0), ALU.add)
-        name("H%d" % q)
         send("HR%d" % s, "HS%d" % s, a, b, "rH%d_%d" % (q, s))
 
     def ways_open(s, names):
         mm(V("pP1", 0, 128), V("ID", 0, 128), V("OW%d" % s, 8, 136), True, False)
         mm(V("pU2", 0, 128), V("ID", 0, 128), names, True, False)
 
-    def ways(s):
-        date = V("ZT%d" % s, 0, 128)
-        line(V("r12", 0, 128), date, -CUT, CUT * (s + 1), ACT.Relu)
+    def ways(date, a1, b1, a2, b2):
+        line(V("r12", 0, 128), date, a1, b1, ACT.Relu)
+        line(V("r12", 128, 256), date, a2, b2, ACT.Relu)
         mm(V("pP1", 0, 128), V("NIb", 0, 128), V("r12", 0, 128), False, True)
         cp(V("OM", 0, 128), V("pP1", 0, 128))
-        line(V("r12", 128, 256), date, CUT, -CUT * s, ACT.Relu)
         mm(V("pU2", 0, 128), V("NIb", 0, 128), V("r12", 128, 256), False, True)
         act(V("NM", 0, 128), V("pU2", 0, 128), ACT.Relu)
 
-    def write(win, fu, data, base=0):
-        for L in (3, 2, 1, 0):
-            cp(IND(win, V("fu", fu + 2 * L, fu + 2 * L + 1)), V(data, base + 16 * L, base + 16 * L + 16))
-            name("%s%d" % (win[1][0][0][0].lower(), L))
+    def write(win, t, data, base=0):
+        cp(IND(win, V("FS", 264 * t, 264 * t + 4) if DIRECT else V("fu", 4 * t, 4 * t + 4)), V(data, base, base + 64))
 
     dma("s", "d_px", V("pxi", 0, 256), ALL("px"), 131072)
     dma("a", "d_ol", V("oli", 0, 128), ALL("ol"), 65536)
@@ -418,7 +412,7 @@ def rank_program(g, core, T, topo):
     dma("a", "d_nl", V("nli", 0, 128), ALL("nl"), 65536)
     dma("s", "d_z", V("ZT0", 128, 192), ALL("z"), 16384)
     dma("a", "d_th", ALL("thi"), ALL("th"), 160)
-    dma("s", "d_x", V("XW", B0, B0 + 2048), (T["x"][:, 0:2048], []), 0)
+    dma("s", "d_x", V("XW", B0, B0 + 2048), (T["x"][:, 0:2048], []), 524288)
     fill(V("ones", 0, 128), 1.0)
     fill(V("PW", 0, WW), 0.0)
     select(V("ID", 0, 128), V("ones", 0, 128), [[1, 128]], ALU.is_equal, 0, -1)
@@ -432,24 +426,25 @@ def rank_program(g, core, T, topo):
     ts(V("pxt", 0, 256), V("pxi", 0, 256), B0, ALU.add)
     tt(V("LH", 0, 256), V("pxt", 0, 256), V("LH", 256, 512), ALU.subtract)
     dma("s", "d_lo", ROW("PW", 0), V("LH", 0, 256), 65536, high)
-    dma("s", "d_x2", V("XW", B0 + 2048, WW), (T["x"][:, 2048:4096], []), 0, None, [V("LH", 0, 256)])
+    dma("s", "d_x2", V("XW", B0 + 2048, WW), (T["x"][:, 2048:4096], []), 524288)
     ts(V("OW0", 8, 136), V("oli", 0, 128), B0, ALU.add)
     cp(V("ZT0", 0, 128), V("tli", 0, 128))
     ts(V("NS0", 0, 128), V("nli", 0, 128), B0, ALU.add)
-    line(V("NIb", 0, 128), V("ID", 0, 128), -1.0, 0.0)
+    for k, c in (("NIb", -1.0), ("NID", -1.0), ("IDb", 1.0), ("N200", -200.0), ("N2", -2.0), ("I8k", 8192.0), ("N4k", -4096.0)):
+        line(V(k, 0, 128), V("ID", 0, 128), c, 0.0)
     ways_open(0, V("NS0", 0, 128))
-    ways(0)
+    ways(V("ZT0", 0, 128), -CUT, CUT, CUT, 0.0)
     cp(V("Z1", 15, 143, 16), V("GM", 0, 128, 16))
-    tile("ZT0", "vvv")
+    tile("ZT0", "vvv"[:len(TILEB)])
     fill(V("OQ", 0, 256, 2), 0.0)
     h_terms(0, A0)
-    iota(ALL("beta"), [[0, 32], [-1, 4]], 3, 0)
+    iota(ALL("beta"), [[0, 32], [1, 4]], 132, 0)
     fill(ALL("oneb"), 1.0)
     fill(ALL("mid"), -2048.0)
     iota(V("pidx", 0, 1), [[0, 1]], 0, 1)
-    iota(V("mod16", 0, 128), [[0, 8], [1, 16]], 0, 0)
+    iota(V("mod16", 0, 64), [[0, 4], [1, 16]], 0, 0)
     iota(V("colc", 0, 128), [[1, 128]], 0, 0)
-    iota(V("L8", 0, 4), [[2, 4]], 121, 0)
+    iota(V("L8", 0, 4), [[2, 4]], 264, 0)
     select(V("G01", 0, 128), V("GM", 0, 128), [[0, 8], [-1, 16]], ALU.is_ge, 1, 0)
     select(ALL("GE1"), (T["ones"][0:8, 0:128], [("ones", 0, 128, 1)], 128), [[1, 128]], ALU.is_ge, 0, -16)
     select(ALL("GE"), ALL("GE1"), [[-1, 128]], ALU.is_ge, 15, 16)
@@ -459,35 +454,35 @@ def rank_program(g, core, T, topo):
     fill(V("UP", 0, 32), 4.0)
     fill(V("DN", 0, 32), -4.0)
     fill(V("HW", 0, 8), 0.0)
-    ts(V("ZK", 0, 144), V("Z1", 0, 144), 256.0, ALU.mult)
-    ts(V("DM", 0, 128), V("mod16", 0, 128), V("p16", 0, 1), ALU.is_equal)
-    ts(V("ND", 0, 128), V("mod16", 0, 128), V("p16", 0, 1), ALU.not_equal)
+    ts(V("ZK", 0, 144), V("Z1", 0, 144), -256.0, ALU.mult)
+    ts(V("DM", 0, 64), V("mod16", 0, 64), V("p16", 0, 1), ALU.is_equal)
+    ts(V("ND", 0, 64), V("mod16", 0, 64), V("p16", 0, 1), ALU.not_equal)
+    line(V("p16m", 0, 1), V("p16", 0, 1), 1.0, -128.0)
     ts(V("q1", 0, 1), V("p16", 0, 1), 1.0, ALU.is_equal)
-    ts(V("dump", 0, 1), V("p16", 0, 1), 16.0, ALU.add)
-    line(V("NID", 0, 128), V("ID", 0, 128), -1.0, 0.0)
+    fill(V("GX", 0, 528), 0.0)
+    fill(V("NE", 0, 528, 66), 1.0)
+    iota(V("dump", 0, 8), [[0, 2], [16, 4]], 16, 0)
+    ts(V("GX", 0, 528, 66), V("dump", 0, 8), V("p16", 0, 1), ALU.add)
     act(V("GMb", 0, 128), V("GM", 0, 128))
     mm(V("pM", 128, 133), ALL("GE"), ALL("thf"))
-    line(V("LM", 0, 5), V("pM", 128, 133), 256.0, 3.0)
+    line(V("LM", 0, 5), V("pM", 128, 133), -256.0, 132.0)
 
     for s in range(S):
         last = s == S - 1
         marks.append(len(nodes))
         zt, zc, nr, hr, zt1, ow1 = "ZT%d" % s, "ZC%d" % s, "NR%d" % s, "HR%d" % s, "ZT%d" % (s + 1), "OW%d" % (s + 1)
         date, lim = V(zc, 0, 128), V("LM", s, s + 1)
-        send(zc, zt, 0, 192, "rZ%d" % s)
         send(ow1, "OW%d" % s, 0, 136, "rO%d" % s)
+        send(zc, zt, 0, 192, "rZ%d" % s)
         send(nr, "NS%d" % s, 0, 128, "rN%d" % s)
         tile(zc, TILEC)
-        for i, (e, a, b) in enumerate(PGATHER):
+        for (e, a, b) in PGATHER:
             copy[e](V("PG", 16 * a, 16 * b), IND(PA, V("OM", a, b)))
-            name("P%d" % i)
         for q, (a, b) in enumerate(ROADS):
             reduce16("PG", a, b, "Z1", V(PB[q], 0, b - a), (V("ID", 0, 128), V("NM", a, b)))
-            name("r%d" % q)
             cp(V("RU", a, b), V(PB[q], 0, b - a))
-            name("R%d" % q)
-        for i, (a, b) in enumerate(UGATHER):
-            distance("DF", "AB", a, b, "RU", zt, ("U%d" % i, "A%d" % i))
+        for (a, b) in UGATHER:
+            distance("DF", "AB", a, b, "RU", zt)
         for q in range(len(HPIECES)):
             h_of(q, s)
         if last:
@@ -498,74 +493,103 @@ def rank_program(g, core, T, topo):
             dma("s", "o_pf", ROW("PF", 0), V("YPg", 0, 256), 131072)
         line(V("e1", 0, 128), date, 1.0, -(s + 99) / 2.0, ACT.Abs)
         line(V("e2", 0, 128), V("e1", 0, 128), -BIG, BIG * (99 - s) / 2.0, ACT.Relu)
-        line(V("RT", 0, 128), V("e2", 0, 128), -1.0, lim)
-        line(V("pP0", 0, 128), date, -1.0, float(s + 2))
-        for i, (a, b) in enumerate(DGATHER):
-            distance("DG", "AC", a, b, hr, zc, ("D%d" % i, "B%d" % i))
+        line(V("RT", 0, 128), V("e2", 0, 128), 1.0, lim)
+        if DATES == "v":
+            line(V("pP0", 0, 128), date, -1.0, float(s + 2))
+        elif not last:
+            line(V("nmx", 0, 128), date, -1.0, float(s + 2), ACT.Relu)
+        if DSHARE:
+            mm(V("pM", 0, 256), V("IDb", 0, 128), V(zc, 128, 384))
+        for (a, b) in DGATHER:
+            if a in DSHARE:
+                act(V("PG", 16 * a, 16 * b), IND(XA, V(hr, a, b)))
+                tt(V("DG", 16 * a, 16 * b), V("PG", 16 * a, 16 * b), V("pM", 0, 16 * (b - a)), ALU.subtract)
+                act(V("AC", 16 * a, 16 * b), V("DG", 16 * a, 16 * b), ACT.Abs)
+            else:
+                distance("DG", "AC", a, b, hr, zc)
         for (a, b) in DSUMS:
             reduce16("AC", a, b, "ZK", V(KD, a, b), (ALL("oneb"), V("beta", a, b)))
-        for words in TURNS:
-            in_turn(words)
         if not last:
             ways_open(s + 1, V(nr, 0, 128))
         cp(V("HW", 8, 136), V(hr, 0, 128))
-        mms(V("pU0", 0, 128), [(V("ID", 0, 128), V("HW", 8, 136)), (V("NID", 0, 128), V(nr, 0, 128))])
+        mms(V("pU0", 0, 128), [(V("NID", 0, 128), V(nr, 0, 128)), (V("ID", 0, 128), V("HW", 8, 136))], True, NAMES == "v")
         for L in range(4):
-            scan(V("SM", 32 * L, 32 * L + 32), V("UP", 0, 32), V(KD, L, 128, 4), lim, ALU.add, ALU.max)
+            scan(V("SM", 32 * L, 32 * L + 32), V("DN", 0, 32), V(KD, L, 128, 4), lim, ALU.add, ALU.min)
         for L in range(4):
-            scan(V("SM", 128 + 32 * L, 160 + 32 * L), V("DN", 0, 32), V(KD, L, 128, 4), BIG, ALU.add, ALU.min)
-        tt(V("red", 0, 128), V(KD, 0, 128), V("RT", 0, 128), ALU.is_le)
-        if PAIRED:
-            ts(V("CI", 0, 4), V("SM", 31, 128, 32), 255, ALU.bitwise_and)
-        else:
-            cp(V("KI", 0, 4), V("SM", 31, 128, 32))
-            ts(V("CI", 0, 4), V("KI", 0, 4), 255, ALU.bitwise_and)
-        ts(V("OFF", 0, 4), V("CI", 0, 4), -1.0, ALU.mult, 135.0, ALU.add)
-        ts(V("NC", 0, 4), V("CI", 0, 4), -127.0, ALU.add)
-        tt(V("KI", 4, 8), V("SM", 159, 256, 32), V("L8", 0, 4), ALU.add)
-        ts(V("CI", 4, 8), V("KI", 4, 8), 255, ALU.bitwise_and)
-        ts(V("OFF", 4, 8), V("CI", 4, 8), 8.0, ALU.add)
-        tt(V("pS", 0, 128), V("pP0", 0, 128), V("red", 0, 128), ALU.mult)
-        tt(V("pS", 256, 384), V("pS", 0, 128), date, ALU.add)
+            scan(V("SM", 128 + 32 * L, 160 + 32 * L), V("UP", 0, 32), V(KD, L, 128, 4), -BIG, ALU.add, ALU.max)
+        tt(V("red", 0, 128), V(KD, 0, 128), V("RT", 0, 128), ALU.is_ge)
+        tt(V("KI", 0, 4), V("L8", 0, 4), V("SM", 159, 256, 32), ALU.subtract)
+        ts(V("CI", 0, 4), V("SM", 31, 128, 32), 255, ALU.bitwise_and)
+        ts(V("CI", 4, 8), V("KI", 0, 4), 255, ALU.bitwise_and)
+        cp(V("OFF", 0, 4), V("CI", 0, 4))
+        cp(V("OFF", 4, 8), V("CI", 4, 8))
+        ts(V("NC", 0, 4), V("CI", 0, 4), -1.0, ALU.mult, 8.0, ALU.add)
         for L in range(4):
             line(V("rf", L, 128, 4), V("colc", L, 128, 4), 1.0, V("NC", L, L + 1), ACT.Abs)
         line(V("RF", 0, 128), V("rf", 0, 128), -99.0, 99.0, ACT.Relu)
-        tt(V("YT", 0, 128) if last else V(zt1, 0, 128), V("pS", 256, 384), V("RF", 0, 128), ALU.max)
-        if not last:
-            ways(s + 1)
+        dates = V("YT", 0, 128) if last else V(zt1, 0, 128)
+        if DATES == "v":
+            tt(V("pS", 0, 128), V("pP0", 0, 128), V("red", 0, 128), ALU.mult)
+            tt(V("pS", 256, 384), V("pS", 0, 128), date, ALU.add)
+            tt(dates, V("pS", 256, 384), V("RF", 0, 128), ALU.max)
+            if not last:
+                ways(V(zt1, 0, 128), -CUT, CUT * (s + 2), CUT, -CUT * (s + 1))
+        else:
+            gone = [(V("N200", 0, 128), V("red", 0, 128)), (V("N2", 0, 128), V("RF", 0, 128))]
+            if not last:
+                mms(V("pS", 0, 128), [(V("IDb", 0, 128), V("nmx", 0, 128))] + gone[:1], True, False)
+                mms(V("pS", 0, 128), gone[1:], False, True)
+                ways(V("pS", 0, 128), CUT, 0.0, -CUT, CUT)
+            mms(V("pS", 128, 256), [(V("IDb", 0, 128), date)] + gone)
+            act(V("Tz", 0, 128), V("pS", 128, 256), ACT.Relu)
+            line(V("Tq", 0, 128), V("red", 0, 128), float(s + 2), 0.0)
+            mms(V("pS", 256, 384), [(V("IDb", 0, 128), V(k, 0, 128)) for k in ("Tq", "RF", "Tz")])
+            act(dates, V("pS", 256, 384))
         for t, (window, bank) in enumerate(((ow1, "pM"), ("HW", "pP0"))):
             a, b = 64 * t, 64 * t + 64
             tt(V("GD", a, b), IND(V(window, 0, 136), V("OFF", 4 * t, 4 * t + 4)), V("DM", 0, 64), ALU.mult)
             mm(V(bank, 128, 192), V("GM", 0, 128), V("GD", a, b))
             scan(BACK("OWN", a, b), BACK("ND", 0, 64), BACK("GD", a, b), 0.0, ALU.mult, ALU.add)
-            tt(V("NE", a, b), V(bank, 128, 192), V("OWN", a, b), ALU.not_equal)
-            scan(BACK("FS", a, b), BACK("NE", a, b), BACK("GD", a, b), 0.0, ALU.mult, ALU.add)
-            ts(V("fu", 8 * t, 8 * t + 8, 2), V("FS", a, b, 16), V("dump", 0, 1), ALU.max)
+            for L in range(4):
+                c, w = 264 * t + 66 * L, 16 * L + 17
+                copy[SPREAD[t]](V("GX", c + w - 16, c + w), V("GD", a + 16 * L, a + 16 * L + 16))
+                ts(V("NE", c + 1, c + w), V(bank, 128, 127 + w), V("OWN", a + 16 * L, a + 16 * L + 1), ALU.not_equal)
+                scan(BACK("FS", 264 * t + L, 264 * t + L + 4 * w, 4), BACK("NE", c, c + w), BACK("GX", c, c + w), 0.0, ALU.mult, ALU.max)
+            if not DIRECT:
+                cp(V("fu", 4 * t, 4 * t + 4), V("FS", 264 * t, 264 * t + 4))
         tt(V("GD", 128, 192), IND(V("HW", 0, 136), V("OFF", 0, 4)), V("DM", 0, 64), ALU.mult)
         mm(V("pR", 0, 64), V("G01", 0, 128), V("GD", 128, 192))
-        cp(V("HB", 0, 4), V("OWN", 64, 128, 16))
-        tt(V("gz", 0, 64), IND(XA, V("HB", 0, 4)), V(zc, 128, 192), ALU.add)
-        ts(V("zi", 0, 64), V("gz", 0, 64), 0.5, ALU.mult, -0.25, ALU.add)
-        cp(V(zt1, 128, 192), V("zi", 0, 64))
+        ts(V("HB", 0, 4), V("CI", 4, 8), 16.0, ALU.mult, V("p16m", 0, 1), ALU.add)
+        ts(V("zi", 0, 64), IND(V("DG", 0, 2048), V("HB", 0, 4)), 0.5, ALU.mult, -0.25, ALU.add)
+        tt(V(zt1, 128, 192), V("zi", 0, 64), V(zc, 128, 192), ALU.add)
         if not last:
             line(V("hx", 0, 64), V("pR", 0, 64), V("q1", 0, 1), 0.0)
             tt(V("PD", 0, 64), V("pR", 0, 64), V("hx", 0, 64), ALU.subtract)
             write(PA, 0, "PD")
             tile(zt1, TILEB)
+        if NAMES != "v":
+            mm(V("pU0", 0, 128), V("I8k", 0, 128), V("red", 0, 128), False, True)
+        if not last:
             mm(V("pU0", 128, 256), V("GMb", 0, 128), V("red", 0, 128))
             line(V("junk", 0, 128), V("pU0", 128, 256), 32.0, A0 / 128, ACT.Identity, V("A32", 0, 1))
-        write(XA, 8, "zi")
-        tt(V("pS", 128, 256), V("pU0", 0, 128), V("red", 0, 128), ALU.mult)
-        tt(V("NS%d" % (s + 1), 0, 128), V("pS", 128, 256), V(nr, 0, 128), ALU.add)
+        write(XA, 1, zt1, 128)
+        if NAMES == "v":
+            tt(V("pU0", 256, 384), V("pU0", 0, 128), V("red", 0, 128), ALU.mult)
+            tt(V("NS%d" % (s + 1), 0, 128), V("pU0", 256, 384), V(nr, 0, 128), ALU.add)
+        else:
+            line(V("Nw", 0, 128), V("pU0", 0, 128), 1.0, -4096.0, ACT.Relu)
+            mms(V("pU0", 256, 384), [(V("ID", 0, 128), V(nr, 0, 128)), (V("N4k", 0, 128), V("red", 0, 128)), (V("ID", 0, 128), V("Nw", 0, 128))])
+            line(V("YN", 0, 128) if last else V("NS%d" % (s + 1), 0, 128), V("pU0", 256, 384), 1.0, -float(B0) if last else 0.0)
         if not last:
             h_terms(s + 1, V("A32", 0, 1))
         if last:
-            dma("s", "o_x", ALL("yx"), V("XW", B0, WW), 1048576)
+            if NAMES == "v":
+                ts(V("YN", 0, 128), V("NS%d" % (s + 1), 0, 128), -float(B0), ALU.add)
             line(V("ht", 0, 64), V("pR", 0, 64), 1.0, -float(B0))
             write(V("PF", 0, WW), 0, "ht")
-            ts(V("YN", 0, 128), V("NS%d" % (s + 1), 0, 128), -float(B0), ALU.add)
-            dma("s", "o_t", ALL("yt"), V("YT", 0, 128), 65536)
             dma("a", "o_z", ALL("yz"), V(zt1, 128, 192), 16384)
+            dma("s", "o_x", ALL("yx"), V("XW", B0, WW), 1048576)
+            dma("a", "o_t", ALL("yt"), V("YT", 0, 128), 65536)
+            dma("a", "o_n", ALL("yn"), V("YN", 0, 128), 65536)
             dma("a", "o_p", ALL("yp"), ROW("PF", 0), 131072)
-            dma("s", "o_n", ALL("yn"), V("YN", 0, 128), 65536)
     issue()

@@ -4,8 +4,8 @@ from concourse.mybir import AluOpType as ALU, ActivationFunctionType as ACT
 
 S, B0, WW, TW = 5, 96, 4192, 512
 DIRECT = True
-SPREAD = "aa"
-BIG, CUT = 2097152.0, 8192.0
+SPREAD = "va"
+BIG, CUT, ROUND, K0 = 4194304.0, 8192.0, 6442450944.0, 272
 DATES = "t"
 NAMES = "t"
 
@@ -24,16 +24,16 @@ SCRATCH = {
     "Z1": _sb(144, "bfloat16"), "ZK": _sb(144, "bfloat16"), "ones": _sb(128),
     "oneb": _sb(128, "bfloat16", 1), "mid": _sb(128, "bfloat16", 1), "beta": _sb(128, "bfloat16", 1),
     "G1": _sb(128), "GM": _sb(128), "GMb": _sb(128, "bfloat16"), "G01": _sb(128), "ID": _sb(128), "NID": _sb(128),
-    "NIb": _sb(128, "bfloat16"), "IDb": _sb(128, "bfloat16"), "N200": _sb(128, "bfloat16"), "N2": _sb(128, "bfloat16"),
+    "N8k": _sb(128, "bfloat16"), "IDb": _sb(128, "bfloat16"), "N200": _sb(128, "bfloat16"), "N2": _sb(128, "bfloat16"),
     "I8k": _sb(128, "bfloat16"), "N4k": _sb(128, "bfloat16"),
-    "mod16": _sb(64), "colc": _sb(128), "DM": _sb(64), "ND": _sb(64), "UP": _sb(32), "DN": _sb(32), "L8": _sb(4),
+    "mod16": _sb(64), "colc": _sb(128), "DM": _sb(64), "AGE": _sb(144),
     "pidx": _sb(1, "int32"), "p16i": _sb(1, "int32"), "p16": _sb(1), "p16m": _sb(1), "q1": _sb(1), "dump": _sb(8), "LM": _sb(5),
     "HW": _sb(136), "A32": _sb(1), "junk": _sb(128), "OQ": _sb(256), "hv": _sb(256, "int32"), "hs": _sb(128, "int32"),
-    "OM": _sb(128, "uint16"), "NM": _sb(128), "RU": _sb(128, "uint16"), "r12": _sb(256, "bfloat16"),
-    "e1": _sb(128), "e2": _sb(128), "RT": _sb(128), "red": _sb(128, "bfloat16"), "SM": _sb(256, "int32"),
-    "nmx": _sb(128, "bfloat16"), "Tz": _sb(128, "bfloat16"), "Tq": _sb(128, "bfloat16"), "Nw": _sb(128),
-    "KI": _sb(4, "int32"), "CI": _sb(8, "int32"), "NC": _sb(4), "OFF": _sb(8, "uint16"),
-    "GD": _sb(192), "OWN": _sb(128), "GX": _sb(528), "NE": _sb(528), "FS": _sb(528, "uint16" if DIRECT else "float32"),
+    "OM": _sb(128, "uint16"), "NM": _sb(128), "RU": _sb(128, "uint16"), "nm": _sb(128, "bfloat16"),
+    "e1": _sb(128), "e2": _sb(128), "RT": _sb(128), "red": _sb(128, "bfloat16"), "SM": _sb(288),
+    "nmx": _sb(128, "bfloat16"), "nmy": _sb(128, "bfloat16"), "Tz": _sb(128, "bfloat16"), "Tq": _sb(128, "bfloat16"), "Nw": _sb(128),
+    "NC": _sb(4), "OFF": _sb(8, "uint16"),
+    "GD": _sb(192), "OWN": _sb(12), "GX": _sb(528), "NE": _sb(528), "FS": _sb(528, "uint16" if DIRECT else "float32"),
     "fu": _sb(8, "uint16"),
     "HB": _sb(4, "uint16"), "zi": _sb(64, "int32"),
     "hx": _sb(64, "bfloat16"), "ht": _sb(64), "PD": _sb(64, "bfloat16"), "rf": _sb(128), "RF": _sb(128, "bfloat16"),
@@ -50,16 +50,18 @@ for _n in ("pU0", "pU1", "pU2", "pP0", "pP1", "pR", "pM", "pS"):
     SCRATCH[_n] = ("psum", [128, 512], "float32")
 PIECE = {"%s%d" % (k, s): (k, SCRATCH[k][1][1] // n * s) for k, n in
          (("ZC", S), ("NR", S), ("HS", S), ("HR", S), ("OW", S + 1), ("ZT", S + 1), ("NS", S + 1)) for s in range(n)}
-PGATHER = (("a", 0, 16), ("a", 16, 40), ("v", 40, 64), ("a", 64, 96), ("a", 96, 128))
-ROADS = ((0, 16), (16, 64), (64, 96), (96, 128))
+PGATHER = (("a", 0, 16), ("v", 16, 32), ("a", 32, 48), ("v", 48, 64), ("a", 64, 80), ("a", 80, 96), ("a", 96, 112), ("a", 112, 128))
+ROADS = ((0, 32), (32, 64), (64, 96), (96, 128))
 UGATHER = ((0, 16), (16, 32), (32, 48), (48, 64), (64, 80), (80, 96), (96, 112), (112, 128))
-HPIECES = ((0, 32), (32, 64), (64, 96), (96, 128))
-DGATHER = ((0, 32), (32, 48), (48, 64), (64, 96), (96, 112), (112, 128))
-DSHARE = (48, 96)
+HPIECES = ((0, 32), (32, 64), (64, 96), (96, 112), (112, 128))
+DGATHER = ((0, 32), (32, 48), (48, 64), (64, 80), (80, 96), (96, 112), (112, 128))
+DSHARE = (48, 80)
 DSUMS = ((0, 64), (64, 128))
 TILEB = "aa"
 TILEC = "ppp"
-RECV = ("rO", "rZ", "rN") + tuple("rH%d_" % i for i in range(len(HPIECES)))
+TSEND = 0
+NSEND = 5
+RECV = ("rO", "rZ", "rT", "rN") + tuple("rH%d_" % i for i in range(len(HPIECES)))
 DMAS = ["d_px", "d_ol", "d_z", "d_tl", "d_nl", "d_th", "d_x", "d_x2", "d_lo", "d_hi",
         "o_x", "o_lo", "o_hi", "o_pf", "o_p", "o_z", "o_n", "o_t"]
 SEMAPHORES = ["v", "a", "t", "p", "loc"] + ["%s%d" % (k, s) for s in range(S) for k in RECV] + DMAS
@@ -71,7 +73,7 @@ CYCLE, PE, GATHER, SCATTER, WAKE, LOAD, HOP, FIRST, LOCAL, LINK = [np.array(c) f
     (0.83, 1.16), (0.45, 0.63), (1.56, 1.9), (3.8, 5.0), (180.0, 200.0), (1600.0, 2000.0), (1600.0, 2200.0), (1500.0, 2000.0),
     (300.0, 200.0), (60.0, 45.0))]
 WEIGHT = (1.0, 0.73)
-TRIES = 30000
+TRIES = 40000
 PLAN = {}
 
 
@@ -395,13 +397,11 @@ def rank_program(g, core, T, topo):
         mm(V("pP1", 0, 128), V("ID", 0, 128), V("OW%d" % s, 8, 136), True, False)
         mm(V("pU2", 0, 128), V("ID", 0, 128), names, True, False)
 
-    def ways(date, a1, b1, a2, b2):
-        line(V("r12", 0, 128), date, a1, b1, ACT.Relu)
-        line(V("r12", 128, 256), date, a2, b2, ACT.Relu)
-        mm(V("pP1", 0, 128), V("NIb", 0, 128), V("r12", 0, 128), False, True)
+    def ways():
+        mm(V("pP1", 0, 128), V("N8k", 0, 128), V("nm", 0, 128), False, True)
         cp(V("OM", 0, 128), V("pP1", 0, 128))
-        mm(V("pU2", 0, 128), V("NIb", 0, 128), V("r12", 128, 256), False, True)
-        act(V("NM", 0, 128), V("pU2", 0, 128), ACT.Relu)
+        mm(V("pU2", 0, 128), V("I8k", 0, 128), V("nm", 0, 128), False, True)
+        line(V("NM", 0, 128), V("pU2", 0, 128), 1.0, -CUT, ACT.Relu)
 
     def write(win, t, data, base=0):
         cp(IND(win, V("FS", 264 * t, 264 * t + 4) if DIRECT else V("fu", 4 * t, 4 * t + 4)), V(data, base, base + 64))
@@ -430,10 +430,11 @@ def rank_program(g, core, T, topo):
     ts(V("OW0", 8, 136), V("oli", 0, 128), B0, ALU.add)
     cp(V("ZT0", 0, 128), V("tli", 0, 128))
     ts(V("NS0", 0, 128), V("nli", 0, 128), B0, ALU.add)
-    for k, c in (("NIb", -1.0), ("NID", -1.0), ("IDb", 1.0), ("N200", -200.0), ("N2", -2.0), ("I8k", 8192.0), ("N4k", -4096.0)):
+    for k, c in (("N8k", -CUT), ("I8k", CUT), ("NID", -1.0), ("IDb", 1.0), ("N200", -200.0), ("N2", -2.0), ("N4k", -4096.0)):
         line(V(k, 0, 128), V("ID", 0, 128), c, 0.0)
     ways_open(0, V("NS0", 0, 128))
-    ways(V("ZT0", 0, 128), -CUT, CUT, CUT, 0.0)
+    ts(V("nm", 0, 128), V("tli", 0, 128), 0.0, ALU.is_le)
+    ways()
     cp(V("Z1", 15, 143, 16), V("GM", 0, 128, 16))
     tile("ZT0", "vvv"[:len(TILEB)])
     fill(V("OQ", 0, 256, 2), 0.0)
@@ -443,29 +444,31 @@ def rank_program(g, core, T, topo):
     fill(ALL("mid"), -2048.0)
     iota(V("pidx", 0, 1), [[0, 1]], 0, 1)
     iota(V("mod16", 0, 64), [[0, 4], [1, 16]], 0, 0)
-    iota(V("colc", 0, 128), [[1, 128]], 0, 0)
-    iota(V("L8", 0, 4), [[2, 4]], 264, 0)
+    iota(V("colc", 0, 128), [[1, 128]], 8, 0)
     select(V("G01", 0, 128), V("GM", 0, 128), [[0, 8], [-1, 16]], ALU.is_ge, 1, 0)
     select(ALL("GE1"), (T["ones"][0:8, 0:128], [("ones", 0, 128, 1)], 128), [[1, 128]], ALU.is_ge, 0, -16)
     select(ALL("GE"), ALL("GE1"), [[-1, 128]], ALU.is_ge, 15, 16)
     ts(V("p16i", 0, 1), V("pidx", 0, 1), 15, ALU.bitwise_and)
     cp(ALL("thf"), ALL("thi"))
     cp(V("p16", 0, 1), V("p16i", 0, 1))
-    fill(V("UP", 0, 32), 4.0)
-    fill(V("DN", 0, 32), -4.0)
+    fill(V("AGE", 0, 144), -4.0)
+    fill(V("AGE", 32, 144, 36), ROUND)
+    fill(V("AGE", 33, 144, 36), -ROUND)
+    iota(V("AGE", 34, 144, 36), [[2, 4]], 140, 0)
+    fill(V(KD, K0 - 12, K0), -4 * ROUND)
+    fill(V(KD, K0 + 128, K0 + 136), 4 * ROUND)
     fill(V("HW", 0, 8), 0.0)
-    ts(V("ZK", 0, 144), V("Z1", 0, 144), -256.0, ALU.mult)
+    ts(V("ZK", 0, 144), V("Z1", 0, 144), -512.0, ALU.mult)
     ts(V("DM", 0, 64), V("mod16", 0, 64), V("p16", 0, 1), ALU.is_equal)
-    ts(V("ND", 0, 64), V("mod16", 0, 64), V("p16", 0, 1), ALU.not_equal)
     line(V("p16m", 0, 1), V("p16", 0, 1), 1.0, -128.0)
     ts(V("q1", 0, 1), V("p16", 0, 1), 1.0, ALU.is_equal)
     fill(V("GX", 0, 528), 0.0)
-    fill(V("NE", 0, 528, 66), 1.0)
+    fill(V("NE", 0, 528, 66), CUT)
     iota(V("dump", 0, 8), [[0, 2], [16, 4]], 16, 0)
     ts(V("GX", 0, 528, 66), V("dump", 0, 8), V("p16", 0, 1), ALU.add)
     act(V("GMb", 0, 128), V("GM", 0, 128))
     mm(V("pM", 128, 133), ALL("GE"), ALL("thf"))
-    line(V("LM", 0, 5), V("pM", 128, 133), -256.0, 132.0)
+    line(V("LM", 0, 5), V("pM", 128, 133), -512.0, 132.0)
 
     for s in range(S):
         last = s == S - 1
@@ -473,8 +476,7 @@ def rank_program(g, core, T, topo):
         zt, zc, nr, hr, zt1, ow1 = "ZT%d" % s, "ZC%d" % s, "NR%d" % s, "HR%d" % s, "ZT%d" % (s + 1), "OW%d" % (s + 1)
         date, lim = V(zc, 0, 128), V("LM", s, s + 1)
         send(ow1, "OW%d" % s, 0, 136, "rO%d" % s)
-        send(zc, zt, 0, 192, "rZ%d" % s)
-        send(nr, "NS%d" % s, 0, 128, "rN%d" % s)
+        send(zc, zt, 128, 192, "rZ%d" % s)
         tile(zc, TILEC)
         for (e, a, b) in PGATHER:
             copy[e](V("PG", 16 * a, 16 * b), IND(PA, V("OM", a, b)))
@@ -483,8 +485,13 @@ def rank_program(g, core, T, topo):
             cp(V("RU", a, b), V(PB[q], 0, b - a))
         for (a, b) in UGATHER:
             distance("DF", "AB", a, b, "RU", zt)
-        for q in range(len(HPIECES)):
-            h_of(q, s)
+        for q in range(len(HPIECES) + 1):
+            if q == TSEND:
+                send(zc, zt, 0, 128, "rT%d" % s)
+            if q == NSEND:
+                send(nr, "NS%d" % s, 0, 128, "rN%d" % s)
+            if q < len(HPIECES):
+                h_of(q, s)
         if last:
             dma("s", "o_lo", V("LO", 0, 256), ROW("PW", 0), 65536)
             dma("s", "o_hi", V("LO", 256, 512), ROW("PW", 1), 65536)
@@ -494,10 +501,9 @@ def rank_program(g, core, T, topo):
         line(V("e1", 0, 128), date, 1.0, -(s + 99) / 2.0, ACT.Abs)
         line(V("e2", 0, 128), V("e1", 0, 128), -BIG, BIG * (99 - s) / 2.0, ACT.Relu)
         line(V("RT", 0, 128), V("e2", 0, 128), 1.0, lim)
-        if DATES == "v":
-            line(V("pP0", 0, 128), date, -1.0, float(s + 2))
-        elif not last:
-            line(V("nmx", 0, 128), date, -1.0, float(s + 2), ACT.Relu)
+        if not last:
+            line(V("nmy", 0, 128), date, 1.0, -float(s + 1), ACT.Relu)
+            line(V("nmx", 0, 128), V("nmy", 0, 128), -1.0, 1.0, ACT.Relu)
         if DSHARE:
             mm(V("pM", 0, 256), V("IDb", 0, 128), V(zc, 128, 384))
         for (a, b) in DGATHER:
@@ -508,60 +514,58 @@ def rank_program(g, core, T, topo):
             else:
                 distance("DG", "AC", a, b, hr, zc)
         for (a, b) in DSUMS:
-            reduce16("AC", a, b, "ZK", V(KD, a, b), (ALL("oneb"), V("beta", a, b)))
+            reduce16("AC", a, b, "ZK", V(KD, K0 + a, K0 + b), (ALL("oneb"), V("beta", a, b)))
+            if a == 0:
+                mm(V(KD, 448, 512), V("IDb", 0, 128), V(zc, 128, 192))
         if not last:
             ways_open(s + 1, V(nr, 0, 128))
         cp(V("HW", 8, 136), V(hr, 0, 128))
         mms(V("pU0", 0, 128), [(V("NID", 0, 128), V(nr, 0, 128)), (V("ID", 0, 128), V("HW", 8, 136))], True, NAMES == "v")
         for L in range(4):
-            scan(V("SM", 32 * L, 32 * L + 32), V("DN", 0, 32), V(KD, L, 128, 4), lim, ALU.add, ALU.min)
+            scan(V("SM", 36 * L, 36 * L + 34), V("AGE", 0, 34), V(KD, K0 + L, K0 + L + 136, 4), lim, ALU.add, ALU.min)
         for L in range(4):
-            scan(V("SM", 128 + 32 * L, 160 + 32 * L), V("UP", 0, 32), V(KD, L, 128, 4), -BIG, ALU.add, ALU.max)
-        tt(V("red", 0, 128), V(KD, 0, 128), V("RT", 0, 128), ALU.is_ge)
-        tt(V("KI", 0, 4), V("L8", 0, 4), V("SM", 159, 256, 32), ALU.subtract)
-        ts(V("CI", 0, 4), V("SM", 31, 128, 32), 255, ALU.bitwise_and)
-        ts(V("CI", 4, 8), V("KI", 0, 4), 255, ALU.bitwise_and)
-        cp(V("OFF", 0, 4), V("CI", 0, 4))
-        cp(V("OFF", 4, 8), V("CI", 4, 8))
-        ts(V("NC", 0, 4), V("CI", 0, 4), -1.0, ALU.mult, 8.0, ALU.add)
+            scan(V("SM", 144 + 36 * L, 179 + 36 * L), V("AGE", 36 * L, 36 * L + 35), BACK(KD, K0 + L - 12, K0 + L + 128, 4),
+                 -BIG, ALU.add, ALU.max)
+        tt(V("red", 0, 128), V(KD, K0, K0 + 128), V("RT", 0, 128), ALU.is_ge)
+        tt(V("OFF", 0, 4), V("SM", 31, 144, 36), V("SM", 33, 144, 36), ALU.subtract)
+        tt(V("OFF", 4, 8), V("SM", 178, 288, 36), V("SM", 175, 288, 36), ALU.subtract)
+        tt(V("NC", 0, 4), V("SM", 33, 144, 36), V("SM", 31, 144, 36), ALU.subtract)
         for L in range(4):
             line(V("rf", L, 128, 4), V("colc", L, 128, 4), 1.0, V("NC", L, L + 1), ACT.Abs)
+        if not last:
+            mms(V("pR", 128, 256), [(V("IDb", 0, 128), V("nmx", 0, 128)), (V("N2", 0, 128), V("red", 0, 128))])
+            act(V("pS", 0, 128), V("pR", 128, 256), ACT.Relu)
+            tt(V("nm", 0, 128), V("pS", 0, 128), V("rf", 0, 128), ALU.min)
+            ways()
         line(V("RF", 0, 128), V("rf", 0, 128), -99.0, 99.0, ACT.Relu)
-        dates = V("YT", 0, 128) if last else V(zt1, 0, 128)
-        if DATES == "v":
-            tt(V("pS", 0, 128), V("pP0", 0, 128), V("red", 0, 128), ALU.mult)
-            tt(V("pS", 256, 384), V("pS", 0, 128), date, ALU.add)
-            tt(dates, V("pS", 256, 384), V("RF", 0, 128), ALU.max)
-            if not last:
-                ways(V(zt1, 0, 128), -CUT, CUT * (s + 2), CUT, -CUT * (s + 1))
-        else:
-            gone = [(V("N200", 0, 128), V("red", 0, 128)), (V("N2", 0, 128), V("RF", 0, 128))]
-            if not last:
-                mms(V("pS", 0, 128), [(V("IDb", 0, 128), V("nmx", 0, 128))] + gone[:1], True, False)
-                mms(V("pS", 0, 128), gone[1:], False, True)
-                ways(V("pS", 0, 128), CUT, 0.0, -CUT, CUT)
-            mms(V("pS", 128, 256), [(V("IDb", 0, 128), date)] + gone)
-            act(V("Tz", 0, 128), V("pS", 128, 256), ACT.Relu)
-            line(V("Tq", 0, 128), V("red", 0, 128), float(s + 2), 0.0)
-            mms(V("pS", 256, 384), [(V("IDb", 0, 128), V(k, 0, 128)) for k in ("Tq", "RF", "Tz")])
-            act(dates, V("pS", 256, 384))
+        mms(V("pS", 128, 256), [(V("IDb", 0, 128), date), (V("N200", 0, 128), V("red", 0, 128)), (V("N2", 0, 128), V("RF", 0, 128))])
+        act(V("Tz", 0, 128), V("pS", 128, 256), ACT.Relu)
+        line(V("Tq", 0, 128), V("red", 0, 128), float(s + 2), 0.0)
+        mms(V("pS", 256, 384), [(V("IDb", 0, 128), V(k, 0, 128)) for k in ("Tq", "RF", "Tz")])
+        act(V("YT", 0, 128) if last else V(zt1, 0, 128), V("pS", 256, 384))
         for t, (window, bank) in enumerate(((ow1, "pM"), ("HW", "pP0"))):
             a, b = 64 * t, 64 * t + 64
             tt(V("GD", a, b), IND(V(window, 0, 136), V("OFF", 4 * t, 4 * t + 4)), V("DM", 0, 64), ALU.mult)
             mm(V(bank, 128, 192), V("GM", 0, 128), V("GD", a, b))
-            scan(BACK("OWN", a, b), BACK("ND", 0, 64), BACK("GD", a, b), 0.0, ALU.mult, ALU.add)
             for L in range(4):
-                c, w = 264 * t + 66 * L, 16 * L + 17
-                copy[SPREAD[t]](V("GX", c + w - 16, c + w), V("GD", a + 16 * L, a + 16 * L + 16))
-                ts(V("NE", c + 1, c + w), V(bank, 128, 127 + w), V("OWN", a + 16 * L, a + 16 * L + 1), ALU.not_equal)
-                scan(BACK("FS", 264 * t + L, 264 * t + L + 4 * w, 4), BACK("NE", c, c + w), BACK("GX", c, c + w), 0.0, ALU.mult, ALU.max)
+                c, w, own = 264 * t + 66 * L, 16 * L + 17, V("OWN", 4 * t + L, 4 * t + L + 1)
+                line(V("GX", c + w - 16, c + w), V("GD", a + 16 * L, a + 16 * L + 16), 1.0, 0.0, ACT.Identity, own)
+            if SPREAD[t] == "a":
+                line(V("OWN", 8, 12), V("OWN", 4 * t, 4 * t + 4), CUT, 0.0)
+            for L in range(4):
+                c, w, own = 264 * t + 66 * L, 16 * L + 17, V("OWN", 4 * t + L, 4 * t + L + 1)
+                if SPREAD[t] == "a":
+                    line(V("NE", c + 1, c + w), V(bank, 128, 127 + w), -CUT, V("OWN", 8 + L, 9 + L), ACT.Abs)
+                else:
+                    ts(V("NE", c + 1, c + w), V(bank, 128, 127 + w), own, ALU.not_equal, CUT, ALU.mult)
+                scan(BACK("FS", 264 * t + L, 264 * t + L + 4 * w, 4), BACK("NE", c, c + w), BACK("GX", c, c + w), 0.0, ALU.min, ALU.max)
             if not DIRECT:
                 cp(V("fu", 4 * t, 4 * t + 4), V("FS", 264 * t, 264 * t + 4))
         tt(V("GD", 128, 192), IND(V("HW", 0, 136), V("OFF", 0, 4)), V("DM", 0, 64), ALU.mult)
         mm(V("pR", 0, 64), V("G01", 0, 128), V("GD", 128, 192))
-        ts(V("HB", 0, 4), V("CI", 4, 8), 16.0, ALU.mult, V("p16m", 0, 1), ALU.add)
+        ts(V("HB", 0, 4), V("OFF", 4, 8), 16.0, ALU.mult, V("p16m", 0, 1), ALU.add)
         ts(V("zi", 0, 64), IND(V("DG", 0, 2048), V("HB", 0, 4)), 0.5, ALU.mult, -0.25, ALU.add)
-        tt(V(zt1, 128, 192), V("zi", 0, 64), V(zc, 128, 192), ALU.add)
+        tt(V(zt1, 128, 192), V("zi", 0, 64), V(KD, 448, 512), ALU.add)
         if not last:
             line(V("hx", 0, 64), V("pR", 0, 64), V("q1", 0, 1), 0.0)
             tt(V("PD", 0, 64), V("pR", 0, 64), V("hx", 0, 64), ALU.subtract)
@@ -587,9 +591,9 @@ def rank_program(g, core, T, topo):
                 ts(V("YN", 0, 128), V("NS%d" % (s + 1), 0, 128), -float(B0), ALU.add)
             line(V("ht", 0, 64), V("pR", 0, 64), 1.0, -float(B0))
             write(V("PF", 0, WW), 0, "ht")
+            dma("s", "o_n", ALL("yn"), V("YN", 0, 128), 65536)
             dma("a", "o_z", ALL("yz"), V(zt1, 128, 192), 16384)
-            dma("s", "o_x", ALL("yx"), V("XW", B0, WW), 1048576)
             dma("a", "o_t", ALL("yt"), V("YT", 0, 128), 65536)
-            dma("a", "o_n", ALL("yn"), V("YN", 0, 128), 65536)
+            dma("s", "o_x", ALL("yx"), V("XW", B0, WW), 1048576)
             dma("a", "o_p", ALL("yp"), ROW("PF", 0), 131072)
     issue()

import math
import numpy as np
from concourse.mybir import AluOpType as ALU, ActivationFunctionType as ACT

S, B0, WW, TW = 5, 96, 4192, 512
DIRECT = True
SPREAD = "va"
BIG, CUT, ROUND, K0 = 4194304.0, 8192.0, 6442450944.0, 272
DATES = "t"
NAMES = "t"


def _sb(n, dtype="float32", p=128):
    return ("sbuf", [p, n], dtype)


SCRATCH = {
    "XW": _sb(WW, "bfloat16"), "PW": _sb(WW, "bfloat16"), "PF": _sb(WW),
    "DF": _sb(2048, "bfloat16"), "AB": _sb(2048, "bfloat16"), "PG": _sb(2048, "bfloat16"),
    "DG": _sb(2048, "bfloat16"), "AC": _sb(2048, "bfloat16"),
    "pxi": _sb(256, "int32"), "pxt": _sb(256, "int32"), "LH": _sb(512, "bfloat16"),
    "oli": _sb(128, "int32"), "nli": _sb(128, "int32"), "tli": _sb(128, "int32"),
    "thi": _sb(5, "int32", 8), "thf": _sb(5, "float32", 8), "GE1": _sb(128, "float32", 8), "GE": _sb(128, "float32", 8),
    "Z1": _sb(144, "bfloat16"), "ZK": _sb(144, "bfloat16"), "ones": _sb(128),
    "oneb": _sb(128, "bfloat16", 1), "mid": _sb(128, "bfloat16", 1), "beta": _sb(128, "bfloat16", 1),
    "G1": _sb(128), "GM": _sb(128), "GMb": _sb(128, "bfloat16"), "G01": _sb(128), "ID": _sb(128), "NID": _sb(128),
    "N8k": _sb(128, "bfloat16"), "IDb": _sb(128, "bfloat16"), "N200": _sb(128, "bfloat16"), "N2": _sb(128, "bfloat16"),
    "I8k": _sb(128, "bfloat16"), "N4k": _sb(128, "bfloat16"),
    "mod16": _sb(64), "colc": _sb(128), "DM": _sb(64), "AGE": _sb(144),
    "pidx": _sb(1, "int32"), "p16i": _sb(1, "int32"), "p16": _sb(1), "p16m": _sb(1), "q1": _sb(1), "dump": _sb(8), "LM": _sb(5),
    "HW": _sb(136), "A32": _sb(1), "junk": _sb(128), "OQ": _sb(256), "hv": _sb(256, "int32"), "hs": _sb(128, "int32"),
    "OM": _sb(128, "uint16"), "NM": _sb(128), "RU": _sb(128, "uint16"), "nm": _sb(128, "bfloat16"),
    "e1": _sb(128), "e2": _sb(128), "RT": _sb(128), "red": _sb(128, "bfloat16"), "SM": _sb(288),
    "nmx": _sb(128, "bfloat16"), "nmy": _sb(128, "bfloat16"), "Tz": _sb(128, "bfloat16"), "Tq": _sb(128, "bfloat16"), "Nw": _sb(128),
    "NC": _sb(4), "OFF": _sb(8, "uint16"),
    "GD": _sb(192), "OWN": _sb(12), "GX": _sb(528), "NE": _sb(528), "FS": _sb(528, "uint16" if DIRECT else "float32"),
    "fu": _sb(8, "uint16"),
    "HB": _sb(4, "uint16"), "zi": _sb(64, "int32"),
    "hx": _sb(64, "bfloat16"), "ht": _sb(64), "PD": _sb(64, "bfloat16"), "rf": _sb(128), "RF": _sb(128, "bfloat16"),
    "YN": _sb(128), "YT": _sb(128), "YPg": _sb(256), "LO": _sb(512, "bfloat16"),
    "ZC": _sb((128 + TW) * S, "bfloat16"),
    "NR": _sb(128 * S),
    "HS": _sb(128 * S, "uint16"),
    "HR": _sb(128 * S, "uint16"),
    "OW": _sb(136 * (S + 1)),
    "ZT": _sb((128 + TW) * (S + 1), "bfloat16"),
    "NS": _sb(128 * (S + 1)),
}
for _n in ("pU0", "pU1", "pU2", "pP0", "pP1", "pR", "pM", "pS"):
    SCRATCH[_n] = ("psum", [128, 512], "float32")
PIECE = {"%s%d" % (k, s): (k, SCRATCH[k][1][1] // n * s) for k, n in
         (("ZC", S), ("NR", S), ("HS", S), ("HR", S), ("OW", S + 1), ("ZT", S + 1), ("NS", S + 1)) for s in range(n)}
PGATHER = (("a", 0, 16), ("v", 16, 32), ("a", 32, 48), ("v", 48, 64), ("a", 64, 80), ("a", 80, 96), ("a", 96, 112), ("a", 112, 128))
ROADS = ((0, 32), (32, 64), (64, 96), (96, 128))
UGATHER = ((0, 16), (16, 32), (32, 48), (48, 64), (64, 80), (80, 96), (96, 112), (112, 128))
HPIECES = ((0, 32), (32, 64), (64, 96), (96, 112), (112, 128))
DGATHER = ((0, 32), (32, 48), (48, 64), (64, 80), (80, 96), (96, 112), (112, 128))
DSHARE = (48, 80)
DSUMS = ((0, 64), (64, 128))
TILEB = "aa"
TILEC = "ppp"
TSEND = 0
NSEND = 5
RECV = ("rO", "rZ", "rT", "rN") + tuple("rH%d_" % i for i in range(len(HPIECES)))
DMAS = ["d_px", "d_ol", "d_z", "d_tl", "d_nl", "d_th", "d_x", "d_x2", "d_lo", "d_hi",
        "o_x", "o_lo", "o_hi", "o_pf", "o_p", "o_z", "o_n", "o_t"]
SEMAPHORES = ["v", "a", "t", "p", "loc"] + ["%s%d" % (k, s) for s in range(S) for k in RECV] + DMAS
UB = ("pU0", "pU1", "pU2", "pU0", "pU1", "pU2")
PB = ("pP0", "pP1", "pP0", "pP1")
KD = "pU1"
A0 = 65536.0 - 8388608.0 - 3232.0 * B0
CYCLE, PE, GATHER, SCATTER, WAKE, LOAD, HOP, FIRST, LOCAL, LINK = [np.array(c) for c in (
    (0.83, 1.16), (0.45, 0.63), (1.56, 1.9), (3.8, 5.0), (180.0, 200.0), (1600.0, 2000.0), (1600.0, 2200.0), (1500.0, 2000.0),
    (300.0, 200.0), (60.0, 45.0))]
WEIGHT = (1.0, 0.73)
TRIES = 40000
PLAN = {}


def arrange(nodes, marks):
    n, last, seed = len(nodes), len(marks) - 1, [12345]
    on, busy0, busy1 = [nd["q"] for nd in nodes], [float(nd["busy"][0]) for nd in nodes], [float(nd["busy"][1]) for nd in nodes]
    step = [max(i for i in range(last + 1) if marks[i] <= k) for k in range(n)]
    pre, post, later, older = [], [[] for _ in nodes], [[] for _ in nodes], []
    for k, nd in enumerate(nodes):
        gaps = {j: (nd["gap"] if on[k] in "ld" else WAKE) if hard else WAKE * 0 for j, hard in nd["before"].items()}
        pre.append([(j, float(gap[0]), float(gap[1])) for j, gap in gaps.items()
                    if not any(older[m] >> j & 1 and other[0] >= gap[0] for m, other in gaps.items())])
        older.append(0)
        for j, gap, _ in pre[k]:
            older[k] |= older[j] | 1 << j
            post[j].append(k)
            later[j].append((k, gap, 0.0))

    def draw(m):
        seed[0] = (seed[0] * 1103515245 + 12345) % 2147483648
        return (seed[0] >> 8) % m

    def landings(order):
        order["l"] = [k + 1 for k in order["p"] if nodes[k]["signal"]]
        order["d"] = [k for k in range(n) if on[k] == "d"]
        return order

    def path(order):
        prev, nxt, miss = [n] * n, [-1] * n, [len(p) for p in pre]
        for q in order.values():
            for a, b in zip(q, q[1:]):
                prev[b], nxt[a] = a, b
                miss[b] += 1
        end0, end1, why0, why1 = [0.0] * (n + 1), [0.0] * (n + 1), [n] * n, [n] * n
        todo, done = [k for k in range(n) if not miss[k]], 0
        while todo:
            k = todo.pop()
            done += 1
            w0 = w1 = prev[k]
            t0, t1 = end0[w0], end1[w1]
            for j, gap0, gap1 in pre[k]:
                if end0[j] + gap0 >= t0:
                    t0, w0 = end0[j] + gap0, j
                if end1[j] + gap1 >= t1:
                    t1, w1 = end1[j] + gap1, j
            end0[k], end1[k], why0[k], why1[k] = t0 + busy0[k], t1 + busy1[k], w0, w1
            for j in post[k]:
                miss[j] -= 1
                if not miss[j]:
                    todo.append(j)
            j = nxt[k]
            if j >= 0:
                miss[j] -= 1
                if not miss[j]:
                    todo.append(j)
        if done < n:
            return None
        arcs = []
        for end, why in ((end0, why0), (end1, why1)):
            k = end.index(max(end))
            while why[k] < n:
                if why[k] == prev[k] and why[k] not in nodes[k]["before"] and on[k] != "d":
                    arcs.append((why[k], k))
                k = why[k]
        return sum(w * (max(end) + 0.05 * sum(end) / n) for w, end in zip(WEIGHT, (end0, end1))) / 2, arcs, end0, (max(end0), max(end1))

    def pack(links, urgency):
        order, end = {q: [] for q in "vatpsld"}, [0.0] * n
        for k in sorted(range(n), key=lambda j: -urgency[j]):
            at, taken = max([0.0] + [end[j] + gap for j, gap, _ in links[k]]), order[on[k]]
            i = len(taken)
            while i and end[taken[i - 1]] > at:
                i -= 1
            while i < len(taken) and end[taken[i]] - busy0[taken[i]] < at + busy0[k]:
                at = max(at, end[taken[i]])
                i += 1
            taken.insert(i, k)
            end[k] = at + busy0[k]
        return landings(order), end

    ahead = [0.0] * n
    for k in range(n - 1, -1, -1):
        ahead[k] = busy0[k] + max([0.0] + [ahead[j] + gap for j, gap, _ in later[k]])
    order = pack(pre, ahead)[0]
    now = path(order)
    best = (now[0], order, now[3])
    for it in range(TRIES):
        if it % 500 == 0:
            for urgency in ([busy0[k] - now[2][k] for k in range(n)], pack(later, now[2])[1]):
                other = pack(pre, urgency)[0]
                new = path(other)
                if new is not None and new[0] < now[0]:
                    order, now = other, new
        forward = draw(2)
        if draw(4) and now[1]:
            a, b = now[1][draw(len(now[1]))]
            a, b = (a - 1, b - 1) if on[a] == "l" else (a, b)
            q = order[on[a]]
            i = q.index(a)
            a, b = (q[max(0, i - (0, 0, 1, 2, 3)[draw(5)])], b) if forward else (a, q[min(len(q) - 1, q.index(b) + draw(4))])
        else:
            q = order["vvvaatp"[draw(7)]]
            i = draw(len(q) - 1)
            a, b = q[i], q[min(len(q) - 1, i + (1, 1, 2, 3)[draw(4)])]
        q = list(q)
        for d in range(-last, last + 1):
            if d == 0 or all(0 < s < last for s in (step[a], step[b], step[a] + d, step[b] + d)):
                i, j = q.index(a + marks[step[a] + d] - marks[step[a]]), q.index(b + marks[step[b] + d] - marks[step[b]])
                if i < j and forward:
                    q.insert(i, q.pop(j))
                elif i < j:
                    q.insert(j, q.pop(i))
        other = dict(order)
        other[on[a]] = q
        new = path(landings(other))
        if new is not None and new[0] - now[0] <= -math.log((draw(4096) + 1) / 4097.0) * 35.0 * (1.0 - it / TRIES) ** 2:
            order, now = other, new
            if now[0] < best[0]:
                best = (now[0], order, now[3])
    PLAN["spans"] = best[2]
    return best[1]


def rank_program(g, core, T, topo):
    rank = T.rank_of(core)
    if rank is None:
        return
    nxt = T.cores[(rank + 1) % len(T.cores)]
    prv = T.cores[(rank - 1) % len(T.cores)]
    queues = {"v": g.vector, "a": g.scalar, "t": g.tensor, "p": g, "s": g.sync}
    psum = set(n for n in SCRATCH if SCRATCH[n][0] == "psum")
    nodes, acc, marks, sends = [], {}, [0], []

    def node(q, calls, rd, wr, busy, signal=None, beside=None, landing=None):
        before = {}
        for views, write in ((rd, False), (wr, True)):
            for (n, lo, hi, st) in [r for v in views for r in v[1]]:
                for (k, alo, ahi, ast, aw) in acc.get(n, ()):
                    same = nodes[k]["q"] == q and (signal is None or n[:4] == "turn")
                    apart = ahi <= lo or alo >= hi or (st == ast and (lo - alo) % st)
                    if k == beside or (not (n in psum and (not same or q == "t")) and (apart or not (aw or write))):
                        continue
                    before[k] = before.get(k, False) or not (same and write and (q == "t" or n[:4] == "turn" or not aw))
        nodes.append({"q": q, "calls": calls, "before": before, "busy": busy + 0 * WAKE, "signal": signal})
        first = len(nodes) - 1
        if landing is not None:
            nodes.append({"q": landing[0], "calls": [], "before": {first: True}, "gap": landing[1], "busy": landing[2], "signal": signal})
        me = len(nodes) - 1
        for views, write in ((rd, False), (wr, True)):
            for (n, lo, hi, st) in [r for v in views for r in v[1]]:
                old = acc.get(n, [])
                if write and st == 1 and n not in psum and beside is None:
                    old = [a for a in old if not (lo <= a[1] and a[2] <= hi)]
                acc[n] = old + [(first if n[:4] == "turn" else me, lo, hi, st, write)]
        return me

    def turn(word):
        return (None, [("turn" + word, 0, 1, 1)])

    def width(name):
        return 2 if SCRATCH[name][2] in ("bfloat16", "uint16") else 4

    def cost(o, ins, both=False):
        if len(ins[0]) > 3:
            return 50 + GATHER * CYCLE * ins[0][2]
        if len(o) > 3:
            return 50 + SCATTER * CYCLE * o[2]
        if both:
            return CYCLE * max(64, ins[0][2] * (1 if any(v[1][0][0] in psum for v in ins) else 2))
        return CYCLE * max(64, ins[0][2] * (0.5 if all(width(v[1][0][0]) == 2 for v in [o] + ins) else 1))

    def dma(q, sem, out, in_, size, beside=None, behind=()):
        return node(q, [lambda: queues[q].dma_start(out=out[0], in_=in_[0])], [in_] + list(behind), [out, turn("d" + q)], 50,
                    (sem, 16), beside, ("d", LOAD, size / LOCAL + 80))

    def send(dst_name, src_name, lo, hi, sem):
        src, dst = V(src_name, lo, hi), V(dst_name, lo, hi)
        rid, pid, _ = topo.addr(nxt)
        node("p", [lambda: g.remote_dma(out_ap=dst[0], in_ap=src[0], remote_sem=T.sem[sem], local_sem=T.sem["loc"],
                                        pid=pid, routing_id=rid, dma_engine_mask=topo.mask(core, nxt))],
             [src], [dst, turn("send")], 150 + (0 if sends else FIRST),
             (sem, len(topo.engines(prv, core))), None, ("l", HOP - 150, 128 * src[2] * width(src[1][0][0]) / LINK + 160))
        sends.append(sem)

    def issue():
        if "order" not in PLAN:
            PLAN["order"] = arrange(nodes, marks)
        order = PLAN["order"]
        count = {}
        for q in order:
            for k in order[q]:
                if nodes[k]["signal"] is None:
                    count[q] = count.get(q, 0) + 1
                nodes[k]["done"] = nodes[k]["signal"] or (q, count[q])
        for q in queues:
            seen = {}
            for k in order[q]:
                needs = {}
                for j, hard in nodes[k]["before"].items():
                    if hard:
                        sem, val = nodes[j]["done"]
                        needs[sem] = max(needs.get(sem, 0), val)
                for sem in sorted(needs):
                    if seen.get(sem, 0) < needs[sem]:
                        queues[q].wait_ge(T.sem[sem], needs[sem])
                        seen[sem] = needs[sem]
                made = [call() for call in nodes[k]["calls"]]
                if nodes[k]["signal"] is None:
                    made[-1].then_inc(T.sem[q], 1)
                elif q != "p":
                    made[-1].then_inc(T.sem[nodes[k]["signal"][0]], 16)
        for q in count:
            g.wait_ge(T.sem[q], count[q])
        g.wait_ge(T.sem["loc"], len(topo.engines(core, nxt)) * len(sends))
        for k in order["l"] + order["d"]:
            g.wait_ge(T.sem[nodes[k]["signal"][0]], nodes[k]["signal"][1])

    def V(name, lo, hi, st=1):
        if name in PIECE:
            name, base = PIECE[name]
            lo, hi = lo + base, hi + base
        return (T[name][:, lo:hi] if st == 1 else T[name][:, lo:hi:st], [(name, lo, hi, st)], len(range(lo, hi, st)))

    def BACK(name, lo, hi, st=1):
        return (T[name][:, hi - st::-st] if lo < st else T[name][:, hi - st:lo - 1:-st], [(name, lo, hi, st)], (hi - lo) // st)

    def ALL(name):
        n = SCRATCH[name][1][1] if name in SCRATCH else 1
        return (T[name][:], [(name, 0, n, 1)], n)

    def ROW(name, first):
        return (T[name][first:128:16, B0:WW], [(name, B0, WW, 1)], WW - B0)

    def IND(win, off):
        return (win[0].indirect(off[0]), win[1] + off[1], 16 * off[2], off)

    def cols(*vs):
        return [v for v in vs if not isinstance(v, (int, float)) and v is not None]

    def raw(v):
        return v if isinstance(v, (int, float)) or v is None else v[0]

    def op(q, call, rd, wr, busy):
        long = [turn(q)] if rd and len(rd[0]) > 3 and rd[0][2] >= 128 else []
        node(q, [call], rd + [o[3] for o in wr if len(o) > 3], [(o[0], o[1][:1]) for o in wr] + long, busy)

    def tt(o, a, b, f):
        op("v", lambda: g.vector.tensor_tensor(out=o[0], in0=a[0], in1=b[0], op=f), [a, b], [o], cost(o, [a, b], True))

    def ts(o, a, s1, f1, s2=None, f2=None):
        if f2 is None:
            op("v", lambda: g.vector.tensor_scalar(out=o[0], in0=a[0], scalar1=raw(s1), scalar2=None, op0=f1), [a] + cols(s1), [o],
               cost(o, [a]))
        else:
            op("v", lambda: g.vector.tensor_scalar(out=o[0], in0=a[0], scalar1=raw(s1), scalar2=raw(s2), op0=f1, op1=f2),
               [a] + cols(s1, s2), [o], cost(o, [a]))

    def cp(o, a):
        op("v", lambda: g.vector.tensor_copy(out=o[0], in_=a[0]), [a], [o], cost(o, [a]))

    def scan(o, d0, d1, first, f0, f1):
        op("v", lambda: g.vector.tensor_tensor_scan(out=o[0], data0=d0[0], data1=d1[0], initial=raw(first), op0=f0, op1=f1),
           [d0, d1] + cols(first), [o], cost(o, [d0, d1]))

    def fill(o, c):
        op("v", lambda: g.vector.memset(o[0], c), [], [o], cost(o, [o]))

    def act(o, a, f=ACT.Copy):
        op("a", lambda: g.scalar.activation(out=o[0], in_=a[0], func=f), [a], [o], 15 + cost(o, [a]) if len(a) > 3 else CYCLE * max(64, a[2]))

    def line(o, a, scale, bias, f=ACT.Identity, total=None):
        op("a", lambda: g.scalar.activation(out=o[0], in_=a[0], func=f, bias=raw(bias), scale=raw(scale), accum_out=raw(total)),
           [a] + cols(bias, scale), [o] + cols(total), CYCLE * max(64, a[2]))

    def mms(o, pairs, start=True, stop=True):
        node("t", [lambda l=l, r=r, i=i: g.tensor.matmul(out=o[0], lhsT=l[0], rhs=r[0], start=start and i == 0,
                                                         stop=stop and i == len(pairs) - 1) for i, (l, r) in enumerate(pairs)],
             [v for p in pairs for v in p], [o], sum(PE * max(64, r[2]) * width(r[1][0][0]) ** 2 / 4 for l, r in pairs))

    def mm(o, l, r, start=True, stop=True):
        mms(o, [(l, r)], start, stop)

    def iota(o, pattern, base, cm):
        op("p", lambda: g.iota(o[0], pattern, base, cm, allow_small_or_imprecise_dtypes=True), [], [o], 130 + 2 * CYCLE * o[2])

    def select(o, a, pattern, f, base, cm):
        op("p", lambda: g.affine_select(o[0], a[0], pattern, f, 0.0, base, cm), [a], [o], 170 + 2 * CYCLE * o[2])

    def pool_copy(o, a):
        select(o, a, [[0, o[2]]], ALU.is_ge, 0, 0)

    XA, PA = V("XW", 0, WW), V("PW", 0, WW)
    copy = {"v": cp, "a": act, "p": pool_copy}

    def tile(name, engines):
        for w, e in zip((64, 128, 256), engines):
            copy[e](V(name, 128 + w, 128 + 2 * w), V(name, 128, 128 + w))

    def reduce16(src, c0, c1, w, out, first):
        mm(out, first[0], first[1], True, False)
        mms(out, [(V(w, 15 - i, 143 - i), V(src, 16 * c0 + i, 16 * c1, 16)) for i in range(16)], False, True)

    def distance(df, ab, a, b, off, tname):
        tt(V(df, 16 * a, 16 * b), IND(XA, V(off, a, b)), V(tname, 128, 128 + 16 * (b - a)), ALU.subtract)
        act(V(ab, 16 * a, 16 * b), V(df, 16 * a, 16 * b), ACT.Abs)

    def h_terms(s, bias):
        line(V("OQ", 1, 256, 2), V("OW%d" % s, 8, 136), 1.0, 32.0 - B0)
        for q, (a, b) in enumerate(HPIECES):
            line(V(UB[q], 2 * a + 1, 2 * b, 2), V("OW%d" % s, 8 + a, 8 + b), 3232.0, bias)

    def h_of(q, s):
        a, b = HPIECES[q]
        reduce16("AB", a, b, "Z1", V(UB[q], 2 * a, 2 * b, 2), (ALL("oneb"), V("mid", 0, b - a)))
        scan(V("hv", 2 * a, 2 * b), V("OQ", 2 * a, 2 * b), V(UB[q], 2 * a, 2 * b), 0.0, ALU.mult, ALU.add)
        ts(V("hs", a, b), V("hv", 2 * a + 1, 2 * b, 2), 5, ALU.arith_shift_right, 4095, ALU.bitwise_and)
        ts(V("HS%d" % s, a, b), V("hs", a, b), float(B0), ALU.add)
        send("HR%d" % s, "HS%d" % s, a, b, "rH%d_%d" % (q, s))

    def ways_open(s, names):
        mm(V("pP1", 0, 128), V("ID", 0, 128), V("OW%d" % s, 8, 136), True, False)
        mm(V("pU2", 0, 128), V("ID", 0, 128), names, True, False)

    def ways():
        mm(V("pP1", 0, 128), V("N8k", 0, 128), V("nm", 0, 128), False, True)
        cp(V("OM", 0, 128), V("pP1", 0, 128))
        mm(V("pU2", 0, 128), V("I8k", 0, 128), V("nm", 0, 128), False, True)
        line(V("NM", 0, 128), V("pU2", 0, 128), 1.0, -CUT, ACT.Relu)

    def write(win, t, data, base=0):
        cp(IND(win, V("FS", 264 * t, 264 * t + 4) if DIRECT else V("fu", 4 * t, 4 * t + 4)), V(data, base, base + 64))

    dma("s", "d_px", V("pxi", 0, 256), ALL("px"), 131072)
    dma("a", "d_ol", V("oli", 0, 128), ALL("ol"), 65536)
    dma("s", "d_tl", V("tli", 0, 128), ALL("tl"), 65536)
    dma("a", "d_nl", V("nli", 0, 128), ALL("nl"), 65536)
    dma("s", "d_z", V("ZT0", 128, 192), ALL("z"), 16384)
    dma("a", "d_th", ALL("thi"), ALL("th"), 160)
    dma("s", "d_x", V("XW", B0, B0 + 2048), (T["x"][:, 0:2048], []), 524288)
    fill(V("ones", 0, 128), 1.0)
    fill(V("PW", 0, WW), 0.0)
    select(V("ID", 0, 128), V("ones", 0, 128), [[1, 128]], ALU.is_equal, 0, -1)
    select(V("G1", 0, 128), V("ones", 0, 128), [[-16, 8], [0, 16]], ALU.is_ge, 0, 1)
    select(V("GM", 0, 128), V("G1", 0, 128), [[16, 8], [0, 16]], ALU.is_ge, 15, -1)
    fill(V("XW", 0, B0), 0.0)
    fill(V("Z1", 0, 144), 0.0)
    fill(V("OW0", 0, 8), 0.0)
    ts(V("LH", 256, 512), V("pxi", 0, 256), B0, ALU.add)
    high = dma("a", "d_hi", ROW("PW", 1), V("LH", 256, 512), 65536)
    ts(V("pxt", 0, 256), V("pxi", 0, 256), B0, ALU.add)
    tt(V("LH", 0, 256), V("pxt", 0, 256), V("LH", 256, 512), ALU.subtract)
    dma("s", "d_lo", ROW("PW", 0), V("LH", 0, 256), 65536, high)
    dma("s", "d_x2", V("XW", B0 + 2048, WW), (T["x"][:, 2048:4096], []), 524288)
    ts(V("OW0", 8, 136), V("oli", 0, 128), B0, ALU.add)
    cp(V("ZT0", 0, 128), V("tli", 0, 128))
    ts(V("NS0", 0, 128), V("nli", 0, 128), B0, ALU.add)
    for k, c in (("N8k", -CUT), ("I8k", CUT), ("NID", -1.0), ("IDb", 1.0), ("N200", -200.0), ("N2", -2.0), ("N4k", -4096.0)):
        line(V(k, 0, 128), V("ID", 0, 128), c, 0.0)
    ways_open(0, V("NS0", 0, 128))
    ts(V("nm", 0, 128), V("tli", 0, 128), 0.0, ALU.is_le)
    ways()
    cp(V("Z1", 15, 143, 16), V("GM", 0, 128, 16))
    tile("ZT0", "vvv"[:len(TILEB)])
    fill(V("OQ", 0, 256, 2), 0.0)
    h_terms(0, A0)
    iota(ALL("beta"), [[0, 32], [1, 4]], 132, 0)
    fill(ALL("oneb"), 1.0)
    fill(ALL("mid"), -2048.0)
    iota(V("pidx", 0, 1), [[0, 1]], 0, 1)
    iota(V("mod16", 0, 64), [[0, 4], [1, 16]], 0, 0)
    iota(V("colc", 0, 128), [[1, 128]], 8, 0)
    select(V("G01", 0, 128), V("GM", 0, 128), [[0, 8], [-1, 16]], ALU.is_ge, 1, 0)
    select(ALL("GE1"), (T["ones"][0:8, 0:128], [("ones", 0, 128, 1)], 128), [[1, 128]], ALU.is_ge, 0, -16)
    select(ALL("GE"), ALL("GE1"), [[-1, 128]], ALU.is_ge, 15, 16)
    ts(V("p16i", 0, 1), V("pidx", 0, 1), 15, ALU.bitwise_and)
    cp(ALL("thf"), ALL("thi"))
    cp(V("p16", 0, 1), V("p16i", 0, 1))
    fill(V("AGE", 0, 144), -4.0)
    fill(V("AGE", 32, 144, 36), ROUND)
    fill(V("AGE", 33, 144, 36), -ROUND)
    iota(V("AGE", 34, 144, 36), [[2, 4]], 140, 0)
    fill(V(KD, K0 - 12, K0), -4 * ROUND)
    fill(V(KD, K0 + 128, K0 + 136), 4 * ROUND)
    fill(V("HW", 0, 8), 0.0)
    ts(V("ZK", 0, 144), V("Z1", 0, 144), -512.0, ALU.mult)
    ts(V("DM", 0, 64), V("mod16", 0, 64), V("p16", 0, 1), ALU.is_equal)
    line(V("p16m", 0, 1), V("p16", 0, 1), 1.0, -128.0)
    ts(V("q1", 0, 1), V("p16", 0, 1), 1.0, ALU.is_equal)
    fill(V("GX", 0, 528), 0.0)
    fill(V("NE", 0, 528, 66), CUT)
    iota(V("dump", 0, 8), [[0, 2], [16, 4]], 16, 0)
    ts(V("GX", 0, 528, 66), V("dump", 0, 8), V("p16", 0, 1), ALU.add)
    act(V("GMb", 0, 128), V("GM", 0, 128))
    mm(V("pM", 128, 133), ALL("GE"), ALL("thf"))
    line(V("LM", 0, 5), V("pM", 128, 133), -512.0, 132.0)

    for s in range(S):
        last = s == S - 1
        marks.append(len(nodes))
        zt, zc, nr, hr, zt1, ow1 = "ZT%d" % s, "ZC%d" % s, "NR%d" % s, "HR%d" % s, "ZT%d" % (s + 1), "OW%d" % (s + 1)
        date, lim = V(zc, 0, 128), V("LM", s, s + 1)
        send(ow1, "OW%d" % s, 0, 136, "rO%d" % s)
        send(zc, zt, 128, 192, "rZ%d" % s)
        tile(zc, TILEC)
        for (e, a, b) in PGATHER:
            copy[e](V("PG", 16 * a, 16 * b), IND(PA, V("OM", a, b)))
        for q, (a, b) in enumerate(ROADS):
            reduce16("PG", a, b, "Z1", V(PB[q], 0, b - a), (V("ID", 0, 128), V("NM", a, b)))
            cp(V("RU", a, b), V(PB[q], 0, b - a))
        for (a, b) in UGATHER:
            distance("DF", "AB", a, b, "RU", zt)
        for q in range(len(HPIECES) + 1):
            if q == TSEND:
                send(zc, zt, 0, 128, "rT%d" % s)
            if q == NSEND:
                send(nr, "NS%d" % s, 0, 128, "rN%d" % s)
            if q < len(HPIECES):
                h_of(q, s)
        if last:
            dma("s", "o_lo", V("LO", 0, 256), ROW("PW", 0), 65536)
            dma("s", "o_hi", V("LO", 256, 512), ROW("PW", 1), 65536)
            line(V("pR", 256, 512), V("LO", 256, 512), 1.0, -float(B0))
            tt(V("YPg", 0, 256), V("pR", 256, 512), V("LO", 0, 256), ALU.add)
            dma("s", "o_pf", ROW("PF", 0), V("YPg", 0, 256), 131072)
        line(V("e1", 0, 128), date, 1.0, -(s + 99) / 2.0, ACT.Abs)
        line(V("e2", 0, 128), V("e1", 0, 128), -BIG, BIG * (99 - s) / 2.0, ACT.Relu)
        line(V("RT", 0, 128), V("e2", 0, 128), 1.0, lim)
        if not last:
            line(V("nmy", 0, 128), date, 1.0, -float(s + 1), ACT.Relu)
            line(V("nmx", 0, 128), V("nmy", 0, 128), -1.0, 1.0, ACT.Relu)
        if DSHARE:
            mm(V("pM", 0, 256), V("IDb", 0, 128), V(zc, 128, 384))
        for (a, b) in DGATHER:
            if a in DSHARE:
                act(V("PG", 16 * a, 16 * b), IND(XA, V(hr, a, b)))
                tt(V("DG", 16 * a, 16 * b), V("PG", 16 * a, 16 * b), V("pM", 0, 16 * (b - a)), ALU.subtract)
                act(V("AC", 16 * a, 16 * b), V("DG", 16 * a, 16 * b), ACT.Abs)
            else:
                distance("DG", "AC", a, b, hr, zc)
        for (a, b) in DSUMS:
            reduce16("AC", a, b, "ZK", V(KD, K0 + a, K0 + b), (ALL("oneb"), V("beta", a, b)))
            if a == 0:
                mm(V(KD, 448, 512), V("IDb", 0, 128), V(zc, 128, 192))
        if not last:
            ways_open(s + 1, V(nr, 0, 128))
        cp(V("HW", 8, 136), V(hr, 0, 128))
        mms(V("pU0", 0, 128), [(V("NID", 0, 128), V(nr, 0, 128)), (V("ID", 0, 128), V("HW", 8, 136))], True, NAMES == "v")
        for L in range(4):
            scan(V("SM", 36 * L, 36 * L + 34), V("AGE", 0, 34), V(KD, K0 + L, K0 + L + 136, 4), lim, ALU.add, ALU.min)
        for L in range(4):
            scan(V("SM", 144 + 36 * L, 179 + 36 * L), V("AGE", 36 * L, 36 * L + 35), BACK(KD, K0 + L - 12, K0 + L + 128, 4),
                 -BIG, ALU.add, ALU.max)
        tt(V("red", 0, 128), V(KD, K0, K0 + 128), V("RT", 0, 128), ALU.is_ge)
        tt(V("OFF", 0, 4), V("SM", 31, 144, 36), V("SM", 33, 144, 36), ALU.subtract)
        tt(V("OFF", 4, 8), V("SM", 178, 288, 36), V("SM", 175, 288, 36), ALU.subtract)
        tt(V("NC", 0, 4), V("SM", 33, 144, 36), V("SM", 31, 144, 36), ALU.subtract)
        for L in range(4):
            line(V("rf", L, 128, 4), V("colc", L, 128, 4), 1.0, V("NC", L, L + 1), ACT.Abs)
        if not last:
            mms(V("pR", 128, 256), [(V("IDb", 0, 128), V("nmx", 0, 128)), (V("N2", 0, 128), V("red", 0, 128))])
            act(V("pS", 0, 128), V("pR", 128, 256), ACT.Relu)
            tt(V("nm", 0, 128), V("pS", 0, 128), V("rf", 0, 128), ALU.min)
            ways()
        line(V("RF", 0, 128), V("rf", 0, 128), -99.0, 99.0, ACT.Relu)
        mms(V("pS", 128, 256), [(V("IDb", 0, 128), date), (V("N200", 0, 128), V("red", 0, 128)), (V("N2", 0, 128), V("RF", 0, 128))])
        act(V("Tz", 0, 128), V("pS", 128, 256), ACT.Relu)
        line(V("Tq", 0, 128), V("red", 0, 128), float(s + 2), 0.0)
        mms(V("pS", 256, 384), [(V("IDb", 0, 128), V(k, 0, 128)) for k in ("Tq", "RF", "Tz")])
        act(V("YT", 0, 128) if last else V(zt1, 0, 128), V("pS", 256, 384))
        for t, (window, bank) in enumerate(((ow1, "pM"), ("HW", "pP0"))):
            a, b = 64 * t, 64 * t + 64
            tt(V("GD", a, b), IND(V(window, 0, 136), V("OFF", 4 * t, 4 * t + 4)), V("DM", 0, 64), ALU.mult)
            mm(V(bank, 128, 192), V("GM", 0, 128), V("GD", a, b))
            for L in range(4):
                c, w, own = 264 * t + 66 * L, 16 * L + 17, V("OWN", 4 * t + L, 4 * t + L + 1)
                line(V("GX", c + w - 16, c + w), V("GD", a + 16 * L, a + 16 * L + 16), 1.0, 0.0, ACT.Identity, own)
            if SPREAD[t] == "a":
                line(V("OWN", 8, 12), V("OWN", 4 * t, 4 * t + 4), CUT, 0.0)
            for L in range(4):
                c, w, own = 264 * t + 66 * L, 16 * L + 17, V("OWN", 4 * t + L, 4 * t + L + 1)
                if SPREAD[t] == "a":
                    line(V("NE", c + 1, c + w), V(bank, 128, 127 + w), -CUT, V("OWN", 8 + L, 9 + L), ACT.Abs)
                else:
                    ts(V("NE", c + 1, c + w), V(bank, 128, 127 + w), own, ALU.not_equal, CUT, ALU.mult)
                scan(BACK("FS", 264 * t + L, 264 * t + L + 4 * w, 4), BACK("NE", c, c + w), BACK("GX", c, c + w), 0.0, ALU.min, ALU.max)
            if not DIRECT:
                cp(V("fu", 4 * t, 4 * t + 4), V("FS", 264 * t, 264 * t + 4))
        tt(V("GD", 128, 192), IND(V("HW", 0, 136), V("OFF", 0, 4)), V("DM", 0, 64), ALU.mult)
        mm(V("pR", 0, 64), V("G01", 0, 128), V("GD", 128, 192))
        ts(V("HB", 0, 4), V("OFF", 4, 8), 16.0, ALU.mult, V("p16m", 0, 1), ALU.add)
        ts(V("zi", 0, 64), IND(V("DG", 0, 2048), V("HB", 0, 4)), 0.5, ALU.mult, -0.25, ALU.add)
        tt(V(zt1, 128, 192), V("zi", 0, 64), V(KD, 448, 512), ALU.add)
        if not last:
            line(V("hx", 0, 64), V("pR", 0, 64), V("q1", 0, 1), 0.0)
            tt(V("PD", 0, 64), V("pR", 0, 64), V("hx", 0, 64), ALU.subtract)
            write(PA, 0, "PD")
            tile(zt1, TILEB)
        if NAMES != "v":
            mm(V("pU0", 0, 128), V("I8k", 0, 128), V("red", 0, 128), False, True)
        if not last:
            mm(V("pU0", 128, 256), V("GMb", 0, 128), V("red", 0, 128))
            line(V("junk", 0, 128), V("pU0", 128, 256), 32.0, A0 / 128, ACT.Identity, V("A32", 0, 1))
        write(XA, 1, zt1, 128)
        if NAMES == "v":
            tt(V("pU0", 256, 384), V("pU0", 0, 128), V("red", 0, 128), ALU.mult)
            tt(V("NS%d" % (s + 1), 0, 128), V("pU0", 256, 384), V(nr, 0, 128), ALU.add)
        else:
            line(V("Nw", 0, 128), V("pU0", 0, 128), 1.0, -4096.0, ACT.Relu)
            mms(V("pU0", 256, 384), [(V("ID", 0, 128), V(nr, 0, 128)), (V("N4k", 0, 128), V("red", 0, 128)), (V("ID", 0, 128), V("Nw", 0, 128))])
            line(V("YN", 0, 128) if last else V("NS%d" % (s + 1), 0, 128), V("pU0", 256, 384), 1.0, -float(B0) if last else 0.0)
        if not last:
            h_terms(s + 1, V("A32", 0, 1))
        if last:
            if NAMES == "v":
                ts(V("YN", 0, 128), V("NS%d" % (s + 1), 0, 128), -float(B0), ALU.add)
            line(V("ht", 0, 64), V("pR", 0, 64), 1.0, -float(B0))
            write(V("PF", 0, WW), 0, "ht")
            dma("s", "o_n", ALL("yn"), V("YN", 0, 128), 65536)
            dma("a", "o_z", ALL("yz"), V(zt1, 128, 192), 16384)
            dma("a", "o_t", ALL("yt"), V("YT", 0, 128), 65536)
            dma("s", "o_x", ALL("yx"), V("XW", B0, WW), 1048576)
            dma("a", "o_p", ALL("yp"), ROW("PF", 0), 131072)
    issue()
